import numpy as np, ml_dtypes
CORES = [23,119,17,113]
N = 4
import mx_ref
BF = ml_dtypes.bfloat16
def gentries(a):
    return np.ascontiguousarray(a.reshape(8, 16, -1).transpose(0, 2, 1)).reshape(8, -1)
def gtable(e):
    e = np.asarray(e); return np.ascontiguousarray(e.reshape(8, -1, 16).transpose(0, 2, 1)).reshape(128, -1).astype(np.int32)
def gcols(t, e):
    v = np.concatenate([t.reshape(8, 16, -1, 4), np.zeros((8, 16, 1, 4), BF)], axis=2)
    return np.ascontiguousarray(np.stack([v[g][:, e[g]] for g in range(8)])).reshape(128, -1)
def tile(rs):
    return np.stack(rs, axis=2).reshape(128, -1).astype(BF)
def pick(q, e):
    c = np.concatenate([q[0].reshape(128, -1, 4), np.zeros((128, 1, 4), np.uint8)], axis=1); s = np.concatenate([q[1], np.ones((16, 1), np.uint8)], axis=1)
    return (np.ascontiguousarray(c[:, e].reshape(128, -1)), np.ascontiguousarray(s[:, e]))
def join(*qs):
    return (np.concatenate([q[0] for q in qs], axis=1), np.concatenate([q[1] for q in qs], axis=1))
def put(q, e, v):
    c, s = q[0].reshape(128, -1, 4).copy(), q[1].copy(); c[:, e] = v[0].reshape(128, -1, 4); s[:, e] = v[1]
    return (c.reshape(128, -1), s)
def pk(c, s):
    return (np.ascontiguousarray(c), mx_ref.live(s))
def emit(q):
    return q[0], q[1]
def packed(v, rng):
    q = [mx_ref.quantize(np.ascontiguousarray(v[r])) for r in range(N)]
    return np.stack([a for a, b in q]), np.stack([mx_ref.plane(b, rng) for a, b in q])
def values_of_codes():
    e, c = np.zeros((128, 128, 4), np.float32), np.zeros((128, 2, 4), np.uint8)
    e[np.arange(128), np.arange(128), 0] = 1
    c[:127, :, 0] = np.arange(256).reshape(2, 128).T[:127]
    return mx_ref.matmul(mx_ref.quantize(e.reshape(128, 512).astype(BF)), (c.reshape(128, 8), np.full((16, 2), 127, np.uint8))).T.reshape(-1).astype(np.float64)
CODE_VALUE, SCALE_VALUE = values_of_codes(), 2.0 ** (np.arange(256) - 127.0)
def decode(q):
    return (CODE_VALUE[q[0]].reshape(16, 8, -1, 4) * SCALE_VALUE[q[1]][:, None, :, None] + 0.0).reshape(128, -1).astype(np.float32)
def f(rng, *shape):
    return mx_ref.flush((rng.standard_normal(shape, dtype=np.float32) * np.exp2(rng.integers(-2, 3, shape[:-1] + (1,)))).astype(BF))
def wide(rng, *shape, cols=0):
    v = rng.standard_normal(shape, dtype=np.float32) * np.exp2(rng.integers(-12, 13, shape)).astype(np.float32)
    if cols: v *= np.repeat(np.exp2(rng.integers(-cols, cols + 1, shape[:-2] + (1, shape[-1] // 4))) * (rng.random(shape[:-2] + (1, shape[-1] // 4)) > 0.0625), 4, axis=-1).astype(np.float32)
    return mx_ref.flush(v.astype(BF))
C, H = 448, 224
STEP = [1, 2, 3]
def numbers_of(rng):
    return {"x": np.array(f(rng, N, 128, 4 * C)), "u": np.array(f(rng, N, 128, 512)), "v": np.array(f(rng, N, 128, 512))}
def stored(m):
    return {"ml": np.stack([gtable(m[r]) for r in range(N)])}
def paired(e):
    m = np.zeros_like(e)
    np.put_along_axis(m, e, np.roll(e, H, axis=-1), axis=-1)
    return m
def pairings(rng):
    return paired(rng.permuted(np.tile(np.arange(C), (N, 8, 1)), axis=2))
def zigzag(rng, loop):
    s, t = rng.permutation(H), rng.permutation(H)
    a = np.concatenate([np.roll(t, -1), H + np.roll(s, -1)]).reshape(-1, 2)
    if not loop: a[H // 2 - 1, 1], a[-1, 0] = int(a[-1, 0]), int(a[H // 2 - 1, 1])
    b = np.concatenate([s, H + t]).reshape(-1, 2)
    return [paired(np.concatenate([k[:, 0], k[:, 1]])) for k in (a, b)]
def coil(rng):
    s = rng.permutation(H)
    k = np.concatenate([s, H + np.roll(s[:-1], -1), H + s[-1:]]).reshape(-1, 2)
    k[H // 2 - 1, 1], k[-1, 0] = int(k[-1, 0]), int(k[H // 2 - 1, 1])
    return paired(np.concatenate([k[:, 0], k[:, 1]]))
def layers(rng, still=[], pairs=False):
    w = np.array(f(rng, N, 128, 2048)).reshape(N, 8, 16, 4, 8, 16, 4)
    for i in still:
        w[:, :, i] = 0
        w[:, :, :, :, :, i] = 0
    if pairs:
        w[:, :, :, :, :, 8:] = 0
        for g in range(8):
            w[:, g, 8, 0, g, 8, 0] = -28.0
            for b in range(4): w[:, g, 10, b, g, 9, 0] = -2.0 ** (b - 5)
    return w
def weights(rng, w):
    c, s = packed(np.ascontiguousarray(w).reshape(N, 128, 2048), rng)
    return {"wc": c, "ws": s}
def setup_inputs(rng):
    return {**numbers_of(rng), **stored(pairings(rng)), **weights(rng, layers(rng))}
def setup_inputs_ties(rng):
    d = numbers_of(rng)
    o = rng.permutation(N)
    k = rng.integers(0, 4, (N, 8, C))
    k[o[0]] = 0
    k[o[1]] -= 4
    k[o[2]] = np.arange(C) < H
    kind = rng.permutation(8)
    m = np.zeros((N, 8, C), np.int64)
    for g in range(8):
        if 4 <= kind[g] < 7: k[:, g] = np.sort(k[:, g].reshape(N, 2, H), axis=1).reshape(N, C)
        for r in range(N):
            p, q = r ^ STEP[0], r ^ STEP[1]
            if kind[g] < 4 and r < p:
                a = zigzag(rng, kind[g] == 3)
                j = int(rng.integers(2))
                m[r, g], m[p, g] = a[j], a[1 - j]
            if 4 <= kind[g] < 6 and r < min(p, q, p ^ STEP[1]):
                m[r, g], m[q, g] = zigzag(rng, False)
                m[p, g] = m[p ^ STEP[1], g] = paired(np.arange(C))
            if kind[g] == 7: m[r, g] = paired(np.concatenate([rng.permutation(H), H + rng.permutation(H)]))
        if kind[g] == 6:
            m[:, g] = paired(np.arange(C))
            r = int(rng.integers(N))
            if STEP[0] ^ STEP[1] == STEP[2]: m[r, g] = coil(rng)
            else: m[r, g], m[r ^ STEP[2], g] = zigzag(rng, False)
    x = d["x"].reshape(N, 8, 16, C, 4)
    x[:, :, 0] = 0
    x[:, :, 0, :, 0] = k.astype(np.float32).astype(BF)
    a = np.exp2(rng.integers(-3, 4, (N, 8, 1)).astype(np.float32))
    x[:, :, 8:] = 0
    x[:, :, 8, :, 0] = (-1.125 * a).astype(BF)
    x[:, :, 10, :, 0] = (-0.0703125 * a).astype(BF)
    u = d["u"].reshape(N, 128, 128, 4)
    u[:, :, ::16] = 0
    for h in range(0, 128, 16): u[:, h, h, 0] = 1.0
    return {"x": x.reshape(N, 128, 4 * C), "u": u.reshape(N, 128, 512), "v": d["v"], **stored(twist(k, m)), **weights(rng, layers(rng, [0], True))}
def setup_inputs_near(rng):
    d = numbers_of(rng)
    x = d["x"].astype(np.float32).reshape(N, 8, 16, C, 4)
    x[:, :, 0] = 0
    x[:, :, 8:] = 0
    u = d["u"].reshape(N, 128, 128, 4)
    u[:, :, ::16] = 0
    w = layers(rng, [0, 8, 9, 10, 11, 12, 13, 14, 15])
    o = rng.permutation(N) % 4
    for r in range(N):
        c = rng.choice([-1.0, 1.0], (8, 1))
        s = rng.integers(0, 16, (8, C))
        digits = ((s[:, :, None] >> np.arange(4)) & 1) * np.exp2(np.arange(4) - 23.0)
        if o[r] < 2:
            x[r, :, 0, :, 0] = c
            x[r, :, 8] = digits
            x[r, :, 11, :, 0] = 2.0 ** -10
        elif o[r] == 2: x[r, :, 8] = digits * rng.choice([-1.0, 1.0], (8, C, 1))
        else:
            x[r, :, 8, :, 0] = np.where(s < 8, 1.25, 0.0) * 2.0 ** -30 * c
            x[r, :, 9, :, 0] = np.where(s < 8, 0.0, 1.125) * 2.0 ** -30 * c
            for g in rng.permutation(8)[:4]:
                e = rng.choice([-1.0, 1.0], C) * 2.0 ** -30
                x[r, g, 8, :, 0] = 1.25 * e
                x[r, g, 9, :, 0] = -1.125 * e
            for g in range(8):
                w[r, g, 8, 0, g, 12, 0] = 2.0 ** -8
                w[r, g, 8, 0, g, 14, 0] = 64.0
                w[r, g, 1, 0, g, 2, 0] = 256.0
        at = [0, C - 1, int(rng.integers(C)), int(rng.integers(C))]
        for g, j in zip(rng.permutation(8)[:4], at): x[r, g, 0, j, 0] = 2.0 ** 29 * rng.choice([-1.0, 1.0])
        k = 1.0 if o[r] == 0 else 2.0 ** -30
        for h in range(0, 128, 16):
            u[r, h, h, 0] = k if o[r] < 2 else 1.0
            if o[r] < 2: u[r, h + 11, h, 0] = k
            if o[r] < 3: u[r, h + 8, h] = k
            else:
                u[r, h + 8, h, 0] = k
                u[r, h + 9, h, 0] = 1.125 * k
                u[r, h + 12, h, 0] = k
    return {"x": x.reshape(N, 128, 4 * C).astype(BF), "u": u.reshape(N, 128, 512), "v": d["v"], **stored(pairings(rng)), **weights(rng, w)}
def setup_inputs_odd(rng):
    d = numbers_of(rng)
    x = (1.0 + (2 * rng.integers(0, 64, (N, 16, 8, C, 4)) + 1) * 2.0 ** -7) * np.exp2(-rng.integers(0, 7, (N, 16, 8, C, 4)).astype(np.float64)) * rng.choice([-1.0, 1.0], (N, 16, 8, C, 4))
    x[:, :, 0, :, 0] = 1.96875 * 2.0 ** 8 * rng.choice([-1.0, 1.0], (N, 16, C))
    u = d["u"].reshape(N, 16, 8, 128, 4)
    u[:, :, 0, ::16] = 0
    for r in range(N):
        for i, g in enumerate(rng.permutation(8)[:4]):
            x[r, 2 * g, 1, :, 0] = (8 + rng.integers(0, 2, C)) * 2.0 ** (i - 8)
            u[r, :, :, 16 * g] = 0
            u[r, 2 * g, 1, 16 * g, 0] = 1.0
    return {"x": x.astype(np.float32).reshape(N, 128, 4 * C).astype(BF), "u": u.reshape(N, 128, 512), "v": d["v"], **stored(pairings(rng)), **weights(rng, layers(rng, [0, 8]))}
def setup_inputs_ends(rng):
    d = numbers_of(rng)
    x = np.zeros((N, 8, 16, C, 4))
    u = d["u"].astype(np.float32).reshape(N, 128, 128, 4)
    v = d["v"].astype(np.float32)
    w = np.zeros((N, 128, 4, 128, 4), np.float32)
    m = pairings(rng)
    o, e = rng.permutation(N) % 4, rng.permutation(N) % 4
    i = np.arange(128)
    for r in range(N):
        h = rng.permutation(8)
        c = np.where(h < 2, 0.0, h % 2 * 2.0 - 1.0)[None, :, None]
        k = np.array([2.0, 4.0, -4.0])[rng.permutation(8) % 3]
        low = -(0.9 + 0.1 * rng.random((8, 16, C, 4))) * 2.0 ** 28
        if o[r] == 0: x[r] = low
        if o[r] == 1: x[r] = low * rng.choice([-1.0, 1.0], (C, 1))
        if o[r] < 2:
            u[r, :, ::16] = c * (0.9 + 0.1 * rng.random((128, 8, 4))) * 2.0 ** 30
            v[r] = rng.choice([-1.0, 1.0], (128, 512)) * (0.9 + 0.1 * rng.random((128, 512))) * 2.0 ** 30
        if o[r] == 2:
            x[r] = -(1.0 + 0.125 * rng.integers(0, 8, (8, 16, C, 4))) * 2.0 ** -30
            u[r, :, ::16] = c * (1.0 + 0.125 * rng.integers(0, 8, (128, 8, 4))) * 2.0 ** -30
            v[r] = rng.choice([-1.0, 1.0], (128, 512)) * (1.0 + 0.125 * rng.integers(0, 8, (128, 512))) * 2.0 ** -30
            k[:] = 32.0
        if o[r] == 3:
            x[r] = d["x"][r].astype(np.float32).reshape(8, 16, C, 4)[:, :, :1]
            u[r, :, ::16] *= np.abs(c).astype(np.float32)
        for b in range(4): w[r, i, b, i, b] = k[i // 16]
        if e[r] < 3: m[r] = [paired(np.arange(C)), np.arange(C) ^ 1, C - 1 - np.arange(C)][e[r]]
    return {"x": x.astype(np.float32).reshape(N, 128, 4 * C).astype(BF), "u": u.reshape(N, 128, 512).astype(BF), "v": v.astype(BF), **stored(m), **weights(rng, w.astype(BF))}
def setup_inputs_spread(rng):
    d = setup_inputs(rng)
    d["x"] = wide(rng, N, 128, 4 * C, cols=6)
    return d
def check_inputs(d):
    b = []
    for k in ("x", "u", "v"):
        a = np.abs(d[k].astype(np.float32))
        if not (np.isfinite(a).all() and ((a == 0) | (a >= 2.0 ** -30) & (a <= 2.0 ** 30)).all()): b.append("a value of " + k)
    none, least, most = [emit(mx_ref.quantize(np.full((128, 16), k, np.float32).astype(BF)))[1][0, 0] for k in (0.0, 2.0 ** -8, 2.0 ** 8)]
    for r in range(N):
        e = gentries(d["ml"][r]).astype(np.int64)
        if not ((e >= 0) & (e < C)).all(): b.append("an entry of ml")
        elif (e == np.arange(C)).any() or (np.take_along_axis(e, e, axis=1) != np.arange(C)).any(): b.append("ml: not a pairing")
        if ((d["wc"][r] == 0x7F) | (d["wc"][r] == 0xFF)).any(): b.append("wc: a code that is no number")
        s = mx_ref.live(d["ws"][r])
        if ((s != none) & ((s < least) | (s > most))).any(): b.append("ws: a scale out of range")
    return b
def twist(s, m):
    e = np.zeros(m.shape, np.int64) + np.arange(C)
    swap = H * (s[..., :H] > s[..., H:])
    e[..., :H] += swap
    e[..., H:] -= swap
    return np.take_along_axis(e, np.take_along_axis(m, e, axis=-1), axis=-1)
def glued(a, b):
    at = np.tile(np.arange(C), (8, 1))
    far = at >= H
    done = np.zeros((8, C), bool)
    for _ in range(H + 1):
        at = np.where(done, at, np.where(far, np.take_along_axis(b, at, axis=1), np.take_along_axis(a, at, axis=1)))
        done = done | ((at >= H) == far)
        at = np.where(done, at, np.where(far, at + H, at - H))
        far = far ^ ~done
        if done.all(): break
    return at
def plus(s, t):
    return (s.astype(np.float32) + t.astype(np.float32)).astype(BF)
def reference(x, u, v, ml, wc, ws):
    qu = [mx_ref.quantize(u[r]) for r in range(N)]
    lay = [pk(wc[r], ws[r]) for r in range(N)]
    now = [x[r] for r in range(N)]
    mate = [gentries(ml[r]).astype(np.int64) for r in range(N)]
    for step in STEP:
        turned, qa = [], []
        for r in range(N):
            s = mx_ref.matmul(qu[r], mx_ref.quantize(now[r]))[::16] + np.float32(0.0)
            turned.append(twist(s, mate[r]))
            qz = mx_ref.quantize(plus(now[r], gcols(now[r], turned[r])))
            qa.append(mx_ref.quantize(tile([mx_ref.matmul(pick(lay[r], np.arange(128 * b, 128 * b + 128)), qz) * np.float32(0.015625) for b in range(4)])))
        made = []
        for r in range(N):
            p = r ^ step
            mate[r] = glued(turned[r], turned[p])
            t = decode(join(pick(qa[r], np.arange(H)), pick(qa[p], np.arange(H, C)))).astype(BF)
            made.append(plus(now[r], gcols(t, mate[r])))
        now = made
    y, mo = np.zeros((N, 128, C), np.float32), np.zeros((N, 8, C), np.float32)
    oc, osc = np.zeros((N, 128, 4 * C), np.uint8), np.zeros((N, 16, C), np.uint8)
    for r in range(N):
        q = mx_ref.quantize(now[r])
        y[r] = mx_ref.matmul(mx_ref.quantize(v[r]), q)
        mo[r] = mate[r]
        oc[r], osc[r] = emit(q)
    return {"y": y, "mo": mo, "oc": oc, "osc": osc}

@@ -1,0 +1,393 @@
+from concourse.mybir import dt, AluOpType, ActivationFunctionType
+
+OP = AluOpType
+COPY = ActivationFunctionType.Copy
+C, H = 448, 224
+ROUNDS = [1, 2, 3]
+F16, BF, F32, I32, U16, U8, MX = "float16", "bfloat16", "float32", "int32", "uint16", "uint8", "float8_e4m3fn_x4"
+
+SCRATCH = {}
+
+
+def _sb(name, n, d):
+    SCRATCH[name] = ("sbuf", [128, n], d)
+
+
+for _r in range(4):
+    _sb("x%d" % _r, 4 * C, BF)
+for _b in range(4):
+    _sb("xp%d" % _b, C, BF)
+    _sb("bp%d" % _b, C, BF)
+for _n in ("zl", "zu", "al", "au"):
+    _sb(_n, 4 * H, BF)
+for _n, _w in (("uq", 128), ("uq2", 128), ("vq", 128), ("wq", 512), ("eq", 512), ("qx", C), ("qzl", H), ("qzu", H),
+               ("qal", H), ("qau", H)):
+    _sb(_n, _w, MX)
+    _sb(_n + "s", _w, U8)
+for _s in ROUNDS:
+    _sb("lq%d" % _s, H, MX)
+    _sb("lq%ds" % _s, H, U8)
+    _sb("lb%d" % _s, 28, U16)
+for _n, _w, _d in (("ut", 512, BF), ("vt", 512, BF), ("mli", 28, I32), ("ones", 512, BF), ("et", 2048, BF),
+                   ("pi", 42, I32), ("pm", 42, I32), ("pmu", 42, U16), ("pf", 1, F32), ("pf1", 1, F32), ("off", 1, F32),
+                   ("fi", 16, F32), ("ka", 16, F32), ("kb", 16, F32), ("k16", 16, BF), ("m1", 16, BF),
+                   ("keep", H, BF), ("mask", H, BF), ("rst", H, BF), ("io", 672, F32), ("raw", C, F32),
+                   ("ui", 8, I32), ("up", 8, U16), ("mm", 28, U16), ("mf", 28, F32), ("sg", 28, F32), ("tt", 28, F32),
+                   ("os0", 28, F32), ("mf2", 28, F32), ("af", 14, F32),
+                   ("mmf", 28, F32), ("sup", H, F32), ("sw", H, BF), ("bu", H, BF), ("bl", H, BF), ("sc", 672, BF),
+                   ("ga", H, F16), ("gb", H, F16), ("sa", H, F16), ("sm", C, F16), ("rr", 28, F32), ("qq", 28, F32),
+                   ("dd", 14, F32), ("ee", 14, F32), ("nn", 28, F32), ("n16", 28, U16), ("m16", 28, U16),
+                   ("la", 14, U16), ("lb", 14, U16), ("wa", C, F32), ("w0", 672, F32), ("w1", 672, F32), ("wu", C, F32),
+                   ("wf", C, F32), ("mrow", C, F32), ("yo", C, F32)):
+    _sb(_n, _w, _d)
+for _b in range(8):
+    SCRATCH["p%d" % _b] = ("psum", [128, 512], "float32")
+
+SEMAPHORES = ["v", "a", "t", "gp"] + ["d%d" % i for i in range(24)]
+for _s in ROUNDS:
+    for _k in ("b", "q", "s"):
+        SEMAPHORES += ["arr%s%d" % (_k, _s), "snt%s%d" % (_k, _s)]
+
+
+def rank_program(g, core, T, topo):
+    rank = T.rank_of(core)
+    if rank is None:
+        return
+    Q = {"v": g.vector, "a": g.scalar, "t": g.tensor, "g": g, "s": g.sync}
+    OWN = {"v": "v", "a": "a", "t": "t", "g": "gp"}
+    cnt, seen, snap, hist = {}, {q: {} for q in Q}, {}, {}
+    tick = [0]
+
+    def need(q, sem, val):
+        if seen[q].get(sem, 0) >= val:
+            return
+        Q[q].wait_ge(T.sem[sem], val)
+        for k, w in snap.get((sem, val), {}).items():
+            if seen[q].get(k, 0) < w:
+                seen[q][k] = w
+        seen[q][sem] = val
+
+    def meets(x, y):
+        (a, b, s), (c, d, t) = x, y
+        if a >= d or c >= b:
+            return False
+        return not (s == t and s > 1 and (a - c) % s)
+
+    def hazards(q, reads, writes):
+        tok = []
+        for kind, regs in ((0, reads), (1, writes)):
+            for n, a, b, s in regs:
+                ps = SCRATCH.get(n, ("",))[0] == "psum"
+                for reg, k, token, at, eng in hist.get(n, []):
+                    if ps and eng != q or (k or kind) and meets(reg, (a, b, s)):
+                        tok.append((at, token))
+        for at, (sem, val) in sorted(set(tok), reverse=True):
+            need(q, sem, val)
+
+    def note(q, reads, writes, token):
+        tick[0] += 1
+        for kind, regs in ((0, reads), (1, writes)):
+            for n, a, b, s in regs:
+                h = hist.setdefault(n, [])
+                if kind and s == 1:
+                    h[:] = [e for e in h if not (e[0][0] >= a and e[0][1] <= b)]
+                h.append(((a, b, s), kind, token, tick[0], q))
+
+    def op(q, writes, reads, call, sem=None, inc=1):
+        hazards(q, reads, writes)
+        sem = sem or OWN[q]
+        ins = call()
+        ins.then_inc(T.sem[sem], inc)
+        cnt[sem] = cnt.get(sem, 0) + inc
+        snap[(sem, cnt[sem])] = dict(seen[q])
+        note(q, reads, writes, (sem, cnt[sem]))
+
+    def R(n, a=0, b=None, s=1):
+        return (n, a, T[n].shape[1] if b is None else b, s)
+
+    def ap(r):
+        return T[r[0]][:, r[1]:r[2]] if r[3] == 1 else T[r[0]][:, r[1]:r[2]:r[3]]
+
+    def tt(out, x, y, o):
+        op("v", [out], [x, y], lambda: g.vector.tensor_tensor(ap(out), ap(x), ap(y), o))
+
+    def ts(out, x, s1, o1, s2=None, o2=None):
+        if o2 is None:
+            op("v", [out], [x], lambda: g.vector.tensor_scalar(ap(out), ap(x), s1, None, o1))
+        else:
+            op("v", [out], [x], lambda: g.vector.tensor_scalar(ap(out), ap(x), s1, s2, o1, o2))
+
+    def tsp(out, x, sc, o1, s2=None, o2=None):
+        if o2 is None:
+            op("v", [out], [x, sc], lambda: g.vector.tensor_scalar(ap(out), ap(x), ap(sc), None, o1))
+        else:
+            op("v", [out], [x, sc], lambda: g.vector.tensor_scalar(ap(out), ap(x), ap(sc), s2, o1, o2))
+
+    def vcopy(out, x):
+        op("v", [out], [x], lambda: g.vector.tensor_copy(ap(out), ap(x)))
+
+    def fill(out, c):
+        op("v", [out], [], lambda: g.vector.memset(ap(out), c))
+
+    def pick_tt(out, win, off, y, o):
+        op("v", [out], [win, off, y], lambda: g.vector.tensor_tensor(ap(out), ap(win).indirect(ap(off)), ap(y), o))
+
+    def scan(out, x):
+        r = R("rst")
+        op("v", [out], [x, r], lambda: g.vector.tensor_tensor_scan(ap(out), ap(r), ap(x), 0.0, OP.mult, OP.add))
+
+    def held(out, x):
+        r = R("keep")
+        op("v", [out], [x, r], lambda: g.vector.tensor_tensor_scan(ap(out), ap(r), ap(x), 0.0, OP.add, OP.max))
+
+    def act(out, x, scale=1.0):
+        op("a", [out], [x], lambda: g.scalar.activation(ap(out), ap(x), COPY, scale=scale))
+
+    def act_pick(out, win, off):
+        op("a", [out], [win, off], lambda: g.scalar.activation(ap(out), ap(win).indirect(ap(off)), COPY))
+
+    def quant(q, x, a=0, b=None):
+        o, s = R(q, a, b), R(q + "s", a, b)
+        op("v", [o, s], [x], lambda: g.vector.quantize_mx(ap(o), ap(s), ap(x)))
+
+    def mm(bank, l, la, r, ra, rb):
+        o = R("p%d" % bank, 0, rb - ra)
+        ops = [R(l, la, la + 128), R(l + "s", la, la + 128), R(r, ra, rb), R(r + "s", ra, rb)]
+        op("t", [o], ops, lambda: g.tensor.matmul_mx(ap(o), ap(ops[0]), ap(ops[1]), ap(ops[2]), ap(ops[3]), True, True))
+
+    nd = [0]
+
+    def dma(q, writes, reads, out, in_):
+        sem = "d%d" % nd[0]
+        nd[0] += 1
+        op(q, writes, reads, lambda: Q[q].dma_start(out, in_), sem, 16)
+
+    def lanes(src, dst):
+        return topo.engines(src, dst)[:8]
+
+    def send(dst, land, src, k, s, codes):
+        e = lanes(core, dst)
+        rid, pid, _ = topo.addr(dst)
+        hazards("g", [src], [])
+        o, i = T[land][:, 0:src[2] - src[1]], ap(src)
+        if codes:
+            o, i = o.bitcast(dt.uint8), i.bitcast(dt.uint8)
+        g.remote_dma(out_ap=o, in_ap=i, remote_sem=T.sem["arr%s%d" % (k, s)], local_sem=T.sem["snt%s%d" % (k, s)],
+                     pid=pid, routing_id=rid, dma_engine_mask=sum(1 << j for j in e))
+        sem = "snt%s%d" % (k, s)
+        cnt[sem] = len(e)
+        note("g", [src], [], (sem, len(e)))
+
+    def arrives(land, k, s, src):
+        sem = "arr%s%d" % (k, s)
+        cnt[sem] = len(lanes(src, core))
+        note("g", [], [R(land)], (sem, cnt[sem]))
+
+    dma("a", [R("ut")], [], T.ut[:, :], T.u[:, :])
+    dma("s", [R("x0", 0, 4 * H)], [], T.x0[:, 0:4 * H], T.x[:, 0:4 * H])
+    dma("s", [R("x0", 4 * H, 4 * C)], [], T.x0[:, 4 * H:4 * C], T.x[:, 4 * H:4 * C])
+    dma("a", [R("mli")], [], T.mli[:, :], T.ml[:, :])
+    dma("s", [R("wq")], [], T.wq[:, :].bitcast(dt.uint8), T.wc[:, :])
+    dma("s", [R("wqs")], [], T.wqs[:, :], T.ws[:, :])
+    dma("s", [R("vt")], [], T.vt[:, :], T.v[:, :])
+
+    def iota(n, w, pattern, base, cm):
+        r = R(n, 0, w)
+        f = SCRATCH[n][2] == F32
+        op("g", [r], [], lambda: g.iota(ap(r), pattern, base, cm, allow_small_or_imprecise_dtypes=True) if f
+           else g.iota(ap(r), pattern, base, cm))
+
+    iota("pi", 42, [[0, 42]], 0, 1)
+    iota("fi", 16, [[1, 16]], 0, 0)
+    iota("ui", 8, [[16, 8]], 0, 0)
+    iota("io", 672, [[1, 672]], 0, 0)
+    ts(R("pm"), R("pi"), 15, OP.bitwise_and)
+    fill(R("ones"), 1.0)
+    vcopy(R("pmu"), R("pm"))
+    vcopy(R("pf"), R("pm", 0, 1))
+    vcopy(R("up"), R("ui"))
+    one = R("ones")
+    for b in range(4):
+        e = R("et", 512 * b, 512 * b + 512)
+        op("g", [e], [one], lambda: g.affine_select(ap(e), ap(one), [[-1, 512]], OP.is_equal, 0.0, b, 4))
+    pf, pf1, off = R("pf"), R("pf1"), R("off")
+    ts(pf1, pf, 1.0, OP.add)
+    ts(off, pf, 15.0, OP.is_lt, 2.0, OP.mult)
+    tsp(R("ka"), R("fi"), pf, OP.is_le, -8.0, OP.mult)
+    tsp(R("m1"), R("fi"), pf, OP.is_equal)
+    tsp(R("kb"), R("fi"), pf1, OP.is_equal, 2.0, OP.mult)
+    fill(R("rst"), 1.0)
+    tt(R("k16"), R("ka"), R("kb"), OP.add)
+    fill(R("rst", 0, H, 16), 0.0)
+    act_pick(R("mask"), R("m1"), R("pmu", 0, 14))
+    act_pick(R("keep"), R("k16"), R("pmu", 0, 14))
+    mask1 = R("mask")
+
+    quant("uq", R("ut"))
+    upk, uqc, uq2 = R("up"), R("uq"), R("uq2")
+    op("v", [uq2], [uqc, upk],
+       lambda: g.vector.tensor_copy(ap(uq2).bitcast(dt.uint32), ap(uqc).bitcast(dt.uint32).indirect(ap(upk))))
+    us, us2 = R("uqs"), R("uq2s")
+    op("v", [us2], [us, upk], lambda: g.vector.tensor_copy(ap(us2), ap(us).indirect(ap(upk))))
+    for w in ("w0", "w1"):
+        act(R(w, H, 672), R("io", H, 672))
+    act(R("raw", 0, H), R("io", H, C))
+    act(R("raw", H, C), R("io", 0, H))
+    act(R("wa", H, C), R("io", C, 672))
+    act(R("wu", 0, H), R("io", 0, H))
+    act(R("wf", H, C), R("io", H, C))
+
+    def prep(m):
+        ts(R("tt"), m, 224.0, OP.is_ge, 224.0, OP.mult)
+        ts(R("sg"), R("tt"), -2.0, OP.mult, 224.0, OP.add)
+        tt(R("mmf"), m, R("tt"), OP.subtract)
+        tsp(R("os0"), R("sg"), off, OP.mult)
+        vcopy(R("mm"), R("mmf"))
+        tt(R("mf2"), m, R("os0"), OP.subtract)
+
+    def plane(x, half, b):
+        act(R("xp%d" % b, half * H, half * H + H), R(x, half * 4 * H + b, half * 4 * H + 4 * H, 4))
+
+    def halfcols(x, half):
+        return R(x, half * 4 * H, half * 4 * H + 4 * H)
+
+    vcopy(R("mf"), R("mli"))
+    quant("qx", halfcols("x0", 0), 0, H)
+    mm(0, "uq2", 0, "qx", 0, H)
+    plane("x0", 0, 0)
+    plane("x0", 0, 1)
+    act(R("sup"), R("p0", 0, H))
+    quant("qx", halfcols("x0", 1), H, C)
+    mm(1, "uq2", 0, "qx", H, C)
+    prep(R("mf"))
+    todo = [(0, 2), (0, 3)]
+
+    for s in ROUNDS:
+        last = s == ROUNDS[-1]
+        xs, xn = "x%d" % (s - 1), "x%d" % s
+        peer = T.cores[rank ^ s]
+        land_b, land_q = "lb%d" % s, "lq%d" % s
+        arrives(land_b, "b", s, peer)
+        arrives(land_q, "q", s, peer)
+        arrives(land_q + "s", "s", s, peer)
+
+        tt(R("sw"), R("sup"), R("p1", 0, H), OP.is_gt)
+        bu, sw, up = R("bu"), R("sw"), R("mm", 0, 14)
+        op("v", [bu], [sw, up], lambda: g.vector.tensor_copy(ap(bu), ap(sw).indirect(ap(up))))
+        act_pick(R("bl"), sw, R("mm", 14, 28))
+        for half, b in todo + [(1, b) for b in range(4)]:
+            plane(xs, half, b)
+        todo = []
+        held(R("sc", C, 672), sw)
+        held(R("sc", 0, H), bu)
+        held(R("sc", H, C), R("bl"))
+        tsp(R("af"), R("sc", C + 15, 672, 16), off, OP.subtract)
+        tt(R("rr"), R("sc", 15, C, 16), R("sg"), OP.mult)
+        tt(R("qq"), R("rr"), R("mf2"), OP.add)
+        tt(R("dd"), R("qq", 14, 28), R("qq", 0, 14), OP.subtract)
+        tt(R("ee"), R("dd"), R("af"), OP.mult)
+        tt(R("nn", 0, 14), R("qq", 0, 14), R("ee"), OP.add)
+        tt(R("nn", 14, 28), R("qq", 14, 28), R("ee"), OP.subtract)
+        vcopy(R("n16"), R("nn"))
+        send(peer, land_b, R("n16"), "b", s, False)
+        n_up, n_lo = R("n16", 0, 14), R("n16", 14, 28)
+        b_up, b_lo = R(land_b, 0, 14), R(land_b, 14, 28)
+
+        act_pick(R("wa", 0, H), R("raw"), n_lo)
+
+        def z(half, b):
+            pick_tt(R(("zu", "zl")[half], b, 4 * H, 4), R("xp%d" % b), (n_up, n_lo)[half],
+                    R(xs, half * 4 * H + b, half * 4 * H + 4 * H, 4), OP.add)
+
+        for b in range(4):
+            z(1, b)
+        z(0, 0)
+        quant("qzl", R("zl"))
+        for b in range(4):
+            mm(2 + b, "wq", 128 * b, "qzl", 0, H)
+            act(R("al", b, 4 * H, 4), R("p%d" % (2 + b), 0, H), 0.015625)
+        for b in range(1, 4):
+            z(0, b)
+        quant("qzu", R("zu"))
+        quant("qal", R("al"))
+        send(peer, land_q, R("qal"), "q", s, True)
+        send(peer, land_q + "s", R("qals"), "s", s, False)
+        for b in range(4):
+            k = (6, 7, 2, 3)[b]
+            mm(k, "wq", 128 * b, "qzu", 0, H)
+            act(R("au", b, 4 * H, 4), R("p%d" % k, 0, H), 0.015625)
+        if s == 1:
+            quant("eq", R("et"))
+            quant("vq", R("vt"))
+
+        gbuf = ("ga", "gb")
+        lists = ("la", "lb")
+        win, lst = R("wa"), b_up
+        for k in range(7):
+            gk, lk, wk = R(gbuf[k % 2]), R(lists[k % 2]), "w%d" % (k % 2)
+            pick_tt(gk, win, lst, mask1, OP.mult)
+            act_pick(R(wk, 0, H), win, lst)
+            if k == 1:
+                quant("qau", R("au"))
+                for b in range(4):
+                    mm(4 + b, "eq", 128 * b, "qau", 0, H)
+            scan(R("sa"), gk)
+            vcopy(lk, R("sa", 15, H, 16))
+            if 1 < k < 6:
+                act(R("bp%d" % (k - 2), 0, H), R("p%d" % (2 + k), 0, H))
+            win, lst = R(wk), lk
+        for b in range(4):
+            mm(2 + b, "eq", 128 * b, land_q, 0, H)
+        w_up = R("wu", H, C)
+        op("v", [w_up], [win, lst],
+           lambda: g.vector.tensor_scalar(ap(w_up), ap(win).indirect(ap(lst)), 224.0, None, OP.subtract))
+        pick_tt(R("ga"), R("wu"), n_up, mask1, OP.mult)
+        act_pick(R("wf", 0, H), R("wu"), n_lo)
+        for b in range(4):
+            act(R("bp%d" % b, H, C), R("p%d" % (2 + b), 0, H))
+
+        def new(half, b):
+            lo, hi = half * 4 * H + b, half * 4 * H + 4 * H
+            pick_tt(R(xn, lo, hi, 4), R("bp%d" % b), R("m16", 14 * half, 14 * half + 14), R(xs, lo, hi, 4), OP.add)
+
+        scan(R("sm", 0, H), R("ga"))
+        vcopy(R("m16", 0, 14), R("sm", 15, H, 16))
+        pick_tt(R("gb"), R("wf"), b_lo, mask1, OP.mult)
+        new(0, 0)
+        scan(R("sm", H, C), R("gb"))
+        new(0, 1)
+        vcopy(R("m16", 14, 28), R("sm", H + 15, C, 16))
+        new(0, 2)
+        new(0, 3)
+        new(1, 0)
+        for half in (0, 1):
+            if half == 1:
+                for b in range(1, 4):
+                    new(1, b)
+            c0, c1 = half * H, half * H + H
+            quant("qx", halfcols(xn, half), c0, c1)
+            if not last:
+                mm(half, "uq2", 0, "qx", c0, c1)
+                if half == 1:
+                    prep(R("sm", 15, C, 16))
+                else:
+                    for b in range(4):
+                        plane(xn, 0, b)
+                    act(R("sup"), R("p0", 0, H))
+            else:
+                mm(half, "vq", 0, "qx", c0, c1)
+                dma("s", [], [R("qx", c0, c1)], T.oc[:, 4 * c0:4 * c1], T.qx[:, c0:c1].bitcast(dt.uint8))
+                if half == 0:
+                    act_pick(R("mrow", 0, H), R("wu"), n_up)
+                    act_pick(R("mrow", H, C), R("wf"), b_lo)
+                    act(R("yo", 0, H), R("p0", 0, H))
+                    dma("s", [], [R("mrow")], T.mo[:, :], T.mrow[0:128:16, :])
+                    dma("s", [], [R("yo", 0, H)], T.y[:, 0:H], T.yo[:, 0:H])
+                else:
+                    vcopy(R("yo", H, C), R("p1", 0, H))
+                    dma("a", [], [R("yo", H, C)], T.y[:, H:C], T.yo[:, H:C])
+                    for k in range(4):
+                        dma("s" if k < 2 else "a", [], [R("qxs")], T.osc[4 * k:4 * k + 4, :], T.qxs[32 * k:32 * k + 4, :])
+
+    for sem in sorted(cnt):
+        need("g", sem, cnt[sem])

@@ -5,6 +5,11 @@ COPY = ActivationFunctionType.Copy
 C, H = 448, 224
 ROUNDS = [1, 2, 3]
 F16, BF, F32, I32, U16, U8, MX = "float16", "bfloat16", "float32", "int32", "uint16", "uint8", "float8_e4m3fn_x4"
+PORT = 32
+RUNS = [(0, 128, 256, 2), (128, 256, 512, 4), (256, 384, 1024, 8), (384, C, 2048, 16)]
+CODES = 3072
+BASE = H - PORT
+LIFT, MANY = 512.0, 4096.0
 
 SCRATCH = {}
 
@@ -28,17 +33,20 @@ for _s in ROUNDS:
     _sb("lq%d" % _s, H, MX)
     _sb("lq%ds" % _s, H, U8)
     _sb("lb%d" % _s, 28, U16)
-for _n, _w, _d in (("ut", 512, BF), ("vt", 512, BF), ("mli", 28, I32), ("ones", 512, BF), ("et", 2048, BF),
-                   ("pi", 42, I32), ("pm", 42, I32), ("pmu", 42, U16), ("pf", 1, F32), ("pf1", 1, F32), ("off", 1, F32),
-                   ("fi", 16, F32), ("ka", 16, F32), ("kb", 16, F32), ("k16", 16, BF), ("m1", 16, BF),
-                   ("keep", H, BF), ("mask", H, BF), ("rst", H, BF), ("io", 672, F32), ("raw", C, F32),
+for _n, _w, _d in (("ut", 512, BF), ("vt", 512, BF), ("mli", 28, I32), ("ones", 516, BF), ("et", 516, BF),
+                   ("pi", 14, I32), ("pm", 14, I32), ("pmu", 14, U16), ("pf", 1, F32), ("pf1", 1, F32), ("off", 1, F32),
+                   ("off1", 1, F32), ("offh", 1, F32), ("inv", 1, F32),
+                   ("fi", 16, F32), ("ka", 16, F32), ("kb", 16, F32), ("kc", 16, F32), ("kd", 16, F32),
+                   ("k16", 16, BF), ("m16k", 16, BF), ("keep", H, BF), ("keepm", H, BF),
+                   ("io", C, F32), ("cc", C, BF), ("raw", C, BF),
                    ("ui", 8, I32), ("up", 8, U16), ("mm", 28, U16), ("mf", 28, F32), ("sg", 28, F32), ("tt", 28, F32),
-                   ("os0", 28, F32), ("mf2", 28, F32), ("af", 14, F32),
-                   ("mmf", 28, F32), ("sup", H, F32), ("sw", H, BF), ("bu", H, BF), ("bl", H, BF), ("sc", 672, BF),
-                   ("ga", H, F16), ("gb", H, F16), ("sa", H, F16), ("sm", C, F16), ("rr", 28, F32), ("qq", 28, F32),
-                   ("dd", 14, F32), ("ee", 14, F32), ("nn", 28, F32), ("n16", 28, U16), ("m16", 28, U16),
-                   ("la", 14, U16), ("lb", 14, U16), ("wa", C, F32), ("w0", 672, F32), ("w1", 672, F32), ("wu", C, F32),
-                   ("wf", C, F32), ("mrow", C, F32), ("yo", C, F32)):
+                   ("os0", 28, F32), ("mf2", 28, F32), ("far", 42, F32), ("ma", 28, F32), ("mb", 28, F32),
+                   ("mmf", 28, F32), ("sup", H, F32), ("sw", H, BF), ("bu", H, BF), ("bl", H, BF), ("sc", 672, F16),
+                   ("sa", 9 * H, BF), ("tr", 3 * H, BF), ("mu", C, F16), ("sm", C, F16), ("rr", 28, F32), ("qa", 28, F32),
+                   ("qb", 28, F32), ("nn", 28, F32), ("n16", 28, U16), ("m16", 28, U16),
+                   ("ls", 126, U16), ("wa", C, BF),
+                   ("w0", BASE + CODES, BF), ("w1", BASE + CODES, BF), ("f0", CODES, F32), ("f1", CODES, F32),
+                   ("mrow", C, F32), ("yo", C, F32)):
     _sb(_n, _w, _d)
 for _b in range(8):
     SCRATCH["p%d" % _b] = ("psum", [128, 512], "float32")
@@ -47,6 +55,10 @@ SEMAPHORES = ["v", "a", "t", "gp"] + ["d%d" % i for i in range(24)]
 for _s in ROUNDS:
     for _k in ("b", "q", "s"):
         SEMAPHORES += ["arr%s%d" % (_k, _s), "snt%s%d" % (_k, _s)]
+
+ORDER = """wa zl0 zl1 zl2 zl3 zu0 qzl p0:a zu1 al0 s0 al1 l0 p1:a zu2 al2 s1 al3 l1 zu3 p2:a qal s2 qzu l2 o:a
+p3:v au0 s3 au1 l3 au2 p4:v au3 s4 so l4 lo qau ebu p5:v f16:a s5 bu0 l5 t:v f48:a st f80:a lt ebl bu1 mu:v bl0 su bu2 lu
+bl1 f112 nu0 bu3 bl2 bl3 ml nu1 nu2 nu3 sl qu ll xu nl0 nl1 nl2 nl3 ql""".split()
 
 
 def rank_program(g, core, T, topo):
@@ -106,22 +118,19 @@ def rank_program(g, core, T, topo):
         return (n, a, T[n].shape[1] if b is None else b, s)
 
     def ap(r):
+        if not isinstance(r, tuple):
+            return r
         return T[r[0]][:, r[1]:r[2]] if r[3] == 1 else T[r[0]][:, r[1]:r[2]:r[3]]
 
     def tt(out, x, y, o):
         op("v", [out], [x, y], lambda: g.vector.tensor_tensor(ap(out), ap(x), ap(y), o))
 
     def ts(out, x, s1, o1, s2=None, o2=None):
+        reads = [x] + [c for c in (s1, s2) if isinstance(c, tuple)]
         if o2 is None:
-            op("v", [out], [x], lambda: g.vector.tensor_scalar(ap(out), ap(x), s1, None, o1))
+            op("v", [out], reads, lambda: g.vector.tensor_scalar(ap(out), ap(x), ap(s1), None, o1))
         else:
-            op("v", [out], [x], lambda: g.vector.tensor_scalar(ap(out), ap(x), s1, s2, o1, o2))
-
-    def tsp(out, x, sc, o1, s2=None, o2=None):
-        if o2 is None:
-            op("v", [out], [x, sc], lambda: g.vector.tensor_scalar(ap(out), ap(x), ap(sc), None, o1))
-        else:
-            op("v", [out], [x, sc], lambda: g.vector.tensor_scalar(ap(out), ap(x), ap(sc), s2, o1, o2))
+            op("v", [out], reads, lambda: g.vector.tensor_scalar(ap(out), ap(x), ap(s1), ap(s2), o1, o2))
 
     def vcopy(out, x):
         op("v", [out], [x], lambda: g.vector.tensor_copy(ap(out), ap(x)))
@@ -132,19 +141,29 @@ def rank_program(g, core, T, topo):
     def pick_tt(out, win, off, y, o):
         op("v", [out], [win, off, y], lambda: g.vector.tensor_tensor(ap(out), ap(win).indirect(ap(off)), ap(y), o))
 
-    def scan(out, x):
-        r = R("rst")
-        op("v", [out], [x, r], lambda: g.vector.tensor_tensor_scan(ap(out), ap(r), ap(x), 0.0, OP.mult, OP.add))
-
     def held(out, x):
         r = R("keep")
         op("v", [out], [x, r], lambda: g.vector.tensor_tensor_scan(ap(out), ap(r), ap(x), 0.0, OP.add, OP.max))
 
+    def heldm(out, x):
+        r = R("keepm")
+        op("v", [out], [x, r], lambda: g.vector.tensor_tensor_scan(ap(out), ap(r), ap(x), 0.0, OP.mult, OP.max))
+
     def act(out, x, scale=1.0):
         op("a", [out], [x], lambda: g.scalar.activation(ap(out), ap(x), COPY, scale=scale))
 
-    def act_pick(out, win, off):
-        op("a", [out], [win, off], lambda: g.scalar.activation(ap(out), ap(win).indirect(ap(off)), COPY))
+    def copy(q, out, x):
+        (act if q == "a" else vcopy)(out, x)
+
+    def pick(q, out, win, off):
+        if q == "a":
+            op("a", [out], [win, off], lambda: g.scalar.activation(ap(out), ap(win).indirect(ap(off)), COPY))
+        elif q == "v":
+            op("v", [out], [win, off], lambda: g.vector.tensor_copy(ap(out), ap(win).indirect(ap(off))))
+        else:
+            k = 8 if q == "h" else 6
+            pick("v", R(out[0], out[1], out[1] + 16 * k), win, R(off[0], off[1], off[1] + k))
+            pick("a", R(out[0], out[1] + 16 * k, out[2]), win, R(off[0], off[1] + k, off[2]))
 
     def quant(q, x, a=0, b=None):
         o, s = R(q, a, b), R(q + "s", a, b)
@@ -191,58 +210,60 @@ def rank_program(g, core, T, topo):
     dma("s", [R("wqs")], [], T.wqs[:, :], T.ws[:, :])
     dma("s", [R("vt")], [], T.vt[:, :], T.v[:, :])
 
-    def iota(n, w, pattern, base, cm):
-        r = R(n, 0, w)
-        f = SCRATCH[n][2] == F32
+    def iota(r, pattern, base, cm):
+        f = SCRATCH[r[0]][2] != I32
         op("g", [r], [], lambda: g.iota(ap(r), pattern, base, cm, allow_small_or_imprecise_dtypes=True) if f
            else g.iota(ap(r), pattern, base, cm))
 
-    iota("pi", 42, [[0, 42]], 0, 1)
-    iota("fi", 16, [[1, 16]], 0, 0)
-    iota("ui", 8, [[16, 8]], 0, 0)
-    iota("io", 672, [[1, 672]], 0, 0)
+    iota(R("pi"), [[0, 14]], 0, 1)
+    iota(R("fi"), [[1, 16]], 0, 0)
+    iota(R("ui"), [[16, 8]], 0, 0)
+    iota(R("io"), [[1, C]], 0, 0)
     ts(R("pm"), R("pi"), 15, OP.bitwise_and)
     fill(R("ones"), 1.0)
     vcopy(R("pmu"), R("pm"))
     vcopy(R("pf"), R("pm", 0, 1))
     vcopy(R("up"), R("ui"))
-    one = R("ones")
-    for b in range(4):
-        e = R("et", 512 * b, 512 * b + 512)
-        op("g", [e], [one], lambda: g.affine_select(ap(e), ap(one), [[-1, 512]], OP.is_equal, 0.0, b, 4))
-    pf, pf1, off = R("pf"), R("pf1"), R("off")
+    pf, pf1, off, off1, offh, inv = R("pf"), R("pf1"), R("off"), R("off1"), R("offh"), R("inv")
     ts(pf1, pf, 1.0, OP.add)
-    ts(off, pf, 15.0, OP.is_lt, 2.0, OP.mult)
-    tsp(R("ka"), R("fi"), pf, OP.is_le, -8.0, OP.mult)
-    tsp(R("m1"), R("fi"), pf, OP.is_equal)
-    tsp(R("kb"), R("fi"), pf1, OP.is_equal, 2.0, OP.mult)
-    fill(R("rst"), 1.0)
+    ts(off, pf, 15.0, OP.is_lt, LIFT, OP.mult)
+    ts(R("ka"), R("fi"), pf, OP.is_equal, -2 * LIFT, OP.mult)
+    ts(R("kc"), R("fi"), pf, OP.not_equal)
+    ts(R("kb"), R("fi"), pf1, OP.is_equal, LIFT, OP.mult)
+    ts(R("kd"), R("fi"), pf1, OP.is_equal, MANY - 1, OP.mult)
+    ts(inv, pf, 15.0, OP.is_equal, 1 / MANY, OP.max)
     tt(R("k16"), R("ka"), R("kb"), OP.add)
-    fill(R("rst", 0, H, 16), 0.0)
-    act_pick(R("mask"), R("m1"), R("pmu", 0, 14))
-    act_pick(R("keep"), R("k16"), R("pmu", 0, 14))
-    mask1 = R("mask")
+    tt(R("m16k"), R("kc"), R("kd"), OP.add)
+    ts(off1, off, 1.0, OP.add)
+    ts(offh, off, float(H), OP.add)
+    pick("a", R("keep"), R("k16"), R("pmu"))
+    pick("a", R("keepm"), R("m16k"), R("pmu"))
+    for a, b, c, st in RUNS:
+        ts(R("cc", a, b), R("io", 0, b - a), float(st), OP.mult, float(c), OP.add)
+    e, one = R("et"), R("ones")
+    op("g", [e], [one], lambda: g.affine_select(ap(e), ap(one), [[-1, 516]], OP.is_equal, 0.0, 3, 4))
 
     quant("uq", R("ut"))
     upk, uqc, uq2 = R("up"), R("uq"), R("uq2")
     op("v", [uq2], [uqc, upk],
        lambda: g.vector.tensor_copy(ap(uq2).bitcast(dt.uint32), ap(uqc).bitcast(dt.uint32).indirect(ap(upk))))
-    us, us2 = R("uqs"), R("uq2s")
-    op("v", [us2], [us, upk], lambda: g.vector.tensor_copy(ap(us2), ap(us).indirect(ap(upk))))
-    for w in ("w0", "w1"):
-        act(R(w, H, 672), R("io", H, 672))
-    act(R("raw", 0, H), R("io", H, C))
-    act(R("raw", H, C), R("io", 0, H))
-    act(R("wa", H, C), R("io", C, 672))
-    act(R("wu", 0, H), R("io", 0, H))
-    act(R("wf", H, C), R("io", H, C))
+    pick("a", R("uq2s"), R("uqs"), upk)
+    act(R("raw", 0, H), R("cc", 0, H))
+    act(R("raw", H, C), R("io", PORT, PORT + H))
+    act(R("wa", H, C), R("cc", H, C))
+    for a, b, c, st in RUNS:
+        n = b - a
+        for w in ("w0", "w1"):
+            act(R(w, BASE + c, BASE + c + st * n, st), R("cc", a, b))
+        for w in ("f0", "f1"):
+            iota(R(w, c, c + st * n, st), [[1, n]], a, 0)
 
     def prep(m):
-        ts(R("tt"), m, 224.0, OP.is_ge, 224.0, OP.mult)
-        ts(R("sg"), R("tt"), -2.0, OP.mult, 224.0, OP.add)
+        ts(R("tt"), m, offh, OP.is_ge, float(H), OP.mult)
+        ts(R("sg"), R("tt"), -2.0, OP.mult, float(H), OP.add)
         tt(R("mmf"), m, R("tt"), OP.subtract)
-        tsp(R("os0"), R("sg"), off, OP.mult)
-        vcopy(R("mm"), R("mmf"))
+        ts(R("os0"), R("sg"), 1.0, OP.add, off, OP.mult)
+        ts(R("mm"), R("mmf"), off, OP.subtract)
         tt(R("mf2"), m, R("os0"), OP.subtract)
 
     def plane(x, half, b):
@@ -251,16 +272,19 @@ def rank_program(g, core, T, topo):
     def halfcols(x, half):
         return R(x, half * 4 * H, half * 4 * H + 4 * H)
 
-    vcopy(R("mf"), R("mli"))
+    ts(R("mf"), R("mli"), off, OP.add)
     quant("qx", halfcols("x0", 0), 0, H)
     mm(0, "uq2", 0, "qx", 0, H)
+    prep(R("mf"))
     plane("x0", 0, 0)
     plane("x0", 0, 1)
     act(R("sup"), R("p0", 0, H))
     quant("qx", halfcols("x0", 1), H, C)
     mm(1, "uq2", 0, "qx", H, C)
-    prep(R("mf"))
-    todo = [(0, 2), (0, 3)]
+    plane("x0", 0, 2)
+    plane("x0", 0, 3)
+    vcopy(R("w1", 0, H), R("cc", 0, H))
+    iota(R("f0", PORT, PORT + H), [[1, H]], 0, 0)
 
     for s in ROUNDS:
         last = s == ROUNDS[-1]
@@ -271,123 +295,150 @@ def rank_program(g, core, T, topo):
         arrives(land_q, "q", s, peer)
         arrives(land_q + "s", "s", s, peer)
 
-        tt(R("sw"), R("sup"), R("p1", 0, H), OP.is_gt)
-        bu, sw, up = R("bu"), R("sw"), R("mm", 0, 14)
-        op("v", [bu], [sw, up], lambda: g.vector.tensor_copy(ap(bu), ap(sw).indirect(ap(up))))
-        act_pick(R("bl"), sw, R("mm", 14, 28))
-        for half, b in todo + [(1, b) for b in range(4)]:
-            plane(xs, half, b)
-        todo = []
+        sw, far, mine = R("sw"), R("far"), R("sc", C + 15, 672, 16)
+        tt(sw, R("sup"), R("p1", 0, H), OP.is_gt)
+        pick("v", R("bu"), sw, R("mm", 0, 14))
+        pick("a", R("bl"), sw, R("mm", 14, 28))
+        if s == 1:
+            for b in range(4):
+                plane(xs, 1, b)
         held(R("sc", C, 672), sw)
-        held(R("sc", 0, H), bu)
+        held(R("sc", 0, H), R("bu"))
         held(R("sc", H, C), R("bl"))
-        tsp(R("af"), R("sc", C + 15, 672, 16), off, OP.subtract)
+        ts(R("far", 0, 14), mine, off, OP.subtract, -MANY, OP.mult)
+        ts(R("far", 14, 28), mine, off1, OP.subtract, MANY, OP.mult)
+        ts(R("far", 28, 42), mine, off, OP.subtract, -MANY, OP.mult)
         tt(R("rr"), R("sc", 15, C, 16), R("sg"), OP.mult)
-        tt(R("qq"), R("rr"), R("mf2"), OP.add)
-        tt(R("dd"), R("qq", 14, 28), R("qq", 0, 14), OP.subtract)
-        tt(R("ee"), R("dd"), R("af"), OP.mult)
-        tt(R("nn", 0, 14), R("qq", 0, 14), R("ee"), OP.add)
-        tt(R("nn", 14, 28), R("qq", 14, 28), R("ee"), OP.subtract)
+        tt(R("ma"), R("mf2"), R("far", 0, 28), OP.add)
+        tt(R("mb"), R("mf2"), R("far", 14, 42), OP.add)
+        tt(R("qa"), R("rr"), R("ma"), OP.add)
+        tt(R("qb"), R("rr"), R("mb"), OP.add)
+        tt(R("nn", 0, 14), R("qa", 0, 14), R("qa", 14, 28), OP.max)
+        tt(R("nn", 14, 28), R("qb", 0, 14), R("qb", 14, 28), OP.max)
         vcopy(R("n16"), R("nn"))
         send(peer, land_b, R("n16"), "b", s, False)
         n_up, n_lo = R("n16", 0, 14), R("n16", 14, 28)
         b_up, b_lo = R(land_b, 0, 14), R(land_b, 14, 28)
 
-        act_pick(R("wa", 0, H), R("raw"), n_lo)
+        def cols(x, half, b):
+            return R(x, half * 4 * H + b, half * 4 * H + 4 * H, 4)
 
-        def z(half, b):
-            pick_tt(R(("zu", "zl")[half], b, 4 * H, 4), R("xp%d" % b), (n_up, n_lo)[half],
-                    R(xs, half * 4 * H + b, half * 4 * H + 4 * H, 4), OP.add)
+        def row(k):
+            return R("w%d" % (k % 2), H, C)
 
-        for b in range(4):
-            z(1, b)
-        z(0, 0)
-        quant("qzl", R("zl"))
-        for b in range(4):
-            mm(2 + b, "wq", 128 * b, "qzl", 0, H)
-            act(R("al", b, 4 * H, 4), R("p%d" % (2 + b), 0, H), 0.015625)
-        for b in range(1, 4):
-            z(0, b)
-        quant("qzu", R("zu"))
-        quant("qal", R("al"))
-        send(peer, land_q, R("qal"), "q", s, True)
-        send(peer, land_q + "s", R("qals"), "s", s, False)
-        for b in range(4):
-            k = (6, 7, 2, 3)[b]
-            mm(k, "wq", 128 * b, "qzu", 0, H)
-            act(R("au", b, 4 * H, 4), R("p%d" % k, 0, H), 0.015625)
-        if s == 1:
-            quant("eq", R("et"))
-            quant("vq", R("vt"))
+        def codes(k):
+            return R("w%d" % (k % 2), BASE)
 
-        gbuf = ("ga", "gb")
-        lists = ("la", "lb")
-        win, lst = R("wa"), b_up
-        for k in range(7):
-            gk, lk, wk = R(gbuf[k % 2]), R(lists[k % 2]), "w%d" % (k % 2)
-            pick_tt(gk, win, lst, mask1, OP.mult)
-            act_pick(R(wk, 0, H), win, lst)
-            if k == 1:
-                quant("qau", R("au"))
+        def ports(w):
+            return R(w, PORT, PORT + H)
+
+        def lst(k):
+            return R("ls", 14 * k, 14 * k + 14)
+
+        mrow = {}
+
+        def step(name, q):
+            kind, k = name[:2], int(name[-1]) if name[-1].isdigit() else 0
+            if name == "wa":
+                pick("a", R("wa", 0, H), R("raw"), n_lo)
+            elif kind in ("zu", "zl"):
+                half = kind == "zl"
+                pick_tt(R(kind, k, 4 * H, 4), R("xp%d" % k), (n_up, n_lo)[half], cols(xs, half, k), OP.add)
+            elif name in ("qzl", "qzu"):
+                quant(name, R(name[1:]))
                 for b in range(4):
-                    mm(4 + b, "eq", 128 * b, "qau", 0, H)
-            scan(R("sa"), gk)
-            vcopy(lk, R("sa", 15, H, 16))
-            if 1 < k < 6:
-                act(R("bp%d" % (k - 2), 0, H), R("p%d" % (2 + k), 0, H))
-            win, lst = R(wk), lk
-        for b in range(4):
-            mm(2 + b, "eq", 128 * b, land_q, 0, H)
-        w_up = R("wu", H, C)
-        op("v", [w_up], [win, lst],
-           lambda: g.vector.tensor_scalar(ap(w_up), ap(win).indirect(ap(lst)), 224.0, None, OP.subtract))
-        pick_tt(R("ga"), R("wu"), n_up, mask1, OP.mult)
-        act_pick(R("wf", 0, H), R("wu"), n_lo)
-        for b in range(4):
-            act(R("bp%d" % b, H, C), R("p%d" % (2 + b), 0, H))
-
-        def new(half, b):
-            lo, hi = half * 4 * H + b, half * 4 * H + 4 * H
-            pick_tt(R(xn, lo, hi, 4), R("bp%d" % b), R("m16", 14 * half, 14 * half + 14), R(xs, lo, hi, 4), OP.add)
-
-        scan(R("sm", 0, H), R("ga"))
-        vcopy(R("m16", 0, 14), R("sm", 15, H, 16))
-        pick_tt(R("gb"), R("wf"), b_lo, mask1, OP.mult)
-        new(0, 0)
-        scan(R("sm", H, C), R("gb"))
-        new(0, 1)
-        vcopy(R("m16", 14, 28), R("sm", H + 15, C, 16))
-        new(0, 2)
-        new(0, 3)
-        new(1, 0)
-        for half in (0, 1):
-            if half == 1:
-                for b in range(1, 4):
-                    new(1, b)
-            c0, c1 = half * H, half * H + H
-            quant("qx", halfcols(xn, half), c0, c1)
-            if not last:
-                mm(half, "uq2", 0, "qx", c0, c1)
-                if half == 1:
-                    prep(R("sm", 15, C, 16))
+                    mm((b + (2 if name == "qzl" else 6)) % 8, "wq", 128 * b, name, 0, H)
+            elif kind in ("al", "au"):
+                o, p = R(kind, k, 4 * H, 4), R("p%d" % ((k + (2 if kind == "al" else 6)) % 8), 0, H)
+                if q == "v":
+                    ts(o, p, 0.015625, OP.mult)
                 else:
+                    act(o, p, 0.015625)
+            elif name == "qal":
+                quant("qal", R("al"))
+                send(peer, land_q, R("qal"), "q", s, True)
+                send(peer, land_q + "s", R("qals"), "s", s, False)
+                if s == 1:
+                    for b in range(4):
+                        quant("eq", R("et", 3 - b, 515 - b), 128 * b, 128 * b + 128)
+            elif name == "qau":
+                quant("qau", R("au"))
+            elif name in ("ebl", "ebu"):
+                for b in range(4):
+                    mm((b + (2 if name == "ebl" else 6)) % 8, "eq", 128 * b, land_q if name == "ebl" else "qau", 0, H)
+            elif kind in ("bl", "bu"):
+                half = kind == "bl"
+                copy(q, R("bp%d" % k, half * H, half * H + H), R("p%d" % ((k + (2 if half else 6)) % 8), 0, H))
+            elif name in ("p0", "o"):
+                pick(q, row(0) if name == "p0" else R("tr", H, C), R("wa"), b_up if name == "p0" else b_lo)
+            elif name[0] == "p":
+                pick(q, row(k), codes(k - 1), lst(k - 1))
+            elif name in ("su", "sl"):
+                half = name == "sl"
+                held(R("sm", half * H, half * H + H), mrow[half])
+            elif name in ("lu", "ll"):
+                half = name == "ll"
+                ts(R("m16", 14 * half, 14 * half + 14), R("sm", half * H + 15, half * H + H, 16), off, OP.subtract)
+            elif name[0] in "sl":
+                k = {"t": 6, "o": 7, "r": 8}.get(name[1], k)
+                if name[0] == "s":
+                    heldm(R("sa", k * H, k * H + H), row(k) if k < 6 else R("tr", (k - 6) * H, (k - 5) * H))
+                else:
+                    ts(lst(k), R("sa", k * H + 15, k * H + H, 16), inv, OP.mult)
+            elif name == "t":
+                pick(q, R("tr", 0, H), R("w1", 0, C), n_up)
+            elif name == "r":
+                pick(q, R("tr", C, C + H), codes(5), lst(7))
+            elif name == "f16":
+                pick(q, ports("f1"), R("f0"), lst(4))
+            elif name == "f48":
+                pick(q, ports("f0"), R("f1"), lst(5))
+            elif name == "f80":
+                pick(q, ports("f1"), R("f0"), lst(5))
+            elif name == "f112":
+                pick(q, ports("f0"), R("f1"), lst(5))
+            elif name in ("mu", "ml", "mr"):
+                half = name != "mu"
+                win, at = R("f0" if name == "ml" else "f1"), lst({"mu": 6, "ml": 7, "mr": 8}[name])
+                mrow[half] = R("mu" if q == "v" else "mrow", half * H, half * H + H)
+                pick(q, mrow[half], win, at)
+                if last and q == "v":
+                    pick("a", R("mrow", half * H, half * H + H), win, at)
+                if last and half:
+                    dma("s", [], [R("mrow")], T.mo[:, :], T.mrow[0:128:16, :])
+            elif kind in ("nu", "nl"):
+                half = kind == "nl"
+                pick_tt(cols(xn, half, k), R("bp%d" % k), R("m16", 14 * half, 14 * half + 14), cols(xs, half, k), OP.add)
+                if half and not last:
+                    plane(xn, 1, k)
+            elif name == "xu":
+                if not last:
                     for b in range(4):
                         plane(xn, 0, b)
-                    act(R("sup"), R("p0", 0, H))
-            else:
-                mm(half, "vq", 0, "qx", c0, c1)
-                dma("s", [], [R("qx", c0, c1)], T.oc[:, 4 * c0:4 * c1], T.qx[:, c0:c1].bitcast(dt.uint8))
-                if half == 0:
-                    act_pick(R("mrow", 0, H), R("wu"), n_up)
-                    act_pick(R("mrow", H, C), R("wf"), b_lo)
-                    act(R("yo", 0, H), R("p0", 0, H))
-                    dma("s", [], [R("mrow")], T.mo[:, :], T.mrow[0:128:16, :])
-                    dma("s", [], [R("yo", 0, H)], T.y[:, 0:H], T.yo[:, 0:H])
+                        if b == 0:
+                            act(R("sup"), R("p0", 0, H))
                 else:
+                    act(R("yo", 0, H), R("p0", 0, H))
+                    dma("s", [], [R("yo", 0, H)], T.y[:, 0:H], T.yo[:, 0:H])
+            else:
+                half = name == "ql"
+                c0, c1 = half * H, half * H + H
+                quant("qx", halfcols(xn, half), c0, c1)
+                mm(int(half), "vq" if last else "uq2", 0, "qx", c0, c1)
+                if last:
+                    dma("s", [], [R("qx", c0, c1)], T.oc[:, 4 * c0:4 * c1], T.qx[:, c0:c1].bitcast(dt.uint8))
+                if half and not last:
+                    prep(R("sm", 15, C, 16))
+                if half and last:
                     vcopy(R("yo", H, C), R("p1", 0, H))
                     dma("a", [], [R("yo", H, C)], T.y[:, H:C], T.yo[:, H:C])
                     for k in range(4):
                         dma("s" if k < 2 else "a", [], [R("qxs")], T.osc[4 * k:4 * k + 4, :], T.qxs[32 * k:32 * k + 4, :])
+
+        for name in ORDER:
+            if name == "qal" and s == 2:
+                quant("vq", R("vt"))
+            step(*(name + ":a").split(":")[:2])
 
     for sem in sorted(cnt):
         need("g", sem, cnt[sem])

@@ -10,6 +10,7 @@ RUNS = [(0, 128, 256, 2), (128, 256, 512, 4), (256, 384, 1024, 8), (384, C, 2048
 CODES = 3072
 BASE = H - PORT
 LIFT, MANY = 512.0, 4096.0
+DZ = 0
 
 SCRATCH = {}
 
@@ -35,12 +36,12 @@ for _s in ROUNDS:
     _sb("lb%d" % _s, 28, U16)
 for _n, _w, _d in (("ut", 512, BF), ("vt", 512, BF), ("mli", 28, I32), ("ones", 516, BF), ("et", 516, BF),
                    ("pi", 14, I32), ("pm", 14, I32), ("pmu", 14, U16), ("pf", 1, F32), ("pf1", 1, F32), ("off", 1, F32),
-                   ("off1", 1, F32), ("offh", 1, F32), ("inv", 1, F32),
+                   ("offq", 1, F32), ("offh", 1, F32), ("inv", 1, F32),
                    ("fi", 16, F32), ("ka", 16, F32), ("kb", 16, F32), ("kc", 16, F32), ("kd", 16, F32),
                    ("k16", 16, BF), ("m16k", 16, BF), ("keep", H, BF), ("keepm", H, BF),
-                   ("io", C, F32), ("cc", C, BF), ("raw", C, BF),
+                   ("io", 256, F32), ("cc", C, BF), ("raw", C, BF),
                    ("ui", 8, I32), ("up", 8, U16), ("mm", 28, U16), ("mf", 28, F32), ("sg", 28, F32), ("tt", 28, F32),
-                   ("os0", 28, F32), ("mf2", 28, F32), ("far", 42, F32), ("ma", 28, F32), ("mb", 28, F32),
+                   ("os0", 28, F32), ("mf2", 28, F32), ("far", 28, F32), ("ma", 28, F32), ("mb", 28, F32),
                    ("mmf", 28, F32), ("sup", H, F32), ("sw", H, BF), ("bu", H, BF), ("bl", H, BF), ("sc", 672, F16),
                    ("sa", 9 * H, BF), ("tr", 3 * H, BF), ("mu", C, F16), ("sm", C, F16), ("rr", 28, F32), ("qa", 28, F32),
                    ("qb", 28, F32), ("nn", 28, F32), ("n16", 28, U16), ("m16", 28, U16),
@@ -51,14 +52,19 @@ for _n, _w, _d in (("ut", 512, BF), ("vt", 512, BF), ("mli", 28, I32), ("ones", 
 for _b in range(8):
     SCRATCH["p%d" % _b] = ("psum", [128, 512], "float32")
 
-SEMAPHORES = ["v", "a", "t", "gp"] + ["d%d" % i for i in range(24)]
+SEMAPHORES = ["v", "a", "t", "gp"] + ["d%d" % i for i in range(28)]
 for _s in ROUNDS:
     for _k in ("b", "q", "s"):
         SEMAPHORES += ["arr%s%d" % (_k, _s), "snt%s%d" % (_k, _s)]
 
-ORDER = """wa zl0 zl1 zl2 zl3 zu0 qzl p0:a zu1 al0 s0 al1 l0 p1:a zu2 al2 s1 al3 l1 zu3 p2:a qal s2 qzu l2 o:a
-p3:v au0 s3 au1 l3 au2 p4:v au3 s4 so l4 lo qau ebu p5:v f16:a s5 bu0 l5 t:v f48:a st f80:a lt ebl bu1 mu:v bl0 su bu2 lu
-bl1 f112 nu0 bu3 bl2 bl3 ml nu1 nu2 nu3 sl qu ll xu nl0 nl1 nl2 nl3 ql""".split()
+ORDER = """wa zl0 zl1 zl2 zl3 qzl p0:a zu0 s0 l0 zu1 zu2 al0 p1:a s1 al1 l1 al2 al3 p2:a zu3 qal s2 l2 o:a qzu
+p3:h s3 au0 l3 p4:h au1 au2:v s4 l4 au3 p5:h qau s5 so f16:a t:a l5 f48:k st f80:k lt ebu bu1:v ebl mu:k bu2:v bu3 su
+bl0 bl1 bu0:v bl2 f112:a lu bl3 lo nu0 ml:a nu1 nu2 nu3 sl qu xu0 up ll nl0 nl1 xu1 nl2 xu2 xu3 xl0 nl3 xl1 pr0 xl2
+ql pr1 xl3""".split()
+ORDER1 = """wa zl0 zl1 zl2 zu0 zl3 p0:a qzl zu1 al0 s0 l0 zu2 +unit al2:v al1 p1:a s1 l1 al3 p2:a zu3 qal s2 l2
+p3:a qzu o:a +eq s3 l3 so p4:h au0:v s4 +vq au1 au2 l4 au3 p5:v qau ebu f16:a s5 t:a l5 f48:k st lo lt f80:k bu1:v
+mu:k ebl bu0:v su bu2 bl0 f112:k bl1 bl2 lu bu3:v bl3 nu0 ml:a nu1 nu2 sl nu3 ll xu0 qu nl0 xu1 nl1 nl2 xu2 nl3 xu3
+xl0 up pr0 xl1 ql pr1 xl2 xl3""".split()
 
 
 def rank_program(g, core, T, topo):
@@ -162,8 +168,9 @@ def rank_program(g, core, T, topo):
             op("v", [out], [win, off], lambda: g.vector.tensor_copy(ap(out), ap(win).indirect(ap(off))))
         else:
             k = 8 if q == "h" else 6
-            pick("v", R(out[0], out[1], out[1] + 16 * k), win, R(off[0], off[1], off[1] + k))
-            pick("a", R(out[0], out[1] + 16 * k, out[2]), win, R(off[0], off[1] + k, off[2]))
+            cut = out[1] + 16 * k * out[3]
+            pick("v", R(out[0], out[1], cut, out[3]), win, R(off[0], off[1], off[1] + k))
+            pick("a", R(out[0], cut, out[2], out[3]), win, R(off[0], off[1] + k, off[2]))
 
     def quant(q, x, a=0, b=None):
         o, s = R(q, a, b), R(q + "s", a, b)
@@ -176,10 +183,10 @@ def rank_program(g, core, T, topo):
 
     nd = [0]
 
-    def dma(q, writes, reads, out, in_):
+    def dma(q, writes, reads, out, in_, **how):
         sem = "d%d" % nd[0]
         nd[0] += 1
-        op(q, writes, reads, lambda: Q[q].dma_start(out, in_), sem, 16)
+        op(q, writes, reads, lambda: Q[q].dma_start(out, in_, **how), sem, 16)
 
     def lanes(src, dst):
         return topo.engines(src, dst)[:8]
@@ -202,11 +209,11 @@ def rank_program(g, core, T, topo):
         cnt[sem] = len(lanes(src, core))
         note("g", [], [R(land)], (sem, cnt[sem]))
 
-    dma("a", [R("ut")], [], T.ut[:, :], T.u[:, :])
+    dma("a", [R("mli")], [], T.mli[:, :], T.ml[:, :])
+    dma("s", [R("ut")], [], T.ut[:, :], T.u[:, :])
     dma("s", [R("x0", 0, 4 * H)], [], T.x0[:, 0:4 * H], T.x[:, 0:4 * H])
     dma("s", [R("x0", 4 * H, 4 * C)], [], T.x0[:, 4 * H:4 * C], T.x[:, 4 * H:4 * C])
-    dma("a", [R("mli")], [], T.mli[:, :], T.ml[:, :])
-    dma("s", [R("wq")], [], T.wq[:, :].bitcast(dt.uint8), T.wc[:, :])
+    dma("s", [R("wq")], [R("x0")], T.wq[:, :].bitcast(dt.uint8), T.wc[:, :])
     dma("s", [R("wqs")], [], T.wqs[:, :], T.ws[:, :])
     dma("s", [R("vt")], [], T.vt[:, :], T.v[:, :])
 
@@ -218,53 +225,40 @@ def rank_program(g, core, T, topo):
     iota(R("pi"), [[0, 14]], 0, 1)
     iota(R("fi"), [[1, 16]], 0, 0)
     iota(R("ui"), [[16, 8]], 0, 0)
-    iota(R("io"), [[1, C]], 0, 0)
+    iota(R("io"), [[1, 256]], 0, 0)
+    for a, b, c, st in RUNS:
+        for w in ("f0", "f1"):
+            iota(R(w, c, c + st * (b - a), st), [[1, b - a]], a, 0)
     ts(R("pm"), R("pi"), 15, OP.bitwise_and)
     fill(R("ones"), 1.0)
-    vcopy(R("pmu"), R("pm"))
     vcopy(R("pf"), R("pm", 0, 1))
+    vcopy(R("pmu"), R("pm"))
     vcopy(R("up"), R("ui"))
-    pf, pf1, off, off1, offh, inv = R("pf"), R("pf1"), R("off"), R("off1"), R("offh"), R("inv")
+    pf, pf1, off, offq, offh, inv = R("pf"), R("pf1"), R("off"), R("offq"), R("offh"), R("inv")
     ts(pf1, pf, 1.0, OP.add)
-    ts(off, pf, 15.0, OP.is_lt, LIFT, OP.mult)
     ts(R("ka"), R("fi"), pf, OP.is_equal, -2 * LIFT, OP.mult)
-    ts(R("kc"), R("fi"), pf, OP.not_equal)
+    ts(off, pf, 15.0, OP.is_lt, LIFT, OP.mult)
     ts(R("kb"), R("fi"), pf1, OP.is_equal, LIFT, OP.mult)
+    ts(R("kc"), R("fi"), pf, OP.not_equal)
     ts(R("kd"), R("fi"), pf1, OP.is_equal, MANY - 1, OP.mult)
-    ts(inv, pf, 15.0, OP.is_equal, 1 / MANY, OP.max)
     tt(R("k16"), R("ka"), R("kb"), OP.add)
-    tt(R("m16k"), R("kc"), R("kd"), OP.add)
-    ts(off1, off, 1.0, OP.add)
     ts(offh, off, float(H), OP.add)
+    tt(R("m16k"), R("kc"), R("kd"), OP.add)
+    ts(R("mf"), R("mli"), off, OP.add)
     pick("a", R("keep"), R("k16"), R("pmu"))
     pick("a", R("keepm"), R("m16k"), R("pmu"))
-    for a, b, c, st in RUNS:
-        ts(R("cc", a, b), R("io", 0, b - a), float(st), OP.mult, float(c), OP.add)
-    e, one = R("et"), R("ones")
-    op("g", [e], [one], lambda: g.affine_select(ap(e), ap(one), [[-1, 516]], OP.is_equal, 0.0, 3, 4))
 
-    quant("uq", R("ut"))
-    upk, uqc, uq2 = R("up"), R("uq"), R("uq2")
-    op("v", [uq2], [uqc, upk],
-       lambda: g.vector.tensor_copy(ap(uq2).bitcast(dt.uint32), ap(uqc).bitcast(dt.uint32).indirect(ap(upk))))
-    pick("a", R("uq2s"), R("uqs"), upk)
-    act(R("raw", 0, H), R("cc", 0, H))
-    act(R("raw", H, C), R("io", PORT, PORT + H))
-    act(R("wa", H, C), R("cc", H, C))
-    for a, b, c, st in RUNS:
-        n = b - a
-        for w in ("w0", "w1"):
-            act(R(w, BASE + c, BASE + c + st * n, st), R("cc", a, b))
-        for w in ("f0", "f1"):
-            iota(R(w, c, c + st * n, st), [[1, n]], a, 0)
-
-    def prep(m):
-        ts(R("tt"), m, offh, OP.is_ge, float(H), OP.mult)
-        ts(R("sg"), R("tt"), -2.0, OP.mult, float(H), OP.add)
-        tt(R("mmf"), m, R("tt"), OP.subtract)
-        ts(R("os0"), R("sg"), 1.0, OP.add, off, OP.mult)
-        ts(R("mm"), R("mmf"), off, OP.subtract)
-        tt(R("mf2"), m, R("os0"), OP.subtract)
+    def prep(m, part):
+        if part == 0:
+            ts(R("tt"), m, offh, OP.is_ge, float(H), OP.mult)
+        elif part == 1:
+            ts(R("sg"), R("tt"), -2.0, OP.mult, float(H), OP.add)
+            tt(R("mmf"), m, R("tt"), OP.subtract)
+        elif part == 2:
+            ts(R("os0"), R("sg"), 1.0, OP.add, off, OP.mult)
+            ts(R("mm"), R("mmf"), off, OP.subtract)
+        else:
+            tt(R("mf2"), m, R("os0"), OP.subtract)
 
     def plane(x, half, b):
         act(R("xp%d" % b, half * H, half * H + H), R(x, half * 4 * H + b, half * 4 * H + 4 * H, 4))
@@ -272,19 +266,46 @@ def rank_program(g, core, T, topo):
     def halfcols(x, half):
         return R(x, half * 4 * H, half * 4 * H + 4 * H)
 
-    ts(R("mf"), R("mli"), off, OP.add)
+    def fixed(w):
+        for a, b, c, st in RUNS:
+            vcopy(R(w, BASE + c, BASE + c + st * (b - a), st), R("cc", a, b))
+
+    for k, (a, b, c, st) in enumerate(RUNS):
+        ts(R("cc", a, b), R("io", 0, b - a), float(st), OP.mult, float(c), OP.add)
+        prep(R("mf"), k)
+        if k == 2:
+            quant("uq", R("ut"))
+    ts(inv, pf, 15.0, OP.is_equal, 1 / MANY, OP.max)
+    ts(offq, off, 0.5, OP.add)
+    upk, uqc, uq2 = R("up"), R("uq"), R("uq2")
+    op("v", [uq2], [uqc, upk],
+       lambda: g.vector.tensor_copy(ap(uq2).bitcast(dt.uint32), ap(uqc).bitcast(dt.uint32).indirect(ap(upk))))
+    pick("a", R("uq2s"), R("uqs"), upk)
+    act(R("raw", 0, H), R("cc", 0, H))
+    vcopy(R("wa", H, C), R("cc", H, C))
     quant("qx", halfcols("x0", 0), 0, H)
     mm(0, "uq2", 0, "qx", 0, H)
-    prep(R("mf"))
+    vcopy(R("w1", 0, H), R("cc", 0, H))
+    fixed("w0")
     plane("x0", 0, 0)
-    plane("x0", 0, 1)
+    act(R("raw", H, C), R("io", PORT, PORT + H))
     act(R("sup"), R("p0", 0, H))
     quant("qx", halfcols("x0", 1), H, C)
     mm(1, "uq2", 0, "qx", H, C)
-    plane("x0", 0, 2)
-    plane("x0", 0, 3)
-    vcopy(R("w1", 0, H), R("cc", 0, H))
-    iota(R("f0", PORT, PORT + H), [[1, H]], 0, 0)
+    fixed("w1")
+    for b in range(1, 4):
+        plane("x0", 0, b)
+
+    def once(name):
+        if name == "unit":
+            e, one = R("et"), R("ones")
+            op("g", [e], [one], lambda: g.affine_select(ap(e), ap(one), [[-1, 516]], OP.is_equal, 0.0, 3, 4))
+            iota(R("f0", PORT, PORT + H), [[1, H]], 0, 0)
+        elif name == "eq":
+            for b in range(4):
+                quant("eq", R("et", 3 - b, 515 - b), 128 * b, 128 * b + 128)
+        else:
+            quant("vq", R("vt"))
 
     for s in ROUNDS:
         last = s == ROUNDS[-1]
@@ -295,7 +316,7 @@ def rank_program(g, core, T, topo):
         arrives(land_q, "q", s, peer)
         arrives(land_q + "s", "s", s, peer)
 
-        sw, far, mine = R("sw"), R("far"), R("sc", C + 15, 672, 16)
+        sw, mine = R("sw"), R("sc", C + 15, 672, 16)
         tt(sw, R("sup"), R("p1", 0, H), OP.is_gt)
         pick("v", R("bu"), sw, R("mm", 0, 14))
         pick("a", R("bl"), sw, R("mm", 14, 28))
@@ -305,17 +326,16 @@ def rank_program(g, core, T, topo):
         held(R("sc", C, 672), sw)
         held(R("sc", 0, H), R("bu"))
         held(R("sc", H, C), R("bl"))
-        ts(R("far", 0, 14), mine, off, OP.subtract, -MANY, OP.mult)
-        ts(R("far", 14, 28), mine, off1, OP.subtract, MANY, OP.mult)
-        ts(R("far", 28, 42), mine, off, OP.subtract, -MANY, OP.mult)
+        ts(R("far", 0, 14), mine, offq, OP.subtract, 2 * MANY, OP.mult)
+        ts(R("far", 14, 28), mine, offq, OP.subtract, 2 * MANY, OP.mult)
         tt(R("rr"), R("sc", 15, C, 16), R("sg"), OP.mult)
-        tt(R("ma"), R("mf2"), R("far", 0, 28), OP.add)
-        tt(R("mb"), R("mf2"), R("far", 14, 42), OP.add)
+        tt(R("ma"), R("mf2"), R("far"), OP.add)
+        tt(R("mb"), R("mf2"), R("far"), OP.subtract)
         tt(R("qa"), R("rr"), R("ma"), OP.add)
         tt(R("qb"), R("rr"), R("mb"), OP.add)
-        tt(R("nn", 0, 14), R("qa", 0, 14), R("qa", 14, 28), OP.max)
-        tt(R("nn", 14, 28), R("qb", 0, 14), R("qb", 14, 28), OP.max)
-        vcopy(R("n16"), R("nn"))
+        tt(R("nn", 0, 14), R("qb", 0, 14), R("qa", 14, 28), OP.max)
+        tt(R("nn", 14, 28), R("qa", 0, 14), R("qb", 14, 28), OP.max)
+        ts(R("n16"), R("nn"), MANY, OP.subtract)
         send(peer, land_b, R("n16"), "b", s, False)
         n_up, n_lo = R("n16", 0, 14), R("n16", 14, 28)
         b_up, b_lo = R(land_b, 0, 14), R(land_b, 14, 28)
@@ -342,8 +362,15 @@ def rank_program(g, core, T, topo):
             if name == "wa":
                 pick("a", R("wa", 0, H), R("raw"), n_lo)
             elif kind in ("zu", "zl"):
-                half = kind == "zl"
-                pick_tt(R(kind, k, 4 * H, 4), R("xp%d" % k), (n_up, n_lo)[half], cols(xs, half, k), OP.add)
+                if kind == "zl":
+                    pick_tt(R(kind, k, 4 * H, 4), R("xp%d" % k), n_lo, cols(xs, 1, k), OP.add)
+                else:
+                    pick_tt(R(kind, 4 * DZ + k, 4 * H, 4), R("xp%d" % k), R("n16", DZ // 16, 14), R(xs, 4 * DZ + k, 4 * H, 4), OP.add)
+            elif kind == "gu":
+                pick(q, R("zu", k, 4 * DZ, 4), R("xp%d" % k), R("n16", 0, DZ // 16))
+            elif name == "dz":
+                o, i = R("zu", 0, 4 * DZ), R(xs, 0, 4 * DZ)
+                dma("g", [o], [o, i], ap(o), ap(i), accum_op=OP.add)
             elif name in ("qzl", "qzu"):
                 quant(name, R(name[1:]))
                 for b in range(4):
@@ -358,9 +385,6 @@ def rank_program(g, core, T, topo):
                 quant("qal", R("al"))
                 send(peer, land_q, R("qal"), "q", s, True)
                 send(peer, land_q + "s", R("qals"), "s", s, False)
-                if s == 1:
-                    for b in range(4):
-                        quant("eq", R("et", 3 - b, 515 - b), 128 * b, 128 * b + 128)
             elif name == "qau":
                 quant("qau", R("au"))
             elif name in ("ebl", "ebu"):
@@ -369,6 +393,9 @@ def rank_program(g, core, T, topo):
             elif kind in ("bl", "bu"):
                 half = kind == "bl"
                 copy(q, R("bp%d" % k, half * H, half * H + H), R("p%d" % ((k + (2 if half else 6)) % 8), 0, H))
+            elif kind == "pr":
+                for part in ([] if last else [0] if k == 0 else [1, 2, 3]):
+                    prep(R("sm", 15, C, 16), part)
             elif name in ("p0", "o"):
                 pick(q, row(0) if name == "p0" else R("tr", H, C), R("wa"), b_up if name == "p0" else b_lo)
             elif name[0] == "p":
@@ -409,16 +436,12 @@ def rank_program(g, core, T, topo):
             elif kind in ("nu", "nl"):
                 half = kind == "nl"
                 pick_tt(cols(xn, half, k), R("bp%d" % k), R("m16", 14 * half, 14 * half + 14), cols(xs, half, k), OP.add)
-                if half and not last:
-                    plane(xn, 1, k)
-            elif name == "xu":
+            elif kind in ("xu", "xl"):
                 if not last:
-                    for b in range(4):
-                        plane(xn, 0, b)
-                        if b == 0:
-                            act(R("sup"), R("p0", 0, H))
-                else:
-                    act(R("yo", 0, H), R("p0", 0, H))
+                    plane(xn, kind == "xl", k)
+            elif name == "up":
+                act(R("yo" if last else "sup", 0, H), R("p0", 0, H))
+                if last:
                     dma("s", [], [R("yo", 0, H)], T.y[:, 0:H], T.yo[:, 0:H])
             else:
                 half = name == "ql"
@@ -426,19 +449,18 @@ def rank_program(g, core, T, topo):
                 quant("qx", halfcols(xn, half), c0, c1)
                 mm(int(half), "vq" if last else "uq2", 0, "qx", c0, c1)
                 if last:
+                    for k in range(4 * half):
+                        dma("sa"[k % 2], [], [R("qxs")], T.osc[4 * k:4 * k + 4, :], T.qxs[32 * k:32 * k + 4, :])
                     dma("s", [], [R("qx", c0, c1)], T.oc[:, 4 * c0:4 * c1], T.qx[:, c0:c1].bitcast(dt.uint8))
-                if half and not last:
-                    prep(R("sm", 15, C, 16))
                 if half and last:
                     vcopy(R("yo", H, C), R("p1", 0, H))
                     dma("a", [], [R("yo", H, C)], T.y[:, H:C], T.yo[:, H:C])
-                    for k in range(4):
-                        dma("s" if k < 2 else "a", [], [R("qxs")], T.osc[4 * k:4 * k + 4, :], T.qxs[32 * k:32 * k + 4, :])
 
-        for name in ORDER:
-            if name == "qal" and s == 2:
-                quant("vq", R("vt"))
-            step(*(name + ":a").split(":")[:2])
+        for name in (ORDER1 if s == 1 else ORDER):
+            if name[0] != "+":
+                step(*(name + ":a").split(":")[:2])
+            else:
+                once(name[1:])
 
     for sem in sorted(cnt):
         need("g", sem, cnt[sem])

@@ -1,3 +1,4 @@
+import math
 from concourse.mybir import dt, AluOpType, ActivationFunctionType
 
 OP = AluOpType
@@ -10,6 +11,10 @@ RUNS = [(0, 128, 256, 2), (128, 256, 512, 4), (256, 384, 1024, 8), (384, C, 2048
 CODES = 3072
 BASE = H - PORT
 LIFT, MANY = 512.0, 4096.0
+FAR = 2.0 ** 23
+POWERS = [1, 2, 4, 8, 16, 32]
+NUMBERS = [16, 48, 80]
+LAST = C - 128
 DZ = 0
 
 SCRATCH = {}
@@ -39,15 +44,15 @@ for _n, _w, _d in (("ut", 512, BF), ("vt", 512, BF), ("mli", 28, I32), ("ones", 
                    ("offq", 1, F32), ("offh", 1, F32), ("inv", 1, F32),
                    ("fi", 16, F32), ("ka", 16, F32), ("kb", 16, F32), ("kc", 16, F32), ("kd", 16, F32),
                    ("k16", 16, BF), ("m16k", 16, BF), ("keep", H, BF), ("keepm", H, BF),
-                   ("io", 256, F32), ("cc", C, BF), ("raw", C, BF),
+                   ("cc", C, BF), ("raw", C, BF),
                    ("ui", 8, I32), ("up", 8, U16), ("mm", 28, U16), ("mf", 28, F32), ("sg", 28, F32), ("tt", 28, F32),
-                   ("os0", 28, F32), ("mf2", 28, F32), ("far", 28, F32), ("ma", 28, F32), ("mb", 28, F32),
+                   ("os0", 28, F32), ("mf2", 14, F32), ("sel", 140, F32),
                    ("mmf", 28, F32), ("sup", H, F32), ("sw", H, BF), ("bu", H, BF), ("bl", H, BF), ("sc", 672, F16),
-                   ("sa", 9 * H, BF), ("tr", 3 * H, BF), ("mu", C, F16), ("sm", C, F16), ("rr", 28, F32), ("qa", 28, F32),
-                   ("qb", 28, F32), ("nn", 28, F32), ("n16", 28, U16), ("m16", 28, U16),
-                   ("ls", 126, U16), ("wa", C, BF),
+                   ("sa", 13 * H, BF), ("tr", 3 * H, BF), ("mu", C, F16), ("sm", C, F16), ("rr", 70, F32),
+                   ("nn", 140, F32), ("n16", 28, U16), ("m16", 28, U16),
+                   ("ls", 182, U16), ("wa", C, BF),
                    ("w0", BASE + CODES, BF), ("w1", BASE + CODES, BF), ("f0", CODES, F32), ("f1", CODES, F32),
-                   ("mrow", C, F32), ("yo", C, F32)):
+                   ("ya", 4 * C, BF), ("yb0", C, BF), ("yb1", C, BF), ("yb2", C, BF), ("yb3", C, BF), ("mrow", C, F32), ("yo", C, F32)):
     _sb(_n, _w, _d)
 for _b in range(8):
     SCRATCH["p%d" % _b] = ("psum", [128, 512], "float32")
@@ -57,14 +62,18 @@ for _s in ROUNDS:
     for _k in ("b", "q", "s"):
         SEMAPHORES += ["arr%s%d" % (_k, _s), "snt%s%d" % (_k, _s)]
 
-ORDER = """wa zl0 zl1 zl2 zl3 qzl p0:a zu0 s0 l0 zu1 zu2 al0 p1:a s1 al1 l1 al2 al3 p2:a zu3 qal s2 l2 o:a qzu
-p3:h s3 au0 l3 p4:h au1 au2:v s4 l4 au3 p5:h qau s5 so f16:a t:a l5 f48:k st f80:k lt ebu bu1:v ebl mu:k bu2:v bu3 su
-bl0 bl1 bu0:v bl2 f112:a lu bl3 lo nu0 ml:a nu1 nu2 nu3 sl qu xu0 up ll nl0 nl1 xu1 nl2 xu2 xu3 xl0 nl3 xl1 pr0 xl2
-ql pr1 xl3""".split()
-ORDER1 = """wa zl0 zl1 zl2 zu0 zl3 p0:a qzl zu1 al0 s0 l0 zu2 +unit al2:v al1 p1:a s1 l1 al3 p2:a zu3 qal s2 l2
-p3:a qzu o:a +eq s3 l3 so p4:h au0:v s4 +vq au1 au2 l4 au3 p5:v qau ebu f16:a s5 t:a l5 f48:k st lo lt f80:k bu1:v
-mu:k ebl bu0:v su bu2 bl0 f112:k bl1 bl2 lu bu3:v bl3 nu0 ml:a nu1 nu2 sl nu3 ll xu0 qu nl0 xu1 nl1 nl2 xu2 nl3 xu3
-xl0 up pr0 xl1 ql pr1 xl2 xl3""".split()
+ORDER1 = """+num +keepm +raw wa +far +w0 zl0 zl1 zl2 zl3 p1 qzl zu0 +w1:v +own:v zu1 s1 al0 l1 al1 p2
+al2 al3 zu2 s2 l2 zu3 p4 qal s4 l4 qzu +eq0 +eq1 +eq2 +eq3
+o p8 s8 so au0 l8 p16:h +vq au2 s16 lo l16 au1 au3:v p32:h qau s32 f16:k l32 r:v t st sr lt f48 ebu f80:h lr mu:v bu1
+bu0:v ebl su mr sl lu ll bl0 pr0 nu0 bl1 iu3 il3:v iu2 ju3 il2 jl3 ku3 ju2 jl2 nl0 ku2 kl3 nu1 nl1 kl2 qu xu1 up ql xu3
+pr1 | xl0 xu2 xl1 xu0 xl3 xl2""".split()
+ORDER = """wa zl0 zl1 zl2 zl3 qzl p1 al0 zu0 s1 l1 zu1 p2 zu2 al1 al2 s2 l2 zu3 al3 qal p4 o s4 l4 p8 qzu s8 au0 l8
+p16:h so s16 lo au1 au2 l16 au3:v p32:h qau s32 l32 f16 ebu r:v t st sr lt f48 f80:h lr ebl bu1 mu:v bu0:v su mr sl bl0
+lu bl1 ll iu3 nu0 il3:v ju3 iu2 jl3 pr0 il2 ku3 nu1 jl2 ju2 kl3 ku2 nl0 nl1 kl2 xu3 xu1 qu up ql xl2 pr1 xu0
+| xu2 xl1 xl0 xl3""".split()
+ORDER3 = """wa zl0 zl1 zl2 zl3 p1 qzl zu0 s1 al0 l1 p2 zu1 zu2 al1 s2 al2 al3 l2 p4 o zu3 qal s4 l4 qzu p8:h s8 so l8 lo
+au0 p16:h s16 au1 au2 l16 au3:v p32:h qau f16 t ebu s32 ebl l32 r:v st sr lt f48 f80:k lr mu:k mr bu0:v su bl0 bu1:v lu
+iu2 sl ll iu3 nu0 bl1 il2 il3:v ju3 jl3 ju2 jl2 nu1 ku3 ku2 km2 km3 nl0 qu nm0 nm1 kl3:v qm nl1 kl2:v ql |""".split()
 
 
 def rank_program(g, core, T, topo):
@@ -89,7 +98,7 @@ def rank_program(g, core, T, topo):
         (a, b, s), (c, d, t) = x, y
         if a >= d or c >= b:
             return False
-        return not (s == t and s > 1 and (a - c) % s)
+        return not (a - c) % math.gcd(s, t)
 
     def hazards(q, reads, writes):
         tok = []
@@ -188,11 +197,11 @@ def rank_program(g, core, T, topo):
         nd[0] += 1
         op(q, writes, reads, lambda: Q[q].dma_start(out, in_, **how), sem, 16)
 
-    def lanes(src, dst):
+    def lanes(src, dst, k):
         return topo.engines(src, dst)[:8]
 
     def send(dst, land, src, k, s, codes):
-        e = lanes(core, dst)
+        e = lanes(core, dst, k)
         rid, pid, _ = topo.addr(dst)
         hazards("g", [src], [])
         o, i = T[land][:, 0:src[2] - src[1]], ap(src)
@@ -206,7 +215,7 @@ def rank_program(g, core, T, topo):
 
     def arrives(land, k, s, src):
         sem = "arr%s%d" % (k, s)
-        cnt[sem] = len(lanes(src, core))
+        cnt[sem] = len(lanes(src, core, k))
         note("g", [], [R(land)], (sem, cnt[sem]))
 
     dma("a", [R("mli")], [], T.mli[:, :], T.ml[:, :])
@@ -225,28 +234,27 @@ def rank_program(g, core, T, topo):
     iota(R("pi"), [[0, 14]], 0, 1)
     iota(R("fi"), [[1, 16]], 0, 0)
     iota(R("ui"), [[16, 8]], 0, 0)
-    iota(R("io"), [[1, 256]], 0, 0)
     for a, b, c, st in RUNS:
-        for w in ("f0", "f1"):
-            iota(R(w, c, c + st * (b - a), st), [[1, b - a]], a, 0)
+        iota(R("cc", a, b), [[st, b - a]], c, 0)
+    iota(R("raw", H, C), [[1, H]], PORT, 0)
+    e, one = R("et"), R("ones")
+    iota(one, [[0, 516]], 1, 0)
+    op("g", [e], [one], lambda: g.affine_select(ap(e), ap(one), [[-1, 516]], OP.is_equal, 0.0, 3, 4))
     ts(R("pm"), R("pi"), 15, OP.bitwise_and)
-    fill(R("ones"), 1.0)
+    fill(R("sel", 0, 140, 5), -FAR)
+    fill(R("rr"), -FAR)
     vcopy(R("pf"), R("pm", 0, 1))
     vcopy(R("pmu"), R("pm"))
     vcopy(R("up"), R("ui"))
     pf, pf1, off, offq, offh, inv = R("pf"), R("pf1"), R("off"), R("offq"), R("offh"), R("inv")
     ts(pf1, pf, 1.0, OP.add)
-    ts(R("ka"), R("fi"), pf, OP.is_equal, -2 * LIFT, OP.mult)
     ts(off, pf, 15.0, OP.is_lt, LIFT, OP.mult)
+    ts(R("ka"), R("fi"), pf, OP.is_equal, -2 * LIFT, OP.mult)
     ts(R("kb"), R("fi"), pf1, OP.is_equal, LIFT, OP.mult)
-    ts(R("kc"), R("fi"), pf, OP.not_equal)
-    ts(R("kd"), R("fi"), pf1, OP.is_equal, MANY - 1, OP.mult)
-    tt(R("k16"), R("ka"), R("kb"), OP.add)
     ts(offh, off, float(H), OP.add)
-    tt(R("m16k"), R("kc"), R("kd"), OP.add)
-    ts(R("mf"), R("mli"), off, OP.add)
+    ts(offq, off, 0.5, OP.add)
+    tt(R("k16"), R("ka"), R("kb"), OP.add)
     pick("a", R("keep"), R("k16"), R("pmu"))
-    pick("a", R("keepm"), R("m16k"), R("pmu"))
 
     def prep(m, part):
         if part == 0:
@@ -257,8 +265,17 @@ def rank_program(g, core, T, topo):
         elif part == 2:
             ts(R("os0"), R("sg"), 1.0, OP.add, off, OP.mult)
             ts(R("mm"), R("mmf"), off, OP.subtract)
+        elif part == 3:
+            (n, a, b, st), mid = m, m[1] + 14 * m[3]
+            tt(R("mf2"), (n, a, mid, st), R("os0", 0, 14), OP.subtract)
+            for half in (0, 1):
+                tt(step5(half, 3), (n, mid, b, st), R("os0", 14, 28), OP.subtract)
         else:
-            tt(R("mf2"), m, R("os0"), OP.subtract)
+            for half in (0, 1):
+                tt(step5(half, 1), R("mf2"), step5(half, 3), OP.subtract)
+
+    def step5(half, k):
+        return R("sel", 70 * half + k, 70 * half + 70, 5)
 
     def plane(x, half, b):
         act(R("xp%d" % b, half * H, half * H + H), R(x, half * 4 * H + b, half * 4 * H + 4 * H, 4))
@@ -266,47 +283,52 @@ def rank_program(g, core, T, topo):
     def halfcols(x, half):
         return R(x, half * 4 * H, half * 4 * H + 4 * H)
 
-    def fixed(w):
-        for a, b, c, st in RUNS:
-            vcopy(R(w, BASE + c, BASE + c + st * (b - a), st), R("cc", a, b))
-
-    for k, (a, b, c, st) in enumerate(RUNS):
-        ts(R("cc", a, b), R("io", 0, b - a), float(st), OP.mult, float(c), OP.add)
-        prep(R("mf"), k)
-        if k == 2:
-            quant("uq", R("ut"))
-    ts(inv, pf, 15.0, OP.is_equal, 1 / MANY, OP.max)
-    ts(offq, off, 0.5, OP.add)
+    held_m = R("mf")
+    ts(held_m, R("mli"), off, OP.add)
+    quant("uq", R("ut"))
+    prep(held_m, 0)
     upk, uqc, uq2 = R("up"), R("uq"), R("uq2")
     op("v", [uq2], [uqc, upk],
        lambda: g.vector.tensor_copy(ap(uq2).bitcast(dt.uint32), ap(uqc).bitcast(dt.uint32).indirect(ap(upk))))
     pick("a", R("uq2s"), R("uqs"), upk)
-    act(R("raw", 0, H), R("cc", 0, H))
-    vcopy(R("wa", H, C), R("cc", H, C))
+    prep(held_m, 1)
     quant("qx", halfcols("x0", 0), 0, H)
     mm(0, "uq2", 0, "qx", 0, H)
-    vcopy(R("w1", 0, H), R("cc", 0, H))
-    fixed("w0")
+    prep(held_m, 2)
     plane("x0", 0, 0)
-    act(R("raw", H, C), R("io", PORT, PORT + H))
     act(R("sup"), R("p0", 0, H))
     quant("qx", halfcols("x0", 1), H, C)
     mm(1, "uq2", 0, "qx", H, C)
-    fixed("w1")
+    prep(held_m, 3)
+    ts(R("kc"), R("fi"), pf, OP.not_equal)
+    ts(R("kd"), R("fi"), pf1, OP.is_equal, MANY - 1, OP.mult)
+    ts(inv, pf, 15.0, OP.is_equal, 1 / MANY, OP.max)
     for b in range(1, 4):
         plane("x0", 0, b)
 
-    def once(name):
-        if name == "unit":
-            e, one = R("et"), R("ones")
-            op("g", [e], [one], lambda: g.affine_select(ap(e), ap(one), [[-1, 516]], OP.is_equal, 0.0, 3, 4))
+    def once(name, q):
+        if name in ("w0", "w1"):
+            for a, b, c, st in RUNS:
+                copy(q, R(name, BASE + c, BASE + c + st * (b - a), st), R("cc", a, b))
+        elif name in ("raw", "own"):
+            copy(q, R("raw" if name == "raw" else "w%d" % ((len(POWERS) - 1) % 2), 0, H), R("cc", 0, H))
+        elif name == "far":
+            copy(q, R("wa", H, C), R("cc", H, C))
+        elif name == "keepm":
+            tt(R("m16k"), R("kc"), R("kd"), OP.add)
+            pick("a", R("keepm"), R("m16k"), R("pmu"))
+        elif name == "num":
+            for a, b, c, st in RUNS:
+                for w in ("f0", "f1"):
+                    iota(R(w, c, c + st * (b - a), st), [[1, b - a]], a, 0)
             iota(R("f0", PORT, PORT + H), [[1, H]], 0, 0)
-        elif name == "eq":
-            for b in range(4):
-                quant("eq", R("et", 3 - b, 515 - b), 128 * b, 128 * b + 128)
-        else:
+        elif name == "vq":
             quant("vq", R("vt"))
+        else:
+            b = int(name[2])
+            quant("eq", R("et", 3 - b, 515 - b), 128 * b, 128 * b + 128)
 
+    late = ["xl0", "xl1", "xl2", "xl3"]
     for s in ROUNDS:
         last = s == ROUNDS[-1]
         xs, xn = "x%d" % (s - 1), "x%d" % s
@@ -318,24 +340,25 @@ def rank_program(g, core, T, topo):
 
         sw, mine = R("sw"), R("sc", C + 15, 672, 16)
         tt(sw, R("sup"), R("p1", 0, H), OP.is_gt)
-        pick("v", R("bu"), sw, R("mm", 0, 14))
-        pick("a", R("bl"), sw, R("mm", 14, 28))
-        if s == 1:
-            for b in range(4):
-                plane(xs, 1, b)
+        prep(held_m, 4)
         held(R("sc", C, 672), sw)
-        held(R("sc", 0, H), R("bu"))
+        pick("a", R("bl"), sw, R("mm", 14, 28))
+        pick("v", R("bu"), sw, R("mm", 0, 14))
+        for name in late:
+            plane(xs, name[1] == "l", int(name[2]))
+        ts(step5(0, 2), mine, offq, OP.subtract, -4 * MANY, OP.mult)
+        ts(step5(0, 4), mine, offq, OP.subtract, 2 * MANY, OP.mult)
         held(R("sc", H, C), R("bl"))
-        ts(R("far", 0, 14), mine, offq, OP.subtract, 2 * MANY, OP.mult)
-        ts(R("far", 14, 28), mine, offq, OP.subtract, 2 * MANY, OP.mult)
-        tt(R("rr"), R("sc", 15, C, 16), R("sg"), OP.mult)
-        tt(R("ma"), R("mf2"), R("far"), OP.add)
-        tt(R("mb"), R("mf2"), R("far"), OP.subtract)
-        tt(R("qa"), R("rr"), R("ma"), OP.add)
-        tt(R("qb"), R("rr"), R("mb"), OP.add)
-        tt(R("nn", 0, 14), R("qb", 0, 14), R("qa", 14, 28), OP.max)
-        tt(R("nn", 14, 28), R("qa", 0, 14), R("qb", 14, 28), OP.max)
-        ts(R("n16"), R("nn"), MANY, OP.subtract)
+        held(R("sc", 0, H), R("bu"))
+        ts(step5(1, 2), mine, offq, OP.subtract, 4 * MANY, OP.mult)
+        tt(R("rr", 2, 70, 5), R("sc", H + 15, C, 16), R("sg", 14, 28), OP.mult)
+        tt(R("rr", 0, 70, 5), R("sc", 15, H, 16), R("sg", 0, 14), OP.mult)
+        ts(step5(1, 4), mine, offq, OP.subtract, -2 * MANY, OP.mult)
+        for half in (0, 1):
+            o, d0, d1 = R("nn", 70 * half, 70 * half + 70), R("sel", 70 * half, 70 * half + 70), R("rr")
+            op("v", [o], [d0, d1], lambda: g.vector.tensor_tensor_scan(ap(o), ap(d0), ap(d1), 0.0, OP.add, OP.max))
+        ts(R("n16"), R("nn", 4, 140, 5), MANY, OP.subtract)
+        held_m = R("sm", 15, C, 16)
         send(peer, land_b, R("n16"), "b", s, False)
         n_up, n_lo = R("n16", 0, 14), R("n16", 14, 28)
         b_up, b_lo = R(land_b, 0, 14), R(land_b, 14, 28)
@@ -349,13 +372,10 @@ def rank_program(g, core, T, topo):
         def codes(k):
             return R("w%d" % (k % 2), BASE)
 
-        def ports(w):
-            return R(w, PORT, PORT + H)
-
         def lst(k):
             return R("ls", 14 * k, 14 * k + 14)
 
-        mrow = {}
+        mrow, top = {}, len(POWERS) - 1
 
         def step(name, q):
             kind, k = name[:2], int(name[-1]) if name[-1].isdigit() else 0
@@ -387,6 +407,8 @@ def rank_program(g, core, T, topo):
                 send(peer, land_q + "s", R("qals"), "s", s, False)
             elif name == "qau":
                 quant("qau", R("au"))
+            elif kind in ("el", "eu"):
+                mm((k + (2 if kind == "el" else 6)) % 8, "eq", 128 * k, land_q if kind == "el" else "qau", 0, H)
             elif name in ("ebl", "ebu"):
                 for b in range(4):
                     mm((b + (2 if name == "ebl" else 6)) % 8, "eq", 128 * b, land_q if name == "ebl" else "qau", 0, H)
@@ -396,71 +418,94 @@ def rank_program(g, core, T, topo):
             elif kind == "pr":
                 for part in ([] if last else [0] if k == 0 else [1, 2, 3]):
                     prep(R("sm", 15, C, 16), part)
-            elif name in ("p0", "o"):
-                pick(q, row(0) if name == "p0" else R("tr", H, C), R("wa"), b_up if name == "p0" else b_lo)
+            elif name in ("p1", "o"):
+                pick(q, row(0) if name == "p1" else R("tr", C, C + H), R("wa"), b_up if name == "p1" else b_lo)
             elif name[0] == "p":
-                pick(q, row(k), codes(k - 1), lst(k - 1))
+                k = POWERS.index(int(name[1:]))
+                pick(q, row(k), codes(k - 1), lst(POWERS.index(POWERS[k] - POWERS[k - 1])))
             elif name in ("su", "sl"):
                 half = name == "sl"
                 held(R("sm", half * H, half * H + H), mrow[half])
             elif name in ("lu", "ll"):
                 half = name == "ll"
                 ts(R("m16", 14 * half, 14 * half + 14), R("sm", half * H + 15, half * H + H, 16), off, OP.subtract)
+            elif name == "lm":
+                ts(R("m16"), R("sm", 15, C, 16), off, OP.subtract)
+            elif name == "lw":
+                ts(R("ls", 14 * top + 14, 14 * top + 42), R("sa", (top + 1) * H + 15, (top + 3) * H, 16), inv, OP.mult)
             elif name[0] in "sl":
-                k = {"t": 6, "o": 7, "r": 8}.get(name[1], k)
+                k = top + 1 + "tro".index(name[1]) if name[1] in "tro" else POWERS.index(int(name[1:]))
                 if name[0] == "s":
-                    heldm(R("sa", k * H, k * H + H), row(k) if k < 6 else R("tr", (k - 6) * H, (k - 5) * H))
+                    heldm(R("sa", k * H, k * H + H), row(k) if k <= top else R("tr", (k - top - 1) * H, (k - top) * H))
                 else:
                     ts(lst(k), R("sa", k * H + 15, k * H + H, 16), inv, OP.mult)
             elif name == "t":
-                pick(q, R("tr", 0, H), R("w1", 0, C), n_up)
+                pick(q, R("tr", 0, H), R("w%d" % (top % 2), 0, C), n_up)
             elif name == "r":
-                pick(q, R("tr", C, C + H), codes(5), lst(7))
-            elif name == "f16":
-                pick(q, ports("f1"), R("f0"), lst(4))
-            elif name == "f48":
-                pick(q, ports("f0"), R("f1"), lst(5))
-            elif name == "f80":
-                pick(q, ports("f1"), R("f0"), lst(5))
-            elif name == "f112":
-                pick(q, ports("f0"), R("f1"), lst(5))
+                pick(q, R("tr", H, C), codes(top), lst(top + 3))
+            elif name[0] == "f":
+                k = NUMBERS.index(int(name[1:]))
+                pick(q, R("f%d" % ((k + 1) % 2), PORT, PORT + H), R("f%d" % (k % 2)),
+                     lst(POWERS.index(NUMBERS[k] - ([0] + NUMBERS)[k])))
             elif name in ("mu", "ml", "mr"):
                 half = name != "mu"
-                win, at = R("f0" if name == "ml" else "f1"), lst({"mu": 6, "ml": 7, "mr": 8}[name])
+                k = len(NUMBERS) if name == "ml" else [n + POWERS[-1] >= H // 2 for n in NUMBERS].index(True) + 1
+                win, at = R("f%d" % (k % 2)), lst(top + {"mu": 1, "ml": 3, "mr": 2}[name])
                 mrow[half] = R("mu" if q == "v" else "mrow", half * H, half * H + H)
                 pick(q, mrow[half], win, at)
                 if last and q == "v":
                     pick("a", R("mrow", half * H, half * H + H), win, at)
                 if last and half:
                     dma("s", [], [R("mrow")], T.mo[:, :], T.mrow[0:128:16, :])
-            elif kind in ("nu", "nl"):
-                half = kind == "nl"
-                pick_tt(cols(xn, half, k), R("bp%d" % k), R("m16", 14 * half, 14 * half + 14), cols(xs, half, k), OP.add)
+            elif kind in ("nu", "nm", "nl"):
+                c0, c1 = {"nu": (0, H), "nm": (H, LAST), "nl": (LAST if last else H, C)}[kind]
+                if last or kind != "nm":
+                    pick_tt(R(xn, 4 * c0 + k, 4 * c1, 4), R("bp%d" % k), R("m16", c0 // 16, c1 // 16),
+                            R(xs, 4 * c0 + k, 4 * c1, 4), OP.add)
+            elif kind in ("iu", "il"):
+                half = kind == "il"
+                pick(q, R("ya", k * C + half * H, k * C + half * H + H), R("xp%d" % k), R("m16", 14 * half, 14 * half + 14))
+            elif kind == "ia":
+                pick(q, R("ya", k * C, k * C + C), R("xp%d" % k), R("m16"))
+            elif kind == "ka":
+                pick(q, R(xn, k, 4 * C, 4), R("yb%d" % k), R("m16"))
+            elif kind in ("ju", "jl"):
+                half = kind == "jl"
+                tt(R("yb%d" % k, half * H, half * H + H), R("ya", k * C + half * H, k * C + half * H + H),
+                   R("p%d" % ((k + (2 if half else 6)) % 8), 0, H), OP.add)
+            elif kind in ("ku", "km", "kl"):
+                c0, c1 = {"ku": (0, H), "km": (H, LAST), "kl": (LAST if last else H, C)}[kind]
+                if last or kind != "km":
+                    pick(q, R(xn, 4 * c0 + k, 4 * c1, 4), R("yb%d" % k), R("m16", c0 // 16, c1 // 16))
             elif kind in ("xu", "xl"):
                 if not last:
                     plane(xn, kind == "xl", k)
             elif name == "up":
-                act(R("yo" if last else "sup", 0, H), R("p0", 0, H))
-                if last:
-                    dma("s", [], [R("yo", 0, H)], T.y[:, 0:H], T.yo[:, 0:H])
+                if not last:
+                    act(R("sup"), R("p0", 0, H))
+            elif not last:
+                if name != "qm":
+                    half = name == "ql"
+                    quant("qx", halfcols(xn, half), half * H, half * H + H)
+                    mm(int(half), "uq2", 0, "qx", half * H, half * H + H)
             else:
-                half = name == "ql"
-                c0, c1 = half * H, half * H + H
-                quant("qx", halfcols(xn, half), c0, c1)
-                mm(int(half), "vq" if last else "uq2", 0, "qx", c0, c1)
-                if last:
-                    for k in range(4 * half):
-                        dma("sa"[k % 2], [], [R("qxs")], T.osc[4 * k:4 * k + 4, :], T.qxs[32 * k:32 * k + 4, :])
-                    dma("s", [], [R("qx", c0, c1)], T.oc[:, 4 * c0:4 * c1], T.qx[:, c0:c1].bitcast(dt.uint8))
-                if half and last:
-                    vcopy(R("yo", H, C), R("p1", 0, H))
-                    dma("a", [], [R("yo", H, C)], T.y[:, H:C], T.yo[:, H:C])
+                k = ("qu", "qm", "ql").index(name)
+                c0, c1 = (0, LAST - 128, LAST, C)[k:k + 2]
+                quant("qx", R(xn, 4 * c0, 4 * c1), c0, c1)
+                mm(k, "vq", 0, "qx", c0, c1)
+                for j in range(4 * (k == 2)):
+                    dma("sa"[j % 2], [], [R("qxs")], T.osc[4 * j:4 * j + 4, :], T.qxs[32 * j:32 * j + 4, :])
+                dma("s", [], [R("qx", c0, c1)], T.oc[:, 4 * c0:4 * c1], T.qx[:, c0:c1].bitcast(dt.uint8))
+                copy("aav"[k], R("yo", c0, c1), R("p%d" % k, 0, c1 - c0))
+                dma("a", [], [R("yo", c0, c1)], T.y[:, c0:c1], T.yo[:, c0:c1])
 
-        for name in (ORDER1 if s == 1 else ORDER):
+        order = ORDER1 if s == 1 else ORDER3 if last else ORDER
+        late = order[order.index("|") + 1:]
+        for name in order[:order.index("|")]:
             if name[0] != "+":
                 step(*(name + ":a").split(":")[:2])
             else:
-                once(name[1:])
+                once(*(name[1:] + ":a").split(":")[:2])
 
-    for sem in sorted(cnt):
+    for sem in sorted(cnt, key=lambda k: nd[0] + int(k[1:]) if k[1:].isdigit() else 0):
         need("g", sem, cnt[sem])

@@ -2,7 +2,7 @@ import math
 from concourse.mybir import dt, AluOpType, ActivationFunctionType
 
 OP = AluOpType
-COPY = ActivationFunctionType.Copy
+COPY, SAME = ActivationFunctionType.Copy, ActivationFunctionType.Identity
 C, H = 448, 224
 ROUNDS = [1, 2, 3]
 F16, BF, F32, I32, U16, U8, MX = "float16", "bfloat16", "float32", "int32", "uint16", "uint8", "float8_e4m3fn_x4"
@@ -10,12 +10,9 @@ PORT = 32
 RUNS = [(0, 128, 256, 2), (128, 256, 512, 4), (256, 384, 1024, 8), (384, C, 2048, 16)]
 CODES = 3072
 BASE = H - PORT
-LIFT, MANY = 512.0, 4096.0
-FAR = 2.0 ** 23
+LIFT, MANY, BIT = 512.0, 4096.0, 2.0
 POWERS = [1, 2, 4, 8, 16, 32]
-NUMBERS = [16, 48, 80]
-LAST = C - 128
-DZ = 0
+NUMBERS = [16, 48, 80, 112]
 
 SCRATCH = {}
 
@@ -29,51 +26,218 @@ for _r in range(4):
 for _b in range(4):
     _sb("xp%d" % _b, C, BF)
     _sb("bp%d" % _b, C, BF)
-for _n in ("zl", "zu", "al", "au"):
-    _sb(_n, 4 * H, BF)
-for _n, _w in (("uq", 128), ("uq2", 128), ("vq", 128), ("wq", 512), ("eq", 512), ("qx", C), ("qzl", H), ("qzu", H),
-               ("qal", H), ("qau", H)):
+    _sb("yb%d" % _b, C, BF)
+for _n in ("zz", "aa", "ya"):
+    _sb(_n, 4 * C, BF)
+for _n, _w in (("uq", 128), ("uq2", 128), ("vq", 128), ("wq", 512), ("eq", 512), ("qx", C), ("qz", C), ("qa", C)):
     _sb(_n, _w, MX)
     _sb(_n + "s", _w, U8)
 for _s in ROUNDS:
-    _sb("lq%d" % _s, H, MX)
-    _sb("lq%ds" % _s, H, U8)
+    _sb("lq%d" % _s, C, MX)
+    _sb("lq%ds" % _s, C, U8)
     _sb("lb%d" % _s, 28, U16)
+    _sb("lc%d" % _s, 14, U16)
 for _n, _w, _d in (("ut", 512, BF), ("vt", 512, BF), ("mli", 28, I32), ("ones", 516, BF), ("et", 516, BF),
                    ("pi", 14, I32), ("pm", 14, I32), ("pmu", 14, U16), ("pf", 1, F32), ("pf1", 1, F32), ("off", 1, F32),
-                   ("offq", 1, F32), ("offh", 1, F32), ("inv", 1, F32),
+                   ("offm", 1, F32), ("ofb", 1, F32), ("ofb1", 1, F32), ("nofb", 1, F32), ("inv", 1, F32),
                    ("fi", 16, F32), ("ka", 16, F32), ("kb", 16, F32), ("kc", 16, F32), ("kd", 16, F32),
-                   ("k16", 16, BF), ("m16k", 16, BF), ("keep", H, BF), ("keepm", H, BF),
+                   ("k16", 16, BF), ("m16k", 16, BF), ("keep", C, BF), ("keepb", C, BF), ("keepm", C, BF),
                    ("cc", C, BF), ("raw", C, BF),
                    ("ui", 8, I32), ("up", 8, U16), ("mm", 28, U16), ("mf", 28, F32), ("sg", 28, F32), ("tt", 28, F32),
-                   ("os0", 28, F32), ("mf2", 14, F32), ("sel", 140, F32),
-                   ("mmf", 28, F32), ("sup", H, F32), ("sw", H, BF), ("bu", H, BF), ("bl", H, BF), ("sc", 672, F16),
-                   ("sa", 13 * H, BF), ("tr", 3 * H, BF), ("mu", C, F16), ("sm", C, F16), ("rr", 70, F32),
+                   ("os0", 28, F32), ("sel", 140, F32),
+                   ("mmf", 28, F32), ("sup", H, F32), ("sw", H, BF), ("bb", C, BF), ("sc", 672, BF),
+                   ("sa", 12 * H, BF), ("tr", 3 * H, BF), ("mu", C, BF), ("sm", C, F16), ("rr", 140, F32),
                    ("nn", 140, F32), ("n16", 28, U16), ("m16", 28, U16),
-                   ("ls", 182, U16), ("wa", C, BF),
-                   ("w0", BASE + CODES, BF), ("w1", BASE + CODES, BF), ("f0", CODES, F32), ("f1", CODES, F32),
-                   ("ya", 4 * C, BF), ("yb0", C, BF), ("yb1", C, BF), ("yb2", C, BF), ("yb3", C, BF), ("mrow", C, F32), ("yo", C, F32)):
+                   ("ls", 168, U16), ("wa", C, BF),
+                   ("w0", BASE + CODES, BF), ("w1", BASE + CODES, BF), ("f0", BASE + CODES, BF), ("f1", BASE + CODES, BF),
+                   ("mrow", C, F32), ("yo", C, F32)):
     _sb(_n, _w, _d)
 for _b in range(8):
     SCRATCH["p%d" % _b] = ("psum", [128, 512], "float32")
 
 SEMAPHORES = ["v", "a", "t", "gp"] + ["d%d" % i for i in range(28)]
 for _s in ROUNDS:
-    for _k in ("b", "q", "s"):
+    for _k in ("b", "c", "q", "s"):
         SEMAPHORES += ["arr%s%d" % (_k, _s), "snt%s%d" % (_k, _s)]
 
-ORDER1 = """+num +keepm +raw wa +far +w0 zl0 zl1 zl2 zl3 p1 qzl zu0 +w1:v +own:v zu1 s1 al0 l1 al1 p2
-al2 al3 zu2 s2 l2 zu3 p4 qal s4 l4 qzu +eq0 +eq1 +eq2 +eq3
-o p8 s8 so au0 l8 p16:h +vq au2 s16 lo l16 au1 au3:v p32:h qau s32 f16:k l32 r:v t st sr lt f48 ebu f80:h lr mu:v bu1
-bu0:v ebl su mr sl lu ll bl0 pr0 nu0 bl1 iu3 il3:v iu2 ju3 il2 jl3 ku3 ju2 jl2 nl0 ku2 kl3 nu1 nl1 kl2 qu xu1 up ql xu3
-pr1 | xl0 xu2 xl1 xu0 xl3 xl2""".split()
-ORDER = """wa zl0 zl1 zl2 zl3 qzl p1 al0 zu0 s1 l1 zu1 p2 zu2 al1 al2 s2 l2 zu3 al3 qal p4 o s4 l4 p8 qzu s8 au0 l8
-p16:h so s16 lo au1 au2 l16 au3:v p32:h qau s32 l32 f16 ebu r:v t st sr lt f48 f80:h lr ebl bu1 mu:v bu0:v su mr sl bl0
-lu bl1 ll iu3 nu0 il3:v ju3 iu2 jl3 pr0 il2 ku3 nu1 jl2 ju2 kl3 ku2 nl0 nl1 kl2 xu3 xu1 qu up ql xl2 pr1 xu0
-| xu2 xl1 xl0 xl3""".split()
-ORDER3 = """wa zl0 zl1 zl2 zl3 p1 qzl zu0 s1 al0 l1 p2 zu1 zu2 al1 s2 al2 al3 l2 p4 o zu3 qal s4 l4 qzu p8:h s8 so l8 lo
-au0 p16:h s16 au1 au2 l16 au3:v p32:h qau f16 t ebu s32 ebl l32 r:v st sr lt f48 f80:k lr mu:k mr bu0:v su bl0 bu1:v lu
-iu2 sl ll iu3 nu0 bl1 il2 il3:v ju3 jl3 ju2 jl2 nu1 ku3 ku2 km2 km3 nl0 qu nm0 nm1 kl3:v qm nl1 kl2:v ql |""".split()
+SPANS = {"u": (0, 14), "l": (14, 28), "w": (0, 28), "": (0, 14)}
+ORDERS = [[], [], []]
+ORDERS = [o.split() for o in """+pm +pf +ofb +ofb1 +ka +pf1 +nofb +off +up +offm +kd +sel0 +kb +k16 +pmu +keepb +sel2 +inv +sel1 +kc +mf Ptt +uq Pmf +uq2s Psg
+x2@u Pos Pmm +uq2 x1.v@u +m16k q0@0-12 x3.v@u q1@12-20 Pq q2@20-28 x0@u u0@0-12 u1@12-14 x1.v@l Tsw1@14-20 x2@l
+Tsw2@20-28 Pdq Tb@l Tb.v@u Tso Th@l +raw Tc0 x3@l Th@u Tr1 Tr4 Tc1 Tr2 Tn0 +far Tn1 Tn@u x0@l +w0 Tn@l +num z1@u z3@l z0@l
+z1@l z2@l +keepm qz@l +w1.v z3@u wa z0@u z2@u a0@l a1@l p1 s1 a3@l l1 a2@l p2 o qz@u qa@l +eq1 s2 l2 p4.8 a0@u a1@u s4 +eq2
+l4 p8.8 s8 a2@u l8 +eq0 a3@u +eq3 p16 qa@u s16 e3@u l16 +keep e2@u e1@u p32.8 e0@u f16 so s32 e3@l l32 e1@l f48.8 lo f80.8
++vq f112.6 my b0@u b1@u mx.v m@u m@l e2@l ml@u ml@l n0@u i3@u i2@u i3.v@l j3@u e0@l j3@l i2@l b1@l k3@u j2@u j2@l b0@l n1@u
+k2@l k2@u n1@l k3@l n0@l
+----
+x2@l q0@u u0@u Ptt Psg q1@l Pmf Pos Pmm Tsw1@l Pq Tb.v@u Tb@l x0@u Tso Pdq Th@l Th@u Tc1 Tc0 x0@l x3@l x1@u Tr1 Tr4 Tr2
+x1@l Tn0 Tn1 Tn@u Tn@l z0@u x3@u z1@l x2@u wa z0@l p1 z2@l z3@l qz@l s1 l1 a0@l p2 a2@l z2@u z1@u a3@l s2 a1@l l2 p4 z3@u
+qa@l s4 l4 qz@u o p8.4 s8 l8 a0@u p16.8 a1@u so a2@u s16 lo l16 p32.8 s32 l32 a3.v@u f16 qa@u f48 f80.8 f112.8 mx.v e0@u
+m@u e2@u my b0@u m@l ml@u e1@u ml@l n0@u e3@u b1@u e2@l i3@u e1@l e3@l i3.v@l e0@l Ptt' j3@u i2@l j2@l i2@u b0@l j3@l j2@u
+b1@l n0@l k3@u n1@u k3@l k2@u k2@l Psg' n1@l
+----
+q0@u x1@u q1@l Pos Pmf x3.v@u u0@u Pq x0@u Pmm Tsw1@l Pdq Tb.v@u Tb@l Tso Th@l x1@l Tc0 Th@u Tr1 x0@l Tr4 Tc1 x3@l x2@l
+x2@u Tr2 Tn0 Tn1 Tn@u Tn@l z3@l z1@l z0@l z2@l wa p1 z0@u qz@l s1 a0@l l1 z1@u p2 a2@l z2@u s2 a1@l l2 z3@u a3@l p4 qa@l s4
+o l4 qz@u p8.4 s8 l8 a0@u p16.8 a1@u a2@u so s16 l16 a3.v@u p32.6 s32 lo l32 qa@u e0@u f16 f48.4 f80.8 f112.8 e2@u b0@u
+mx.v m@u e1@u my m@l ml@u b1@u ml@l e3@u e0@l e2@l mo e3@l e1@l i2@u i3.v@u i2@l n0@u j3@u i3@l j2@u j2@l b1@l k2@u j3@l
+n1@u k3.4@u b0@l y0@0-12 k2.v@14-20 n0@20-28 n1@14-20 k3@14-20 k3@20-28 n0@14-20 y1@12-20 k2.v@20-28 n1@20-28 y2.v@20-28""".split("----")]
+ORDERS = [o.split() for o in """+pm +pf +off +ka +offm +up +pf1 +kb +ofb +pmu +k16 +keepb +sel0 +ofb1 +nofb +sel2 +sel1 +mf Ptt +inv +kc +uq Psg.v +uq2s +kd x3@u +uq2 Pos.v
+q0@0-12 x0.v@u Pq +m16k u0@0-12 x1@u x2.v@u Pmf Pdq q1@12-20 q2@20-28 x3@l u1@12-14 Pmm Tsw1@14-20
+Tsw2@20-28 Tso Tb@l Tb.v@u Th@l Th@u Tr1 Tr4 x1@l Tr2 Tc0 Tc1 Tn0 Tn1 Tn@u Tn@l x0@l z1@u +num x2@l +far +raw z0@l z2@l
++keepm z1@l wa z3@l z2@u qz@l z3@u +eq2 +w0 a0@l +w1.v a1@l p1 z0@u s1 l1 qz@u a3@l a2@l p2 qa@l +eq1 s2 l2 o +eq0 p4.6
+a1@u s4 a0@u l4 p8.8 s8 l8 a2@u a3@u +eq3 qa@u e0@u e2@u p16 +vq e3@u +keep s16 l16 p32.8 so f16 e1@u s32 l32 f48.8 f80.8
+lo f112.6 b0@u my e0@l mx.v e1@l m@u m@l b1@u e2@l b0@l ml@u ml@l i3.v@l i3@u n0@u i2@u e3@l j3@u j3@l j2@u i2@l b1@l j2@l
+n1@l k3@u k2@u n1@u k3@l k2@l n0@l
+----
+q0@u q1@l Ptt x2@l u0@u Pmf Psg.v Pmm Tsw1@l Pos Pq x0@l Tso Tb@l Tb.10@u Tc0 Pdq Th@l Th@u Tr1 Tr4 Tr2 x0@u Tc1 Tn0 x3@u
+x3@l x2@u Tn1 Tn@u x1@u x1@l Tn@l wa z0@u z0@l p1 z3@l z1@l z2@l qz@l s1 l1 z1@u a0@l p2 a2@l a1@l z2@u a3@l s2 l2 z3@u p4
+qa@l s4 l4 qz@u o p8.4 s8 a0@u l8 so p16.8 a1@u s16 a2@u l16 p32.8 s32 lo f16 l32 a3.v@u qa@u e1@u f48 e0@u e0@l e2@l e3@l
+f80.8 f112.8 e3@u b1@u mx.v e1@l m@u my m@l e2@u b0@u ml@u b0@l ml@l Ptt' i3@u i3.v@l n0@u i2@l i2@u j3@l j3@u b1@l n0@l
+k3@l j2@l j2@u n1@u k3@u n1@l k2@u Psg' k2@l
+----
+x0@u q0@u q1@l Pos Pmf Pq Pmm u0@u Tsw1@l Pdq Tso Tb@l x1@u Tc0 x3@l Tc1 x0@l Tb.v@u x1@l Th@l Th@u Tr4 x2@u x3@u Tr1 Tr2
+Tn0 Tn1 Tn@u Tn@l wa z0@l x2@l z1@l z3@l z2@l z0@u qz@l p1 s1 l1 z1@u z2@u a0@l p2 s2 a1@l l2 z3@u a2@l a3@l p4 qa@l s4 o
+l4 qz@u p8.4 a0@u s8 so l8 p16.8 a1@u s16 l16 lo a2@u p32.6 f16 a3.v@u s32 l32 qa@u f48.4 f80.8 f112.8 my e0@u mx.v m@u
+e1@u m@l ml@u b1@u e2@u b0@u ml@l e3@u e0@l i3.8@u mo e2@l i2.v@u j3@u j2@u b0@l i2@l e1@l i3@l e3@l n0@u j2@l j3@l b1@l
+n1@u k2@u k3.4@u k2@14-20 y0@0-12 k3@14-20 n1@14-20 n0@20-28 k3@20-28 k2.4@20-28 n0@14-20 y1@12-20 n1@20-28 y2.v@20-28""".split("----")]
+ORDERS = [o.split() for o in """+pm +pf +ka +pf1 +off +ofb +pmu +kb +k16 +keepb +sel0 +offm +sel2 +up +sel1 +nofb +ofb1 +mf Ptt +kc +inv +uq Psg.v +raw +uq2s Pos.v +uq2
+x1.v@u +kd Pq q0@0-12 +m16k Pdq x0@u Pmf Pmm q1@12-20 u0@0-12 x2@u x3@u +far q2@20-28 u1.v@12-14
+Tsw1@14-20 Tsw2@20-28 Tb@l Tso Tb.10@u Tc0.v x1@l Th@l Th@u Tr1 Tr4 x3@l Tr2 x0@l Tc1.v Tn0 x2@l Tn1 Tn@w z1@l +w0 z2@l
+z0@l +num z3@l z2@u wa qz@l +eq2 +keepm a0@l z0@u z1@u z3@u a1@l p1 a2@l +w1.v s1 l1 qz@u +eq1 a3@l p2 qa@l s2 l2 +eq0 o
+p4.6 a1@u s4 l4 a0@u p8.6 a3@u a2@u s8 l8 +eq3 +vq p16 qa@u s16 l16 +keep p32.8 e0@u s32 e1@u f16 so e0@l l32 f48.8 f80.8
+lo f112.8 e1@l e3@l my mx.v m@l m@u e3@u ml@l b1@u e2@l b0@u ml@u b0@l e2@u i3@u i2@u i3.v@l n0@u j3@l i2@l j3@u b1@l j2@u
+j2@l n1@u k3@l k2@u n0@l k3@u k2@l n1@l
+----
+q0@u Ptt q1@l Pmf Psg.v Pmm u0@u Pos.v Tsw1@l Tb@l Pq Tb.10@u Tso x0@u Pdq Th@l Tc0.v Th@u x0@l Tr1 Tr4 Tr2 Tc1.v Tn0 x2@u
+Tn1 x1@u Tn@w x1@l x2@l z0@l x3@l z1@l x3@u z3@l z2@l wa qz@l z0@u p1 a0@l s1 l1 z1@u a1@l p2 a2@l z2@u s2 l2 a3@l qa@l
+z3@u p4 s4 l4 qz@u o p8.4 s8 l8 a0@u p16.8 a1@u s16 a2@u l16 p32.8 s32 so l32 a3.v@u qa@u e0@u e2@u f16 e1@u f48 e0@l e3@l
+e1@l f80.8 lo f112.8 e3@u my mx.v b1@u e2@l m@u b0@u m@l ml@u b0@l i3@u ml@l Ptt' i3.v@l n0@u j3@u i2@l i2@u b1@l j3@l j2@l
+k3@u j2@u n1@u n1@l k3@l k2@u k2@l n0@l
+----
+q0@u Psg.v x1@l q1@l Pos.v Pmf x1@u Pq u0@u Pmm Tsw1@l Pdq Tso x0@u Tb@l Tb.10@u Tc0.v x0@l Th@l Th@u x3@l Tr1 x2@u Tr4 Tr2
+Tc1.v Tn0 Tn1 Tn@w x2@l z0@l wa z1@l z2@l x3@u p1 z3@l z0@u qz@l s1 l1 a0@l z1@u p2 z2@u s2 a3@l l2 a2@l a1@l p4 z3@u qa@l
+s4 l4 qz@u o p8.4 so s8 a0@u l8 p16.8 a1@u s16 l16 a2@u p32.6 f16 a3.v@u s32 l32 qa@u f48.4 lo e3@u f80.8 e1@u f112.8 my
+e0@u mx.v e2@u b0@u m@u b1@u m@l ml@u ml@l i3.8@u i2.v@u e0@l e1@l mo b0@l j3@u e2@l j2@u i2@l n0@u i3@l e3@l j2@l j3@l
+b1@l k2@u n1@u k3.4@u k3@14-20 y0@0-12 k2@14-20 k2@20-28 n0@14-20 k3.4@20-28 n0@20-28 n1@14-20 y1@12-20 n1@20-28 y2.v@20-28""".split("----")]
+ORDERS = [o.split() for o in """+pm +sel0 +sel1 +sel2 +pf +pmu +up +pf1 +off +ofb +ka +kb +offm +ofb1 +nofb +k16 +keepb +mf +uq Ptt +uq2 +uq2s Psg.v Pmf q0@u Pos.v Pmm
+x0@u u0@u q1@l Pq +kc +kd +inv x1@u x2@u x3@u
+Tsw1@l Pdq Tso Tb@l Tb.v@u x0@l x1@l x2@l x3@l Tc0.v Tc1.v Th@l Th@u Tr1 Tr4 Tr2 Tn0 Tn1 Tn@w
++num +m16k +keepm +raw wa +far +w0 z0@l z1@l z2@l z3@l p1 qz@l z0@u +w1.v +own.v z1@u s1 a0@l l1 a1@l p2
+a2@l a3@l z2@u s2 l2 z3@u p4 qa@l s4 l4 qz@u +eq0 +eq1 +eq2 +eq3 +keep
+o p8 s8 so a0@u l8 p16.8 +vq a2@u s16 lo l16 a1@u a3.v@u p32.8 qa@u s32 f16.6 l32 r.v t st sr lt f48 eb@u f80.8 lr mu.v b1@u
+b0.v@u eb@l m@u mr m@l ml@u ml@l b0@l Ptt' n0@u b1@l i3@u i3.v@l i2@u j3@u i2@l j3@l k3@u j2@u j2@l n0@l k2@u k3@l n1@u n1@l
+k2@l q0@u' x1@u' u0@u' q1@l' x3@u' Psg.v' Pmf' Pos.v' Pmm' Pq'
+----
+Tsw1@l Pdq Tso Tb@l Tb.v@u x0@l x2@u x1@l x0@u x3@l x2@l Tc0.v Tc1.v Th@l Th@u Tr1 Tr4 Tr2 Tn0 Tn1 Tn@w
+wa z0@l z1@l z2@l z3@l qz@l p1 a0@l z0@u s1 l1 z1@u p2 z2@u a1@l a2@l s2 l2 z3@u a3@l qa@l p4 o s4 l4 p8 qz@u s8 a0@u l8
+p16.8 so s16 lo a1@u a2@u l16 a3.v@u p32.8 qa@u s32 l32 f16 eb@u r.v t st sr lt f48 f80.8 lr eb@l b1@u mu.v b0.v@u m@u mr m@l b0@l
+ml@u b1@l ml@l i3@u n0@u i3.v@l j3@u i2@u j3@l Ptt' i2@l k3@u n1@u j2@l j2@u k3@l k2@u n0@l n1@l k2@l x3@u' x1@u' q0@u' u0@u' q1@l'
+x2@l' Psg.v' Pmf' Pos.v' Pmm' Pq' x0@u'
+----
+Tsw1@l Pdq Tso Tb@l Tb.v@u x2@u x1@l x0@l x3@l Tc0.v Tc1.v Th@l Th@u Tr1 Tr4 Tr2 Tn0 Tn1 Tn@w
+wa z0@l z1@l z2@l z3@l p1 qz@l z0@u s1 a0@l l1 p2 z1@u z2@u a1@l s2 a2@l a3@l l2 p4 o z3@u qa@l s4 l4 qz@u p8.8 s8 so l8 lo
+a0@u p16.8 s16 a1@u a2@u l16 a3.v@u p32.8 qa@u f16 t eb@u s32 eb@l l32 r.v st sr lt f48 f80.6 lr mu.6 mr b0.v@u m@u b0@l b1.v@u
+ml@u i2@u m@l ml@l i3@u n0@u b1@l i2@l i3.v@l j3@u j3@l j2@u j2@l n1@u k3@u k2@u k2@14-20 k3@14-20 mo n0@20-28 y0@0-12 n0@14-20
+n1@14-20 k3.v@20-28 y1@12-20 n1@20-28 k2.v@20-28 y2.v@20-28""".split("----")]
+ORDERS = [o.split() for o in """+pm +pf +pmu +off +sel0 +up +offm +mf +pf1 +ofb Ptt +kb +uq +ka +uq2 +k16 +uq2s Psg.v +ofb1 +inv +kc Pmf q0@u q1@l +nofb
+Pos.v +kd x2@u x1@u x3.v@u +keepb +sel2 u0.v@u +sel1 Pmm x0.v@u Pq Tsw1@l Pdq x3@l +raw Tb@l x0@l x1@l Tso Tb.v@u x2@l
+Tc1.v Tc0.v Th@l Th@u Tr4 Tr1 Tr2 Tn1 Tn0 +m16k Tn@w z0@l wa z1@l z3@l +w0 +num z2@l qz@l +keepm +w1.v z0@u +far p1.10
++own.v a1@l s1 l1 z1@u a0@l p2 z2@u a2@l a3@l s2 l2 z3@u +eq1 p4 qa@l s4 l4 qz@u +eq0 +eq3 +keep +eq2 +vq p8 s8 l8 p16.v o
+a0@u so a2@u s16 a1.v@u l16 a3.v@u p32.8 qa@u e1@u lo s32 f16.6 t e0@u l32 f48 r.v st sr lt lr e3@u e2@u f80.8 b0.v@u mu.v
+e0@l e1@l mr b1.v@u b0@l e3@l m@u m@l b1@l ml@u i3@u i2@u ml@l Ptt' i3.v@l e2@l n0@u i2.4@l j3@u j3@l k3@u j2@u j2@l n1@l
+n1@u x3.v@u' k2@u k2@l k3@l q0@u' n0@l
+----
+x2@u Psg.v q1@l x0.v@u Pmf u0.v@u Pos.v Pmm x1.v@u Pq x1.v@l Tsw1@l Tso x0@l Tb.v@u x2@l Tc0.v Pdq Tb@l Th@u x3@l Th@l
+Tc1.v Tr1 Tr4 Tr2 Tn1 Tn0 Tn@w z2@l z3@l z1@l wa z0@l qz@l z0@u p1 s1 l1 z2@u a0@l z1@u p2 s2 a2@l l2 a1@l p4 a3.v@l z3@u
+qa@l s4 qz@u o l4 p8.v s8 l8 p16.8 a0.v@u s16 a1@u a2@u so l16 a3.v@u p32.8 qa@u s32 lo f16 e0@u l32 e1@u t.6 r.v st sr lt
+e2@u e0@l e1@l f48 e3@u f80.8 e3@l lr mu.v b1@u b0.v@u m@u mr e2@l b0@l m@l ml@u b1@l ml@l n0@u i3.v@l i3@u j3@u i2@u i2@l
+j3@l j2@u k3@l n1@u Ptt' k3@u j2@l n1@l Pmf' n0@l k2@u k2@l
+----
+q0@u q1@l x3.v@u x1@u Psg.v x2@l u0.v@u Pmm x0@u Pos.v Tsw1@l Pq x2@u Tso Tb.v@u Tc1.v Pdq Tb@l Tc0.v Th@u x0@l Th@l Tr2
+Tr1 Tr4 Tn0 x1@l Tn1 Tn@w wa z0@l x3@l z1@l z2@l p1 z3@l qz@l z0@u s1 l1 p2 a0@l z2@u a2@l z1@u s2 a3@l a1.v@l l2 z3@u p4.4
+qa@l s4 o l4 qz@u p8.8 s8 l8 so p16.10 s16 a2.v@u l16 a3.v@u a0@u a1@u p32.8 qa@u f16 s32 e1@u e0@u e0@l e3@u lo e2@u e3@l
+t l32 r.v f48.v e1@l sr st e2@l f80.6 lt lr mu.10 b1.v@u m@u mr mo b0.v@u m@l ml@u b0.v@l ml@l i3.6@u i3.v@l i2@u n0@u i2@l
+b1@l j3@l j3@u j2@u j2@l k3@u k2@u n1@u k3@14-20 k2@14-20 y0@0-12 n1@14-20 n0@14-20 y1@12-20 n0@20-28 k2.v@20-28 k3.v@20-28
+n1@20-28 y2.v@20-28""".split("----")]
+ORDERS = [o.split() for o in """+pm +pf +up +off +ofb +nofb +offm +pf1 +sel0 +ka +sel1 +kb +sel2 +k16 +pmu +keepb +mf +uq +uq2s +uq2 +kc Ptt +inv q0@u
+Psg.v Pmf +raw +kd q1@l Pos.v +ofb1 u0@u Pmm x0@w Pq Tsw1@l Pdq Tso Tb@l Tb.v@u Th@l x1@w Th@u Tr4 x3@w Tr1 Tc1.v Tr2 x2@w
+Tc0.v Tn1 Tn0 Tn@w +m16k +far +w1.v +num z1@l z0@l z2@l wa.4 z3@l +keepm qz@l z0@u +w0 z1@u +eq3 a0.v@l p1 s1 a1@l l1 +eq1
+p2 z2@u a2@l s2 a3@l +own.v l2 p4 z3@u qa@l qz@u s4 o +eq0 +keep l4 +vq p8.4 +eq2 so s8 a0@u l8 p16.8 a2@u a1@u s16 l16
+a3.v@u p32.4 lo qa@u s32 f16.6 l32 t r.10 e0@u st e1@u f48 sr lt e2@u e3@u e3@l f80.8 lr e0@l b0.v@u mu.4 m@u mr e1@l m@l
+ml@u b1@u i3@u ml@l e2@l b0@l Ptt' b1@l i3.v@l j3@u i2@u j3@l i2@l n0@u n1@u j2@u j2@l n0@l n1@l k3@l k3@u k2@u k2@l
+----
+q0@u q1@l Psg.v x0@w Pmf u0@u Pos.v Pq Pmm Tsw1@l Tb@l Pdq Tb.v@u Tso Th@l x2@w x3@w Th@u x1@w Tr4 Tr1 Tc1.v Tr2 Tc0.v Tn1
+Tn0 Tn@w z0@l z3@l wa z1@l z2@l qz@l p1 z0@u z3@u s1 a0@l l1 z2@u p2 z1@u s2 qz@u l2 a1@l a2@l p4.v a3@l qa@l o s4 l4 a0@u
+p8.8 a2@u a1@u so s8 l8 a3.v@u p16.4 s16 lo l16 p32.4 f16 qa@u s32 l32 t e1@u r.v e2@u st f48.6 e0@u lt b1@u sr e0@l f80.6
+lr mu.4 e1@l b0.v@u mr.6 m@u b0@l m@l e3@u ml@u ml@l b1@l e3@l n0@u i3@u i3@l i2@l i2@u e2@l n1@u j3@u j3@l Ptt' j2@l k3@u
+j2@u n0@l n1@l k3@l k2@u k2@l
+----
+x1@w q0@u u0@u q1@l Pmf Psg.v Pos.v Pmm x0.v@w Pq Tsw1@l Tb.v@u Tb@l Tso Th@u Th@l Tc1.v Pdq Tr2 Tr1 Tr4 x3@w Tc0.v Tn1 Tn0
+Tn@w z3@l z1@l x2@w wa z2@l z0@l p1 qz@l z0@u z3@u s1 l1 z2@u z1@u a0@l p2 a1@l s2 a2@l l2 a3.v@l p4 o qz@u qa@l s4 l4 p8.6
+so s8 a0@u l8 p16.10 a2@u s16 lo l16 a1.v@u a3@u p32.10 qa@u e3@u s32 f16 e1@u t l32 e2@u e0@u r.6 st sr e3@l lt e1@l lr
+e0@l f48 e2@l f80.6 mr.8 mu.6 m@l m@u ml@l ml@u i3.v@l i2.v@u b1@u b0@u i3@u i2@l j3@l b1@l b0@l j3@u k3@20-28 k3@u j2@u
+j2@l n0@u k2@u n1@u mo k2@14-20 k3@14-20 y0@0-12 n1@14-20 n0@14-20 n0@20-28 y1@12-20 k2.v@20-28 n1@20-28 y2.v@20-28""".split("----")]
+ORDERS[0] = """+pm +sel0 +sel1 +sel2 +pf +pmu +up +pf1 +off +ofb +ka +kb +offm +ofb1 +nofb +k16 +keepb +mf +uq Ptt +uq2 +uq2s Psg.v Pmf q0@u Pos.v Pmm x0@u u0@u q1@l Pq +kc +kd +inv x1@u x2@u x3@u Tsw1@l Pdq Tso Tb@l Tb.v@u x0@l x1@l x2@l x3@l Tc0.v Tc1.v Th@l Th@u Tr1 Tr4 Tr2 Tn0 Tn1 Tn@w +num +m16k +keepm +raw wa +far +w0 z0@l z1@l z2@l z3@l p1 qz@l z0@u +w1.v +own.v z1@u s1 a0@l l1 a1@l p2 a2@l a3@l z2@u s2 l2 z3@u p4 qa@l s4 l4 qz@u +eq0 +eq1 +eq2 +eq3 +keep o p8 s8 so a0@u l8 p16.8 +vq a2@u s16 lo l16 a1@u a3.v@u p32.8 qa@u s32 f16.6 l32 r.v t st sr lt f48 eb@u f80.8 lr mu.v b1@u b0.v@u eb@l m@u mr m@l ml@u ml@l b0@l Ptt' n0@u b1@l i3@u i3.v@l i2@u j3@u i2@l j3@l k3@u j2@u j2@l n0@l k2@u k3@l n1@u n1@l k2@l""".split()
+ORDERS = [o.split() for o in """+sel0 +pm +pf +pmu +up +off +pf1 +ofb +kd +offm +sel1 +kc +kb +mf +uq +ka +ofb1 +uq2s Ptt +uq2 +far +w1.v x3@u Psg.v q0@u
++k16 +keepb x2.v@u u0@u Pos.v Pmf q1@l +nofb x2.v@l x0@u Pq Pmm +m16k x1.v@u Tsw1@l x3.v@l Pdq Tso x0@l +sel2 Tb.10@l Tb@u
+Tc0.v Th@l Th@u +raw Tr1 Tr4 Tr2 x1@l Tc1.v Tn0 Tn1 Tn@w +eq0 z2@l z0@l +keepm z3@l z1@l c2.6@u c1@u c0@u qz@l c3@u wa +w0
++eq2 d@u p1.6 qz@u o s1 +inv a2@l +num a1.v@l a0@l l1 a3.v@l p2.6 qa@l s2 l2 +eq3 a1@u p4.v a2@u so s4 a3@u a0@u +eq1 l4
++keep qa@u p8.6 s8 l8 eb@u +vq p16.8 s16 b2@u l16 p32.8 lo s32 f16 eb@l l32 f48.10 b0@u f80.8 b1.v@u f112.8 b3.v@u my.4
+b0@l mx.v b1@l m@l b2@l m@u ml@l ml@u b3@l g2@u n0@l g2@l n1@u g3@u n1@l n0@u g3@l h2@u h3@u x0@u' h2@l q0@u' h3@l
+----
+x3@u Ptt q1@l x2@u u0@u x1.v@l Psg.v Pmf Pos.v Pmm Pq x0@l x1@u Tsw1@l Pdq Tb.8@u Tb.6@l Tso Th@u Th@l Tc1.v Tr2 Tr1 Tr4
+x2@l Tc0.v Tn1 Tn0 x3@l Tn@w z3@l z0@l z2@l c2@u c3@u c0@u z1@l c1@u wa p1 qz@l a0@l a1@l d@u s1 qz@u o l1 p2.v a2@l s2 l2
+a3.v@l p4.8 a0.v@u a1@u s4 l4 a2@u a3@u qa@l p8.6 qa@u s8 l8 so eb@u p16.10 s16 l16 b1@u eb@l p32.6 f16.8 b2@u s32 lo l32
+f48.10 f80.8 f112.10 b0@u my mx.v m@u b0@l b1@l m@l b3@l b3@u ml@u b2.v@l g2@u ml@l n0@u n1@l g3@u g3@l n0@l n1@u g2@l h2@u
+h3@u h3@l x0@l' q0@u' h2@l
+----
+Ptt q1@l x1@u Psg.v x1@l Pos.v Pmf u0@u x3@l x0.v@u Pmm Tsw1@l Pq Tso Pdq Tb@l x2@u Tb.v@u Tc0.v Th@l Th@u x3@u Tc1.v Tr1
+Tr4 x2@l Tr2 Tn1 Tn0 Tn@w z0@l c3@u c1@u z2@l c0@u c2@u z3@l wa z1@l qz@l d@u p1 s1 a2.v@l l1 a3.v@l qz@u a0@l a1@l qa@l p2
+s2 l2 o p4.10 s4 a1@u so a2@u l4 p8.v a3@u s8 l8 p16.10 s16 a0@u lo l16 qa@u eb@u p32.4 f16.4 s32 l32 f48.8 eb@l b0.v@u
+f80.6 b2@u b1.v@u f112.10 mx.v b2.v@l b3@u my m@u b0@l b3@l m@l ml@u b1.v@l g2@u n0@u ml@l g3@u mo n1@u g3@14-20 g2@14-20
+h2@u h3@u g2@20-28 g3@20-28 n1@14-20 y0@0-12 h3@14-20 n0@14-20 h2@14-20 y1@12-20 h2@20-28 n1@20-28 n0@20-28 h3@20-28
+y2.v@20-28""".split("----")]
+POWERS, NUMBERS = [1, 2, 3, 5, 8, 13, 21, 34], [5, 13, 26, 47, 81, 115]
+ORDERS = [o.split() for o in """+sel0 +pm +pf +off +sel1 +ofb +pmu +pf1 +kc +ka +kb +offm +kd +up +mf +own.v +uq Ptt +uq2 +uq2s +k16 Psg.v q0@u +w1.v
++keepb x0@u q1@l +nofb +far +m16k +ofb1 Pos.v u0@u x3@u Pmf +sel2 Pq Pmm x2.v@l x1@l Tsw1@l x1.v@u Tb.10@l Tb@u Pdq Tso
+x3.v@l Tc0.v Th@l +keepm Th@u Tr4 Tr1 Tr2 Tc1.v x0@l Tn0 Tn1 Tn@w x2@u +eq2 +w0 z1@l +raw z0@l c0@u wa.8 c1@u +eq0 z3@l
+z2@l c3@u c2.6@u qz@l d@u +inv p1.6 +num qz@u s1 a1@l l1 a3.v@l a2@l p2 a0.v@l o.10 p3 s2 qa@l a1@u l2 s3 p5 so l3 a0@u p8
+a2.v@u +keep lo a3.v@u s5 l5 qa@u p13 s8 +eq1 l8 f5.6 +eq3 eb@u s13 p21.4 l13 eb@l f13.4 s21 +vq l21 p34 f26.v s34 b2@u r.v
+t.8 f47 l34 sr st lr f81 b3.v@u lt mr b1.v@u b0@u mu.v m@l m@u ml@l b0@l b2@l b1.v@l b3@l ml@u n0@l g2@u g3@u Ptt' n1@l
+g2@l n1@u h2@u h3@u g3@l n0@u h2@l q0@u' x2@u' x1@l' h3@l
+----
+Psg.v q1@l x1@u u0@u Pmf x3@l x0.v@u Pos.v Pq Pmm Pdq Tsw1@l Tso x2@l Tb.10@u Tb.6@l Tc1.v Th@u Th@l x3@u Tr2 Tr4 Tr1 Tc0.v
+x0@l Tn1 Tn0 Tn@w z3@l wa z0@l z2@l c0@u c1@u c2@u z1@l c3@u qz@l d@u p1 s1 l1 qz@u o p2 a1@l a0.v@l so s2 p3.8 l2 a2@l
+a3.v@l p5 a1@u s3 a2@u qa@l a3@u a0.v@u s5 l3 l5 p8 p13 f5.v qa@u s8 l8 p21 lo f13.v s13 eb@u l13 s21 p34 f26.v l21 eb@l
+r.v s34 b2@u f47.6 t l34 sr st lr f81 lt b1@u b0.v@u mr mu.v m@u b0@l m@l b1@l b3@l ml@u b2.v@l b3@u ml@l g2@u g3@u g3@l
+n0@u n1@l n0@l n1@u h2@u h3@u h3@l q0@u' g2@l h2@l
+----
+Ptt q1@l x1@l Pmf u0@u Psg.v Pos.v x0@l Pmm Pq x0.v@u Tsw1@l Pdq Tso Tb.v@u x3@l Tb@l x3@u Tc0.v Th@u x2@l Th@l Tc1.v Tr1
+Tr2 x1@u Tr4 Tn0 Tn1 x2@u Tn@w z0@l c2@u z1@l z3@l z2@l wa c0@u c1@u c3@u p1 qz@l d@u s1 l1 a2.v@l a3.v@l a0@l qz@u a1@l p2
+o qa@l s2 p3.6 l2 so s3 p5.8 l3 s5 a1@u p8.8 a3@u l5 a2.v@u s8 p13 f5.v a0@u l8 s13 p21.4 l13 qa@u f13.10 lo p34 s21 eb@u
+f26.4 l21 t s34 r.v b0.v@u f47 l34 eb@l st sr b2@u f81.10 lr lt b1.v@u mu.v b2.v@l b3@u m@u mr m@l b0@l ml@u b1@l ml@l b3@l
+n0@u g2@u n1@u g3@u g2@14-20 g3@20-28 g3@14-20 h2@u h3@u n1@14-20 mo g2@20-28 y0@0-12 n0@14-20 h2@14-20 h3@14-20 h3@20-28
+y1@12-20 h2@20-28 n1@20-28 n0@20-28 y2.v@20-28""".split("----")]
+ORDERS = [o.split() for o in """+sel0 +pm +sel1 +pf +kc +off +pf1 +up +pmu +kb +ka +offm +ofb +kd +k16 +mf +keepb +own.v Ptt +uq Psg.v +ofb1 +uq2s x3@u
++far +uq2 q0@u +w1.v q1@l Pos.v +nofb Pmf +sel2 x0@u u0@u Pq +m16k Pmm Tsw1@l x2@l Pdq x3.v@l x1@l Tb.10@l x1.v@u Tso Th@l
+Tb@u +w0 Tc0.v Th@u Tr1 Tr4 +raw Tr2 x2@u +keepm Tc1.v Tn0 Tn1 +eq2 Tn@w x0@l +eq0 z2@l z3@l z0@l z1@l c2.6@u c0@u wa.4
+c3@u c1@u +inv +num qz@l d@u p1.6 qz@u s1 l1 a3.v@l a0.v@l a1@l a2@l p2 o.10 s2 qa@l p3 a1@u l2 s3 p5 a0@u a3.v@u l3 a2.v@u
+p8 s5 so +keep l5 qa@u p13 s8 +eq1 l8 +eq3 f5.10 s13 p21.4 l13 eb@u f13.4 s21 +vq l21 p34 lo f26.v b2@u s34 r.v l34 t.8 sr
+f47 st f81.4 lr lt b1.v@u mu.v b3@u mr eb@l m@l m@u ml@l b0@u b0@l b1@l b2@l b3@l ml@u Ptt' g2@u g3@u n0@l n1@l g2@l n0@u
+n1@u h3@u g3@l h2@u h2@l q0@u' h3@l
+----
+q1@l Psg.v x1@u u0@u Pmf Pos.v Pmm x1@l Pq Pdq Tsw1@l x0@u x2.v@l Tso Tb.10@u Tb.6@l x2@u Th@u x0@l x3@u Th@l x3@l Tr2
+Tc1.v Tr4 Tr1 Tc0.v Tn1 Tn0 Tn@w c2@u z2@l z0@l wa c1@u c3@u z3@l c0@u z1@l qz@l p1 d@u s1 o l1 qz@u p2.6 a0.v@l s2 a1@l
+p3.4 a2@l l2 a3.v@l s3 qa@l p5 a2@u l3 s5 a1.v@u p8 a3@u l5 so a0.v@u s8 p13 f5.6 qa@u l8 s13 p21 eb@u f13.v l13 lo p34
+f26.v s21 eb@l b2@u l21 s34 f47.6 l34 r.v t sr st lr lt f81 b1@u mr b0.v@u mu.v b0@l m@u b3@u b1@l m@l ml@u b3@l ml@l
+b2.v@l g2@u n0@u n1@l g3@u n1@u n0@l h2@u g3@l g2@l h3@u x0@u' h3@l q0@u' h2@l
+----
+Ptt q1@l x3@l x2.v@u Pmf Psg.v u0@u Pos.v Pmm Pq Tsw1@l Pdq x3@u Tb.v@u Tso Tb@l Th@u x2@l Tc1.v x0@l Th@l Tr2 Tr1 x1@l
+x1@u Tr4 Tc0.v Tn1 Tn0 Tn@w wa c0@u c3@u z0@l z2@l z3@l c2@u z1@l c1@u p1 qz@l d@u s1 qz@u l1 a0@l a2.v@l a3.v@l a1@l p2
+qa@l s2 p3.6 l2 o.4 s3 p5.6 l3 so a1@u s5 p8.8 l5 a3@u a2.v@u p13 a0@u s8 f5.v l8 lo s13 p21.6 l13 qa@u f13.10 p34 eb@u
+eb@l s21 f26.6 l21 s34 r.v t l34 b0.v@u f47 st sr b2@u f81.10 lt lr b1.v@u mu.v b3@u b2.v@l mr m@u b0@l m@l ml@u b1@l ml@l
+b3@l g2@u g3@u g3@20-28 n0@u n1@u h2@u g2@14-20 g3@14-20 mo h3@u g2@20-28 n1@14-20 y0@0-12 h3@14-20 n0@14-20 h2@14-20
+h3@20-28 y1@12-20 n1@20-28 n0@20-28 h2@20-28 y2.v@20-28""".split("----")]
 
 
 def rank_program(g, core, T, topo):
@@ -147,6 +311,13 @@ def rank_program(g, core, T, topo):
         else:
             op("v", [out], reads, lambda: g.vector.tensor_scalar(ap(out), ap(x), ap(s1), ap(s2), o1, o2))
 
+    def axb(q, out, x, a, b):
+        if q == "v":
+            ts(out, x, a, OP.mult, b, OP.add)
+        else:
+            reads = [x] + [c for c in (a, b) if isinstance(c, tuple)]
+            op("a", [out], reads, lambda: g.scalar.activation(ap(out), ap(x), SAME, bias=ap(b), scale=ap(a)))
+
     def vcopy(out, x):
         op("v", [out], [x], lambda: g.vector.tensor_copy(ap(out), ap(x)))
 
@@ -156,13 +327,11 @@ def rank_program(g, core, T, topo):
     def pick_tt(out, win, off, y, o):
         op("v", [out], [win, off, y], lambda: g.vector.tensor_tensor(ap(out), ap(win).indirect(ap(off)), ap(y), o))
 
-    def held(out, x):
-        r = R("keep")
-        op("v", [out], [x, r], lambda: g.vector.tensor_tensor_scan(ap(out), ap(r), ap(x), 0.0, OP.add, OP.max))
+    def scan(out, d0, d1, o0, o1):
+        op("v", [out], [d0, d1], lambda: g.vector.tensor_tensor_scan(ap(out), ap(d0), ap(d1), 0.0, o0, o1))
 
-    def heldm(out, x):
-        r = R("keepm")
-        op("v", [out], [x, r], lambda: g.vector.tensor_tensor_scan(ap(out), ap(r), ap(x), 0.0, OP.mult, OP.max))
+    def held(out, x, keep):
+        scan(out, R(keep, 0, x[2] - x[1]), x, OP.mult if keep == "keepm" else OP.add, OP.max)
 
     def act(out, x, scale=1.0):
         op("a", [out], [x], lambda: g.scalar.activation(ap(out), ap(x), COPY, scale=scale))
@@ -176,7 +345,7 @@ def rank_program(g, core, T, topo):
         elif q == "v":
             op("v", [out], [win, off], lambda: g.vector.tensor_copy(ap(out), ap(win).indirect(ap(off))))
         else:
-            k = 8 if q == "h" else 6
+            k = int(q)
             cut = out[1] + 16 * k * out[3]
             pick("v", R(out[0], out[1], cut, out[3]), win, R(off[0], off[1], off[1] + k))
             pick("a", R(out[0], cut, out[2], out[3]), win, R(off[0], off[1] + k, off[2]))
@@ -200,11 +369,14 @@ def rank_program(g, core, T, topo):
     def lanes(src, dst, k):
         return topo.engines(src, dst)[:8]
 
-    def send(dst, land, src, k, s, codes):
+    def send(s, land, src, k, codes=False):
+        dst = T.cores[rank ^ s]
+        cnt["arr%s%d" % (k, s)] = len(lanes(dst, core, k))
+        note("g", [], [land], ("arr%s%d" % (k, s), len(lanes(dst, core, k))))
         e = lanes(core, dst, k)
         rid, pid, _ = topo.addr(dst)
         hazards("g", [src], [])
-        o, i = T[land][:, 0:src[2] - src[1]], ap(src)
+        o, i = ap(land), ap(src)
         if codes:
             o, i = o.bitcast(dt.uint8), i.bitcast(dt.uint8)
         g.remote_dma(out_ap=o, in_ap=i, remote_sem=T.sem["arr%s%d" % (k, s)], local_sem=T.sem["snt%s%d" % (k, s)],
@@ -213,15 +385,10 @@ def rank_program(g, core, T, topo):
         cnt[sem] = len(e)
         note("g", [src], [], (sem, len(e)))
 
-    def arrives(land, k, s, src):
-        sem = "arr%s%d" % (k, s)
-        cnt[sem] = len(lanes(src, core, k))
-        note("g", [], [R(land)], (sem, cnt[sem]))
-
     dma("a", [R("mli")], [], T.mli[:, :], T.ml[:, :])
     dma("s", [R("ut")], [], T.ut[:, :], T.u[:, :])
-    dma("s", [R("x0", 0, 4 * H)], [], T.x0[:, 0:4 * H], T.x[:, 0:4 * H])
-    dma("s", [R("x0", 4 * H, 4 * C)], [], T.x0[:, 4 * H:4 * C], T.x[:, 4 * H:4 * C])
+    for a, b in LOADS:
+        dma("s", [R("x0", 64 * a, 64 * b)], [], T.x0[:, 64 * a:64 * b], T.x[:, 64 * a:64 * b])
     dma("s", [R("wq")], [R("x0")], T.wq[:, :].bitcast(dt.uint8), T.wc[:, :])
     dma("s", [R("wqs")], [], T.wqs[:, :], T.ws[:, :])
     dma("s", [R("vt")], [], T.vt[:, :], T.v[:, :])
@@ -240,272 +407,246 @@ def rank_program(g, core, T, topo):
     e, one = R("et"), R("ones")
     iota(one, [[0, 516]], 1, 0)
     op("g", [e], [one], lambda: g.affine_select(ap(e), ap(one), [[-1, 516]], OP.is_equal, 0.0, 3, 4))
-    ts(R("pm"), R("pi"), 15, OP.bitwise_and)
-    fill(R("sel", 0, 140, 5), -FAR)
-    fill(R("rr"), -FAR)
-    vcopy(R("pf"), R("pm", 0, 1))
-    vcopy(R("pmu"), R("pm"))
-    vcopy(R("up"), R("ui"))
-    pf, pf1, off, offq, offh, inv = R("pf"), R("pf1"), R("off"), R("offq"), R("offh"), R("inv")
-    ts(pf1, pf, 1.0, OP.add)
-    ts(off, pf, 15.0, OP.is_lt, LIFT, OP.mult)
-    ts(R("ka"), R("fi"), pf, OP.is_equal, -2 * LIFT, OP.mult)
-    ts(R("kb"), R("fi"), pf1, OP.is_equal, LIFT, OP.mult)
-    ts(offh, off, float(H), OP.add)
-    ts(offq, off, 0.5, OP.add)
-    tt(R("k16"), R("ka"), R("kb"), OP.add)
-    pick("a", R("keep"), R("k16"), R("pmu"))
 
-    def prep(m, part):
-        if part == 0:
-            ts(R("tt"), m, offh, OP.is_ge, float(H), OP.mult)
-        elif part == 1:
-            ts(R("sg"), R("tt"), -2.0, OP.mult, float(H), OP.add)
-            tt(R("mmf"), m, R("tt"), OP.subtract)
-        elif part == 2:
-            ts(R("os0"), R("sg"), 1.0, OP.add, off, OP.mult)
-            ts(R("mm"), R("mmf"), off, OP.subtract)
-        elif part == 3:
-            (n, a, b, st), mid = m, m[1] + 14 * m[3]
-            tt(R("mf2"), (n, a, mid, st), R("os0", 0, 14), OP.subtract)
-            for half in (0, 1):
-                tt(step5(half, 3), (n, mid, b, st), R("os0", 14, 28), OP.subtract)
-        else:
-            for half in (0, 1):
-                tt(step5(half, 1), R("mf2"), step5(half, 3), OP.subtract)
-
-    def step5(half, k):
-        return R("sel", 70 * half + k, 70 * half + 70, 5)
-
-    def plane(x, half, b):
-        act(R("xp%d" % b, half * H, half * H + H), R(x, half * 4 * H + b, half * 4 * H + 4 * H, 4))
-
-    def halfcols(x, half):
-        return R(x, half * 4 * H, half * 4 * H + 4 * H)
-
-    held_m = R("mf")
-    ts(held_m, R("mli"), off, OP.add)
-    quant("uq", R("ut"))
-    prep(held_m, 0)
+    pf, pf1, off, offm, ofb, ofb1, nofb, inv = [R(n) for n in ("pf", "pf1", "off", "offm", "ofb", "ofb1", "nofb", "inv")]
     upk, uqc, uq2 = R("up"), R("uq"), R("uq2")
-    op("v", [uq2], [uqc, upk],
-       lambda: g.vector.tensor_copy(ap(uq2).bitcast(dt.uint32), ap(uqc).bitcast(dt.uint32).indirect(ap(upk))))
-    pick("a", R("uq2s"), R("uqs"), upk)
-    prep(held_m, 1)
-    quant("qx", halfcols("x0", 0), 0, H)
-    mm(0, "uq2", 0, "qx", 0, H)
-    prep(held_m, 2)
-    plane("x0", 0, 0)
-    act(R("sup"), R("p0", 0, H))
-    quant("qx", halfcols("x0", 1), H, C)
-    mm(1, "uq2", 0, "qx", H, C)
-    prep(held_m, 3)
-    ts(R("kc"), R("fi"), pf, OP.not_equal)
-    ts(R("kd"), R("fi"), pf1, OP.is_equal, MANY - 1, OP.mult)
-    ts(inv, pf, 15.0, OP.is_equal, 1 / MANY, OP.max)
-    for b in range(1, 4):
-        plane("x0", 0, b)
+    small = {
+        "pm": lambda: ts(R("pm"), R("pi"), 15, OP.bitwise_and),
+        "sel0": lambda: fill(R("sel"), 1.0),
+        "sel1": lambda: fill(R("sel", 0, 140, 5), 0.0),
+        "sel2": lambda: fill(R("sel", 2, 140, 5), -1.0),
+        "pf": lambda: vcopy(pf, R("pm", 0, 1)),
+        "pmu": lambda: vcopy(R("pmu"), R("pm")),
+        "up": lambda: vcopy(upk, R("ui")),
+        "pf1": lambda: ts(pf1, pf, 1.0, OP.add),
+        "off": lambda: ts(off, pf, 15.0, OP.is_lt, LIFT, OP.mult),
+        "ofb": lambda: ts(ofb, pf, 15.0, OP.is_lt, BIT, OP.mult),
+        "ka": lambda: ts(R("ka"), R("fi"), pf, OP.is_equal, -2 * BIT, OP.mult),
+        "kb": lambda: ts(R("kb"), R("fi"), pf1, OP.is_equal, BIT, OP.mult),
+        "offm": lambda: ts(offm, off, float(H), OP.subtract),
+        "ofb1": lambda: ts(ofb1, ofb, 1.0, OP.add),
+        "nofb": lambda: ts(nofb, ofb, -1.0, OP.mult),
+        "k16": lambda: tt(R("k16"), R("ka"), R("kb"), OP.add),
+        "keepb": lambda: pick("a", R("keepb", 0, H), R("k16"), R("pmu")),
+        "keep": lambda: act(R("keep", 0, H), R("keepb", 0, H), LIFT / BIT),
+        "keep2": lambda: vcopy(R("keep", H, C), R("keep", 0, H)),
+        "keepb2": lambda: vcopy(R("keepb", H, C), R("keepb", 0, H)),
+        "keepm2": lambda: vcopy(R("keepm", H, C), R("keepm", 0, H)),
+        "mf": lambda: ts(R("mf"), R("mli"), offm, OP.add),
+        "uq": lambda: quant("uq", R("ut")),
+        "uq2": lambda: op("v", [uq2], [uqc, upk], lambda: g.vector.tensor_copy(
+            ap(uq2).bitcast(dt.uint32), ap(uqc).bitcast(dt.uint32).indirect(ap(upk)))),
+        "uq2s": lambda: pick("a", R("uq2s"), R("uqs"), upk),
+        "kc": lambda: ts(R("kc"), R("fi"), pf, OP.not_equal),
+        "kd": lambda: ts(R("kd"), R("fi"), pf1, OP.is_equal, MANY - 1, OP.mult),
+        "inv": lambda: ts(inv, pf, 15.0, OP.is_equal, 1 / MANY, OP.max),
+        "m16k": lambda: tt(R("m16k"), R("kc"), R("kd"), OP.add),
+        "keepm": lambda: pick("a", R("keepm", 0, H), R("m16k"), R("pmu")),
+        "vq": lambda: quant("vq", R("vt")),
+    }
+    top = len(POWERS) - 1
 
     def once(name, q):
-        if name in ("w0", "w1"):
+        if name in small:
+            small[name]()
+        elif name in ("w0", "w1"):
             for a, b, c, st in RUNS:
                 copy(q, R(name, BASE + c, BASE + c + st * (b - a), st), R("cc", a, b))
         elif name in ("raw", "own"):
-            copy(q, R("raw" if name == "raw" else "w%d" % ((len(POWERS) - 1) % 2), 0, H), R("cc", 0, H))
+            copy(q, R("raw" if name == "raw" else "w%d" % (top % 2), 0, H), R("cc", 0, H))
         elif name == "far":
             copy(q, R("wa", H, C), R("cc", H, C))
-        elif name == "keepm":
-            tt(R("m16k"), R("kc"), R("kd"), OP.add)
-            pick("a", R("keepm"), R("m16k"), R("pmu"))
         elif name == "num":
             for a, b, c, st in RUNS:
                 for w in ("f0", "f1"):
-                    iota(R(w, c, c + st * (b - a), st), [[1, b - a]], a, 0)
-            iota(R("f0", PORT, PORT + H), [[1, H]], 0, 0)
-        elif name == "vq":
-            quant("vq", R("vt"))
+                    iota(R(w, BASE + c, BASE + c + st * (b - a), st), [[1, b - a]], a - H, 0)
+            iota(R("f0", H, C), [[1, H]], 0, 0)
+        elif name == "nup":
+            iota(R("f%d" % (len(NUMBERS) % 2), 0, H), [[1, H]], -H, 0)
         else:
             b = int(name[2])
             quant("eq", R("et", 3 - b, 515 - b), 128 * b, 128 * b + 128)
 
-    late = ["xl0", "xl1", "xl2", "xl3"]
-    for s in ROUNDS:
-        last = s == ROUNDS[-1]
+    first, lower, banks = {}, {}, {}
+
+    def step(s, name, q, b0, b1):
         xs, xn = "x%d" % (s - 1), "x%d" % s
-        peer = T.cores[rank ^ s]
         land_b, land_q = "lb%d" % s, "lq%d" % s
-        arrives(land_b, "b", s, peer)
-        arrives(land_q, "q", s, peer)
-        arrives(land_q + "s", "s", s, peer)
+        c0, c1, low = 16 * b0, 16 * b1, int(b0 >= 14)
+        kind, k = name[0], int(name[-1]) if name[-1].isdigit() else 0
+        m = R("mf") if s == 1 else R("sm", 15, C, 16)
 
-        sw, mine = R("sw"), R("sc", C + 15, 672, 16)
-        tt(sw, R("sup"), R("p1", 0, H), OP.is_gt)
-        prep(held_m, 4)
-        held(R("sc", C, 672), sw)
-        pick("a", R("bl"), sw, R("mm", 14, 28))
-        pick("v", R("bu"), sw, R("mm", 0, 14))
-        for name in late:
-            plane(xs, name[1] == "l", int(name[2]))
-        ts(step5(0, 2), mine, offq, OP.subtract, -4 * MANY, OP.mult)
-        ts(step5(0, 4), mine, offq, OP.subtract, 2 * MANY, OP.mult)
-        held(R("sc", H, C), R("bl"))
-        held(R("sc", 0, H), R("bu"))
-        ts(step5(1, 2), mine, offq, OP.subtract, 4 * MANY, OP.mult)
-        tt(R("rr", 2, 70, 5), R("sc", H + 15, C, 16), R("sg", 14, 28), OP.mult)
-        tt(R("rr", 0, 70, 5), R("sc", 15, H, 16), R("sg", 0, 14), OP.mult)
-        ts(step5(1, 4), mine, offq, OP.subtract, -2 * MANY, OP.mult)
-        for half in (0, 1):
-            o, d0, d1 = R("nn", 70 * half, 70 * half + 70), R("sel", 70 * half, 70 * half + 70), R("rr")
-            op("v", [o], [d0, d1], lambda: g.vector.tensor_tensor_scan(ap(o), ap(d0), ap(d1), 0.0, OP.add, OP.max))
-        ts(R("n16"), R("nn", 4, 140, 5), MANY, OP.subtract)
-        held_m = R("sm", 15, C, 16)
-        send(peer, land_b, R("n16"), "b", s, False)
-        n_up, n_lo = R("n16", 0, 14), R("n16", 14, 28)
-        b_up, b_lo = R(land_b, 0, 14), R(land_b, 14, 28)
+        def cols(x, b=None):
+            return R(x, 4 * c0, 4 * c1) if b is None else R(x, 4 * c0 + b, 4 * c1, 4)
 
-        def cols(x, half, b):
-            return R(x, half * 4 * H + b, half * 4 * H + 4 * H, 4)
+        def bank(b):
+            n, a = banks[b, low]
+            return R("p%d" % n, c0 - a, c1 - a)
 
-        def row(k):
-            return R("w%d" % (k % 2), H, C)
+        def product(b, l, r):
+            n = (b + (2 if low or c1 - c0 == C and l == "eq" else 6)) % 8
+            for half in range(low, 1 + (c1 > H)):
+                banks[b, half] = n, c0
+            mm(n, l, 128 * b, r, c0, c1)
 
-        def codes(k):
-            return R("w%d" % (k % 2), BASE)
+        def scores():
+            return R("p%d" % k, c0 - first[k], c1 - first[k])
 
-        def lst(k):
-            return R("ls", 14 * k, 14 * k + 14)
+        def row(j):
+            return R("w%d" % (j % 2), H + c0, H + c1) if j <= top else R("tr", (j - top - 1) * H + c0, (j - top - 1) * H + c1)
 
-        mrow, top = {}, len(POWERS) - 1
+        def codes(j):
+            return R("w%d" % (j % 2), BASE)
 
-        def step(name, q):
-            kind, k = name[:2], int(name[-1]) if name[-1].isdigit() else 0
-            if name == "wa":
-                pick("a", R("wa", 0, H), R("raw"), n_lo)
-            elif kind in ("zu", "zl"):
-                if kind == "zl":
-                    pick_tt(R(kind, k, 4 * H, 4), R("xp%d" % k), n_lo, cols(xs, 1, k), OP.add)
-                else:
-                    pick_tt(R(kind, 4 * DZ + k, 4 * H, 4), R("xp%d" % k), R("n16", DZ // 16, 14), R(xs, 4 * DZ + k, 4 * H, 4), OP.add)
-            elif kind == "gu":
-                pick(q, R("zu", k, 4 * DZ, 4), R("xp%d" % k), R("n16", 0, DZ // 16))
-            elif name == "dz":
-                o, i = R("zu", 0, 4 * DZ), R(xs, 0, 4 * DZ)
-                dma("g", [o], [o, i], ap(o), ap(i), accum_op=OP.add)
-            elif name in ("qzl", "qzu"):
-                quant(name, R(name[1:]))
-                for b in range(4):
-                    mm((b + (2 if name == "qzl" else 6)) % 8, "wq", 128 * b, name, 0, H)
-            elif kind in ("al", "au"):
-                o, p = R(kind, k, 4 * H, 4), R("p%d" % ((k + (2 if kind == "al" else 6)) % 8), 0, H)
-                if q == "v":
-                    ts(o, p, 0.015625, OP.mult)
-                else:
-                    act(o, p, 0.015625)
-            elif name == "qal":
-                quant("qal", R("al"))
-                send(peer, land_q, R("qal"), "q", s, True)
-                send(peer, land_q + "s", R("qals"), "s", s, False)
-            elif name == "qau":
-                quant("qau", R("au"))
-            elif kind in ("el", "eu"):
-                mm((k + (2 if kind == "el" else 6)) % 8, "eq", 128 * k, land_q if kind == "el" else "qau", 0, H)
-            elif name in ("ebl", "ebu"):
-                for b in range(4):
-                    mm((b + (2 if name == "ebl" else 6)) % 8, "eq", 128 * b, land_q if name == "ebl" else "qau", 0, H)
-            elif kind in ("bl", "bu"):
-                half = kind == "bl"
-                copy(q, R("bp%d" % k, half * H, half * H + H), R("p%d" % ((k + (2 if half else 6)) % 8), 0, H))
-            elif kind == "pr":
-                for part in ([] if last else [0] if k == 0 else [1, 2, 3]):
-                    prep(R("sm", 15, C, 16), part)
-            elif name in ("p1", "o"):
-                pick(q, row(0) if name == "p1" else R("tr", C, C + H), R("wa"), b_up if name == "p1" else b_lo)
-            elif name[0] == "p":
-                k = POWERS.index(int(name[1:]))
-                pick(q, row(k), codes(k - 1), lst(POWERS.index(POWERS[k] - POWERS[k - 1])))
-            elif name in ("su", "sl"):
-                half = name == "sl"
-                held(R("sm", half * H, half * H + H), mrow[half])
-            elif name in ("lu", "ll"):
-                half = name == "ll"
-                ts(R("m16", 14 * half, 14 * half + 14), R("sm", half * H + 15, half * H + H, 16), off, OP.subtract)
-            elif name == "lm":
-                ts(R("m16"), R("sm", 15, C, 16), off, OP.subtract)
-            elif name == "lw":
-                ts(R("ls", 14 * top + 14, 14 * top + 42), R("sa", (top + 1) * H + 15, (top + 3) * H, 16), inv, OP.mult)
-            elif name[0] in "sl":
-                k = top + 1 + "tro".index(name[1]) if name[1] in "tro" else POWERS.index(int(name[1:]))
-                if name[0] == "s":
-                    heldm(R("sa", k * H, k * H + H), row(k) if k <= top else R("tr", (k - top - 1) * H, (k - top) * H))
-                else:
-                    ts(lst(k), R("sa", k * H + 15, k * H + H, 16), inv, OP.mult)
-            elif name == "t":
-                pick(q, R("tr", 0, H), R("w%d" % (top % 2), 0, C), n_up)
-            elif name == "r":
-                pick(q, R("tr", H, C), codes(top), lst(top + 3))
-            elif name[0] == "f":
-                k = NUMBERS.index(int(name[1:]))
-                pick(q, R("f%d" % ((k + 1) % 2), PORT, PORT + H), R("f%d" % (k % 2)),
-                     lst(POWERS.index(NUMBERS[k] - ([0] + NUMBERS)[k])))
-            elif name in ("mu", "ml", "mr"):
-                half = name != "mu"
-                k = len(NUMBERS) if name == "ml" else [n + POWERS[-1] >= H // 2 for n in NUMBERS].index(True) + 1
-                win, at = R("f%d" % (k % 2)), lst(top + {"mu": 1, "ml": 3, "mr": 2}[name])
-                mrow[half] = R("mu" if q == "v" else "mrow", half * H, half * H + H)
-                pick(q, mrow[half], win, at)
-                if last and q == "v":
-                    pick("a", R("mrow", half * H, half * H + H), win, at)
-                if last and half:
-                    dma("s", [], [R("mrow")], T.mo[:, :], T.mrow[0:128:16, :])
-            elif kind in ("nu", "nm", "nl"):
-                c0, c1 = {"nu": (0, H), "nm": (H, LAST), "nl": (LAST if last else H, C)}[kind]
-                if last or kind != "nm":
-                    pick_tt(R(xn, 4 * c0 + k, 4 * c1, 4), R("bp%d" % k), R("m16", c0 // 16, c1 // 16),
-                            R(xs, 4 * c0 + k, 4 * c1, 4), OP.add)
-            elif kind in ("iu", "il"):
-                half = kind == "il"
-                pick(q, R("ya", k * C + half * H, k * C + half * H + H), R("xp%d" % k), R("m16", 14 * half, 14 * half + 14))
-            elif kind == "ia":
-                pick(q, R("ya", k * C, k * C + C), R("xp%d" % k), R("m16"))
-            elif kind == "ka":
-                pick(q, R(xn, k, 4 * C, 4), R("yb%d" % k), R("m16"))
-            elif kind in ("ju", "jl"):
-                half = kind == "jl"
-                tt(R("yb%d" % k, half * H, half * H + H), R("ya", k * C + half * H, k * C + half * H + H),
-                   R("p%d" % ((k + (2 if half else 6)) % 8), 0, H), OP.add)
-            elif kind in ("ku", "km", "kl"):
-                c0, c1 = {"ku": (0, H), "km": (H, LAST), "kl": (LAST if last else H, C)}[kind]
-                if last or kind != "km":
-                    pick(q, R(xn, 4 * c0 + k, 4 * c1, 4), R("yb%d" % k), R("m16", c0 // 16, c1 // 16))
-            elif kind in ("xu", "xl"):
-                if not last:
-                    plane(xn, kind == "xl", k)
-            elif name == "up":
-                if not last:
-                    act(R("sup"), R("p0", 0, H))
-            elif not last:
-                if name != "qm":
-                    half = name == "ql"
-                    quant("qx", halfcols(xn, half), half * H, half * H + H)
-                    mm(int(half), "uq2", 0, "qx", half * H, half * H + H)
+        def lst(j):
+            return R("ls", 14 * j + b0, 14 * j + b1)
+
+        def slot(n, half, j):
+            return R(n, 70 * half + j, 70 * half + 70, 5)
+
+        if kind == "P":
+            if name == "Ptt":
+                ts(R("tt"), m, off, OP.is_ge, float(H), OP.mult)
+            elif name == "Psg":
+                axb(q, R("sg"), R("tt"), -2.0, float(H))
+            elif name == "Pmf":
+                tt(R("mmf"), m, R("tt"), OP.subtract)
+            elif name == "Pmm":
+                ts(R("mm"), R("mmf"), offm, OP.subtract)
+            elif name == "Pos":
+                axb(q, R("os0"), R("sg"), ofb, offm)
+            elif name == "Pq":
+                tt(R("rr", 3, 140, 5), m, R("os0"), OP.subtract)
             else:
-                k = ("qu", "qm", "ql").index(name)
-                c0, c1 = (0, LAST - 128, LAST, C)[k:k + 2]
-                quant("qx", R(xn, 4 * c0, 4 * c1), c0, c1)
-                mm(k, "vq", 0, "qx", c0, c1)
-                for j in range(4 * (k == 2)):
-                    dma("sa"[j % 2], [], [R("qxs")], T.osc[4 * j:4 * j + 4, :], T.qxs[32 * j:32 * j + 4, :])
-                dma("s", [], [R("qx", c0, c1)], T.oc[:, 4 * c0:4 * c1], T.qx[:, c0:c1].bitcast(dt.uint8))
-                copy("aav"[k], R("yo", c0, c1), R("p%d" % k, 0, c1 - c0))
-                dma("a", [], [R("yo", c0, c1)], T.y[:, c0:c1], T.yo[:, c0:c1])
-
-        order = ORDER1 if s == 1 else ORDER3 if last else ORDER
-        late = order[order.index("|") + 1:]
-        for name in order[:order.index("|")]:
-            if name[0] != "+":
-                step(*(name + ":a").split(":")[:2])
+                tt(slot("rr", 1, 0), slot("rr", 1, 3), slot("rr", 0, 3), OP.subtract)
+        elif kind == "T":
+            sw, mine = R("sw"), R("sc", C + 15, 672, 16)
+            if name[:3] == "Tsw":
+                tt(R("sw", c0 - H, c1 - H), R("sup", c0 - H, c1 - H), scores(), OP.is_gt)
+            elif name == "Tso":
+                held(R("sc", C + c0, C + c1), R("sw", c0, c1), "keepb")
+            elif name == "Tb":
+                pick(q, R("bb", c0, c1), sw, R("mm", b0, b1))
+            elif name == "Th":
+                held(R("sc", c0, c1), R("bb", c0, c1), "keepb")
+            elif name == "Tc0":
+                axb(q, slot("sel", 0, 3), mine, -1.0, ofb1)
+            elif name == "Tc1":
+                axb(q, slot("sel", 1, 3), mine, 1.0, nofb)
+            elif name[1] == "r":
+                a = 0 if k == 2 else 14
+                tt(slot("rr", 1, k), R("sc", 16 * a + 15, 16 * a + H, 16), R("sg", a, a + 14), OP.mult)
+            elif name != "Tn":
+                scan(R("nn", 70 * k, 70 * k + 70), R("sel", 70 * k, 70 * k + 70), R("rr", 70, 140), OP.mult, OP.add)
             else:
-                once(*(name[1:] + ":a").split(":")[:2])
+                vcopy(R("n16", b0, b1), R("nn", 4 + 5 * b0, 5 * b1, 5))
+                lower[s] = R("lc%d" % s) if low else R(land_b, 14, 28)
+                send(s, R(lower[s][0], 0, b1 - b0), R("n16", b0, b1), "bc"[low])
+        elif name == "wa":
+            pick(q, R("wa", c0, c1), R("raw"), R("n16", 14 + b0, 14 + b1))
+        elif kind == "z":
+            pick_tt(cols("zz", k), R("xp%d" % k), R("n16", b0, b1), cols(xs, k), OP.add)
+        elif kind == "c":
+            pick(q, cols("zz", k), R("xp%d" % k), R("n16", b0, b1))
+        elif name == "d":
+            tt(cols("zz"), cols("zz"), cols(xs), OP.add)
+        elif kind == "g":
+            pick(q, cols("ya", k), R("bp%d" % k), R("m16", b0, b1))
+        elif kind == "h":
+            tt(cols(xn, k), cols("ya", k), cols(xs, k), OP.add)
+        elif name == "dz":
+            o, i = cols("zz"), cols(xs)
+            dma("g", [o], [o, i], ap(o), ap(i), accum_op=OP.add)
+        elif name == "qz":
+            quant("qz", cols("zz"), c0, c1)
+            for b in range(4):
+                product(b, "wq", "qz")
+        elif name == "qa":
+            quant("qa" if low else land_q, cols("aa"), c0, c1)
+            if low:
+                send(s, R(land_q, c0, c1), R("qa", c0, c1), "q", True)
+                send(s, R(land_q + "s", c0, c1), R("qas", c0, c1), "s")
+        elif kind == "a":
+            if q == "v":
+                ts(cols("aa", k), bank(k), 0.015625, OP.mult)
+            else:
+                act(cols("aa", k), bank(k), 0.015625)
+        elif kind == "e":
+            for b in (range(4) if name == "eb" else [k]):
+                product(b, "eq", land_q)
+        elif kind == "b":
+            copy(q, R("bp%d" % k, c0, c1), bank(k))
+        elif name == "p1":
+            pick(q, row(0), R("wa"), R(land_b, b0, b1))
+        elif name == "o":
+            pick(q, row(top + 3), R("wa"), R(lower[s][0], lower[s][1] + b0, lower[s][1] + b1))
+        elif kind == "p":
+            j = POWERS.index(int(name[1:]))
+            pick(q, row(j), codes(j - 1), lst(POWERS.index(POWERS[j] - POWERS[j - 1])))
+        elif kind in "sl":
+            j = top + 1 + "tro".index(name[1]) if name[1] in "tro" else POWERS.index(int(name[1:]))
+            if kind == "s":
+                held(R("sa", j * H + c0, j * H + c1), row(j), "keepm")
+            else:
+                ts(lst(j), R("sa", j * H + c0 + 15, j * H + c1, 16), inv, OP.mult)
+        elif name == "t":
+            pick(q, row(top + 1), R("w%d" % (top % 2), 0, C), R("n16", b0, b1))
+        elif name == "r":
+            pick(q, row(top + 2), codes(top), lst(top + 3))
+        elif kind == "f":
+            j = NUMBERS.index(int(name[1:]))
+            pick(q, R("f%d" % ((j + 1) % 2), H + c0, H + c1), R("f%d" % (j % 2), BASE),
+                 lst(POWERS.index(NUMBERS[j] - ([0] + NUMBERS)[j])))
+        elif name in ("mu", "mr", "mx", "my"):
+            half = name in ("mr", "my")
+            f = "f%d" % (([n + POWERS[-1] * (name in ("mu", "mr")) >= H // 2 for n in NUMBERS].index(True) + 1) % 2)
+            win, at = {"mu": (R(f, BASE), lst(top + 1)), "mr": (R(f, BASE), lst(top + 2)),
+                       "mx": (R(f, 0, C), R("n16", b0, b1)), "my": (R(f, BASE), lst(top + 3))}[name]
+            pick(q, R("mu", half * H + c0, half * H + c1), win, at)
+        elif name == "mo":
+            op("a", [R("mrow")], [R("mu")], lambda: g.scalar.activation(T.mrow[:, :], T.mu[:, :], COPY, bias=float(H)))
+            dma("s", [], [R("mrow")], T.mo[:, :], T.mrow[0:128:16, :])
+        elif name == "m":
+            held(R("sm", c0, c1), R("mu", c0, c1), "keep")
+        elif name == "ml":
+            ts(R("m16", b0, b1), R("sm", c0 + 15, c1, 16), offm, OP.subtract)
+        elif kind == "n":
+            pick_tt(cols(xn, k), R("bp%d" % k), R("m16", b0, b1), cols(xs, k), OP.add)
+        elif kind == "i":
+            pick(q, cols("ya", k), R("xp%d" % k), R("m16", b0, b1))
+        elif kind == "j":
+            tt(R("yb%d" % k, c0, c1), cols("ya", k), bank(k), OP.add)
+        elif kind == "k":
+            pick(q, cols(xn, k), R("yb%d" % k), R("m16", b0, b1))
+        elif kind == "x":
+            copy(q, R("xp%d" % k, c0, c1), cols(xs, k))
+        elif kind == "u":
+            copy(q, R("sup", c0, c1), scores())
+        elif kind == "q":
+            first[k] = c0
+            quant("qx", cols(xs), c0, c1)
+            mm(k, "uq2", 0, "qx", c0, c1)
+        else:
+            quant("qx", cols(xn), c0, c1)
+            mm(k, "vq", 0, "qx", c0, c1)
+            for j in range(4 * (c1 == C)):
+                dma("sa"[j % 2], [], [R("qxs")], T.osc[4 * j:4 * j + 4, :], T.qxs[32 * j:32 * j + 4, :])
+            dma("s", [], [R("qx", c0, c1)], T.oc[:, 4 * c0:4 * c1], T.qx[:, c0:c1].bitcast(dt.uint8))
+            copy(q, R("yo", c0, c1), R("p%d" % k, 0, c1 - c0))
+            dma("a", [], [R("yo", c0, c1)], T.y[:, c0:c1], T.yo[:, c0:c1])
+
+    for s, order in zip(ROUNDS, ORDERS):
+        for word in order:
+            ahead = word.endswith("'")
+            head, _, span = word.rstrip("'").partition("@")
+            name, _, q = head.partition(".")
+            if name[0] == "+":
+                once(name[1:], q or "a")
+            else:
+                step(s + ahead, name, q or "a", *(SPANS[span] if span in SPANS else [int(n) for n in span.split("-")]))
 
     for sem in sorted(cnt, key=lambda k: nd[0] + int(k[1:]) if k[1:].isdigit() else 0):
         need("g", sem, cnt[sem])
+
+
+LOADS = [(0, 14), (14, 28)]

@@ -6,13 +6,13 @@ COPY, SAME = ActivationFunctionType.Copy, ActivationFunctionType.Identity
 C, H = 448, 224
 ROUNDS = [1, 2, 3]
 F16, BF, F32, I32, U16, U8, MX = "float16", "bfloat16", "float32", "int32", "uint16", "uint8", "float8_e4m3fn_x4"
-PORT = 32
-RUNS = [(0, 128, 256, 2), (128, 256, 512, 4), (256, 384, 1024, 8), (384, C, 2048, 16)]
-CODES = 3072
-BASE = H - PORT
-LIFT, MANY, BIT = 512.0, 4096.0, 2.0
-POWERS = [1, 2, 4, 8, 16, 32]
-NUMBERS = [16, 48, 80, 112]
+LIFT, BIT = 1024.0, 2.0
+BIG = 2.0 ** -4
+SMALL = 1 / (BIG * C * C)
+POWERS = [1, 2, 3, 5, 8, 13, 21, 34, 55, 89]
+MID = 34
+END = "o"
+NW = 2
 
 SCRATCH = {}
 
@@ -24,9 +24,8 @@ def _sb(name, n, d):
 for _r in range(4):
     _sb("x%d" % _r, 4 * C, BF)
 for _b in range(4):
-    _sb("xp%d" % _b, C, BF)
+    _sb("xp%d" % _b, 2 * C, BF)
     _sb("bp%d" % _b, C, BF)
-    _sb("yb%d" % _b, C, BF)
 for _n in ("zz", "aa", "ya"):
     _sb(_n, 4 * C, BF)
 for _n, _w in (("uq", 128), ("uq2", 128), ("vq", 128), ("wq", 512), ("eq", 512), ("qx", C), ("qz", C), ("qa", C)):
@@ -36,20 +35,17 @@ for _s in ROUNDS:
     _sb("lq%d" % _s, C, MX)
     _sb("lq%ds" % _s, C, U8)
     _sb("lb%d" % _s, 28, U16)
-    _sb("lc%d" % _s, 14, U16)
+for _j in range(NW):
+    _sb("w%d" % _j, H + 2 * C, BF)
 for _n, _w, _d in (("ut", 512, BF), ("vt", 512, BF), ("mli", 28, I32), ("ones", 516, BF), ("et", 516, BF),
                    ("pi", 14, I32), ("pm", 14, I32), ("pmu", 14, U16), ("pf", 1, F32), ("pf1", 1, F32), ("off", 1, F32),
-                   ("offm", 1, F32), ("ofb", 1, F32), ("ofb1", 1, F32), ("nofb", 1, F32), ("inv", 1, F32),
-                   ("fi", 16, F32), ("ka", 16, F32), ("kb", 16, F32), ("kc", 16, F32), ("kd", 16, F32),
-                   ("k16", 16, BF), ("m16k", 16, BF), ("keep", C, BF), ("keepb", C, BF), ("keepm", C, BF),
-                   ("cc", C, BF), ("raw", C, BF),
-                   ("ui", 8, I32), ("up", 8, U16), ("mm", 28, U16), ("mf", 28, F32), ("sg", 28, F32), ("tt", 28, F32),
-                   ("os0", 28, F32), ("sel", 140, F32),
-                   ("mmf", 28, F32), ("sup", H, F32), ("sw", H, BF), ("bb", C, BF), ("sc", 672, BF),
-                   ("sa", 12 * H, BF), ("tr", 3 * H, BF), ("mu", C, BF), ("sm", C, F16), ("rr", 140, F32),
-                   ("nn", 140, F32), ("n16", 28, U16), ("m16", 28, U16),
-                   ("ls", 168, U16), ("wa", C, BF),
-                   ("w0", BASE + CODES, BF), ("w1", BASE + CODES, BF), ("f0", BASE + CODES, BF), ("f1", BASE + CODES, BF),
+                   ("offm", 1, F32), ("offq", 1, F32), ("offh", 1, F32), ("ofb", 1, F32), ("nofb", 1, F32), ("cb0", 1, F32), ("cb2", 1, F32),
+                   ("fi", 16, F32), ("ka", 16, F32), ("kb", 16, F32), ("k16", 16, BF), ("keep", H, BF), ("keepb", H, BF),
+                   ("cc", C, BF), ("raw", 2 * C, BF), ("ui", 8, I32), ("up", 8, U16),
+                   ("mm", 28, U16), ("mf", 28, F32), ("tt", 28, F32), ("os0", 28, F32), ("sel", 196, F32),
+                   ("mmf", 28, F32), ("sup", H, F32), ("sw", C, BF), ("bb", C, BF), ("so", H, BF), ("sc", 1680, F16),
+                   ("sa", 16 * H, F16), ("tr", 3 * H, BF), ("mu", C, BF), ("sm", C, F16),
+                   ("nn", 196, F32), ("n16", 28, U16), ("m16", 28, U16), ("ls", 16 * 14, U16), ("wa", 2 * C, BF),
                    ("mrow", C, F32), ("yo", C, F32)):
     _sb(_n, _w, _d)
 for _b in range(8):
@@ -57,187 +53,28 @@ for _b in range(8):
 
 SEMAPHORES = ["v", "a", "t", "gp"] + ["d%d" % i for i in range(28)]
 for _s in ROUNDS:
-    for _k in ("b", "c", "q", "s"):
+    for _k in ("b", "q", "s"):
         SEMAPHORES += ["arr%s%d" % (_k, _s), "snt%s%d" % (_k, _s)]
 
 SPANS = {"u": (0, 14), "l": (14, 28), "w": (0, 28), "": (0, 14)}
-ORDERS = [[], [], []]
-ORDERS = [o.split() for o in """+pm +pf +ofb +ofb1 +ka +pf1 +nofb +off +up +offm +kd +sel0 +kb +k16 +pmu +keepb +sel2 +inv +sel1 +kc +mf Ptt +uq Pmf +uq2s Psg
-x2@u Pos Pmm +uq2 x1.v@u +m16k q0@0-12 x3.v@u q1@12-20 Pq q2@20-28 x0@u u0@0-12 u1@12-14 x1.v@l Tsw1@14-20 x2@l
-Tsw2@20-28 Pdq Tb@l Tb.v@u Tso Th@l +raw Tc0 x3@l Th@u Tr1 Tr4 Tc1 Tr2 Tn0 +far Tn1 Tn@u x0@l +w0 Tn@l +num z1@u z3@l z0@l
-z1@l z2@l +keepm qz@l +w1.v z3@u wa z0@u z2@u a0@l a1@l p1 s1 a3@l l1 a2@l p2 o qz@u qa@l +eq1 s2 l2 p4.8 a0@u a1@u s4 +eq2
-l4 p8.8 s8 a2@u l8 +eq0 a3@u +eq3 p16 qa@u s16 e3@u l16 +keep e2@u e1@u p32.8 e0@u f16 so s32 e3@l l32 e1@l f48.8 lo f80.8
-+vq f112.6 my b0@u b1@u mx.v m@u m@l e2@l ml@u ml@l n0@u i3@u i2@u i3.v@l j3@u e0@l j3@l i2@l b1@l k3@u j2@u j2@l b0@l n1@u
-k2@l k2@u n1@l k3@l n0@l
+LOADS = [(0, 14), (14, 28)]
+BODY = """q@u u@u q@l Ptt Pmf Pos Pmm Pq@u Pq@l Ps1 Ps3 Ps4 Psc x0@u x1@u x2@u x3@u x0@l x1@l x2@l x3@l Tsw@l Tso Tb@l Tb@u Th@l Th@u
+Tc0 Tc1 Tc2 Tc3 Tn0 Tn1 Tn@w wa c0@l d0@l c1@l d1@l c2@l d2@l c3@l d3@l qz@l c0@u d0@u c1@u d1@u c2@u d2@u c3@u d3@u
+a0@l a1@l a2@l a3@l qa@l qz@u a0@u a1@u a2@u a3@u qa@u eb@u b0@u b1@u b2@u b3@u eb@l b0@l b1@l b2@l b3@l GLUE m@u m@l ml@u ml@l"""
+GLUE = " ".join("p%d" % n + " s%d l%d" % (n, n) * (n in [b - a for a, b in zip(POWERS, POWERS[1:])])
+                + " o so lo" * (n == 1 and END == "o") + {"tv": " t mv r st lt sr lr", "o": " t r st lt sr lr", "": ""}[END] * (n == MID)
+                for n in POWERS) + (" mu mr" if END else " mu mv mr")
+NEW = " g0@u h0@u g1@u h1@u g2@u h2@u g3@u h3@u g0@l h0@l g1@l h1@l g2@l h2@l g3@l h3@l"
+LAST = " mo g0@u h0@u g1@u h1@u g2@u h2@u g3@u h3@u" + "".join(
+    " g%d@%s h%d@%s" % (b, k, b, k) for k in ("14-20", "20-28") for b in range(4)) + " y0@0-12 y1@12-20 y2@20-28"
+ONCE = """+pi +fi +ui +cc +port +one +et +pm +sel0 +sc2 +sc5 +sc6 +pf +pmu +up +pf1 +off +ofb +ka +kb +offm +offq +offh +nofb +cb0 +cb2 +k16
++keepb +keep +mf +uq +uq2 +uq2s +own +raw +far +eq0 +eq1 +eq2 +eq3 +vq """ + "".join("+w%d " % j for j in range(NW))
+ORDERS = [o.replace("GLUE", GLUE).split() for o in (ONCE + BODY + NEW, BODY + NEW, BODY + LAST)]
+ORDERS = [o.split() for o in """+pi +fi +sel0 +ui +pm +pf +off +pf1 +nofb +sc2 +offm +cc +ka +kb +pmu +sc5 +k16 +sc6 +cb0 +mf +up +offq Ptt +uq +far.v Pos.v +uq2 +keepb +ofb Ps4 Pq@l Ps1 +keep.v Pmf Ps3 +uq2s x2@u q@u Psc.v +port Pq@u Pmm q@l u.v@u x2.v@l x1@u +w0 +cb2.v Tsw@l x0.v@l x0@u Tso Tb.v@u Tb@l Tc0 x3@l Tc2.v +raw Tc1 Th@u Th@l Tc3 +w1 Tn0 Tn1 x3.v@u Tn@w x1.v@l c3@l c2@u z0@l z1@l z2@l +own c1@u +one d3@l d2@u +et qz@l wa z0@u z3@u d1@u p1.v a0@l s1 a1@l a2@l a3@l +offh.v l1 qa@l o p2.6 qz@u s2 p3.6 l2 +eq1 s3 p5.4 so l3 a1.v@u a2@u s5 p8.4 l5 lo +eq3 s8 a0@u p13.8 a3@u l8 +eq0 s13 p21.6 l13 qa@u p34.4 s21 +eq2 l21 eb@u s34 r.v l34 t p55 st eb@l b2@u sr lt p89.8 b3@u lr b1.v@u mr.v mu.4 b0@u m@l b0@l m@u b1@l b3.v@l b2@l ml@u g3@u Ptt' ml@l g1@u n0@u n0@l n3@l g1@l g2@l Pos' Ps4' n2@u h3@u h1@u h1@l x0@u' Ps1' h2@l Ps3' q@u'
 ----
-x2@l q0@u u0@u Ptt Psg q1@l Pmf Pos Pmm Tsw1@l Pq Tb.v@u Tb@l x0@u Tso Pdq Th@l Th@u Tc1 Tc0 x0@l x3@l x1@u Tr1 Tr4 Tr2
-x1@l Tn0 Tn1 Tn@u Tn@l z0@u x3@u z1@l x2@u wa z0@l p1 z2@l z3@l qz@l s1 l1 a0@l p2 a2@l z2@u z1@u a3@l s2 a1@l l2 p4 z3@u
-qa@l s4 l4 qz@u o p8.4 s8 l8 a0@u p16.8 a1@u so a2@u s16 lo l16 p32.8 s32 l32 a3.v@u f16 qa@u f48 f80.8 f112.8 mx.v e0@u
-m@u e2@u my b0@u m@l ml@u e1@u ml@l n0@u e3@u b1@u e2@l i3@u e1@l e3@l i3.v@l e0@l Ptt' j3@u i2@l j2@l i2@u b0@l j3@l j2@u
-b1@l n0@l k3@u n1@u k3@l k2@u k2@l Psg' n1@l
+Pmf Pq@u q@l Pq@l u.v@u x3.v@l Pmm Tsw@l Psc x1@u x3.v@u Tso x2@l Tb.v@u x0@l Tc1 Tb@l Tc2 Tc3 Th@u Th@l Tc0 x2.v@u Tn0 Tn1 x1.v@l Tn@w c3@u z1@l z0@l c0@u wa z2@l z3@l d3@u c2@u qz@l c1@u d0@u p1 d2@u d1@u s1 l1 a0@l a2@l a1.v@l p2.8 qz@u a3@l s2 p3.4 l2 qa@l s3 o p5.10 l3 so s5 a2@u p8.6 a3@u l5 a0.v@u s8 p13.8 a1@u l8 lo s13 p21.8 l13 qa@u s21 p34.6 l21 t.v s34 r p55.6 l34 st eb@u b0@u sr p89.6 lt lr b3@u b2.v@u mr.v mu.4 b1@u m@l eb@l m@u b2.v@l ml@u ml@l b0@l b1@l Ptt' b3@l n0@u n1@l g2@l g0@l n1@u g2@u n3@u g3@l h2@l h0@l Ps4' Ps1' h2@u h3@l
 ----
-q0@u x1@u q1@l Pos Pmf x3.v@u u0@u Pq x0@u Pmm Tsw1@l Pdq Tb.v@u Tb@l Tso Th@l x1@l Tc0 Th@u Tr1 x0@l Tr4 Tc1 x3@l x2@l
-x2@u Tr2 Tn0 Tn1 Tn@u Tn@l z3@l z1@l z0@l z2@l wa p1 z0@u qz@l s1 a0@l l1 z1@u p2 a2@l z2@u s2 a1@l l2 z3@u a3@l p4 qa@l s4
-o l4 qz@u p8.4 s8 l8 a0@u p16.8 a1@u a2@u so s16 l16 a3.v@u p32.6 s32 lo l32 qa@u e0@u f16 f48.4 f80.8 f112.8 e2@u b0@u
-mx.v m@u e1@u my m@l ml@u b1@u ml@l e3@u e0@l e2@l mo e3@l e1@l i2@u i3.v@u i2@l n0@u j3@u i3@l j2@u j2@l b1@l k2@u j3@l
-n1@u k3.4@u b0@l y0@0-12 k2.v@14-20 n0@20-28 n1@14-20 k3@14-20 k3@20-28 n0@14-20 y1@12-20 k2.v@20-28 n1@20-28 y2.v@20-28""".split("----")]
-ORDERS = [o.split() for o in """+pm +pf +off +ka +offm +up +pf1 +kb +ofb +pmu +k16 +keepb +sel0 +ofb1 +nofb +sel2 +sel1 +mf Ptt +inv +kc +uq Psg.v +uq2s +kd x3@u +uq2 Pos.v
-q0@0-12 x0.v@u Pq +m16k u0@0-12 x1@u x2.v@u Pmf Pdq q1@12-20 q2@20-28 x3@l u1@12-14 Pmm Tsw1@14-20
-Tsw2@20-28 Tso Tb@l Tb.v@u Th@l Th@u Tr1 Tr4 x1@l Tr2 Tc0 Tc1 Tn0 Tn1 Tn@u Tn@l x0@l z1@u +num x2@l +far +raw z0@l z2@l
-+keepm z1@l wa z3@l z2@u qz@l z3@u +eq2 +w0 a0@l +w1.v a1@l p1 z0@u s1 l1 qz@u a3@l a2@l p2 qa@l +eq1 s2 l2 o +eq0 p4.6
-a1@u s4 a0@u l4 p8.8 s8 l8 a2@u a3@u +eq3 qa@u e0@u e2@u p16 +vq e3@u +keep s16 l16 p32.8 so f16 e1@u s32 l32 f48.8 f80.8
-lo f112.6 b0@u my e0@l mx.v e1@l m@u m@l b1@u e2@l b0@l ml@u ml@l i3.v@l i3@u n0@u i2@u e3@l j3@u j3@l j2@u i2@l b1@l j2@l
-n1@l k3@u k2@u n1@u k3@l k2@l n0@l
-----
-q0@u q1@l Ptt x2@l u0@u Pmf Psg.v Pmm Tsw1@l Pos Pq x0@l Tso Tb@l Tb.10@u Tc0 Pdq Th@l Th@u Tr1 Tr4 Tr2 x0@u Tc1 Tn0 x3@u
-x3@l x2@u Tn1 Tn@u x1@u x1@l Tn@l wa z0@u z0@l p1 z3@l z1@l z2@l qz@l s1 l1 z1@u a0@l p2 a2@l a1@l z2@u a3@l s2 l2 z3@u p4
-qa@l s4 l4 qz@u o p8.4 s8 a0@u l8 so p16.8 a1@u s16 a2@u l16 p32.8 s32 lo f16 l32 a3.v@u qa@u e1@u f48 e0@u e0@l e2@l e3@l
-f80.8 f112.8 e3@u b1@u mx.v e1@l m@u my m@l e2@u b0@u ml@u b0@l ml@l Ptt' i3@u i3.v@l n0@u i2@l i2@u j3@l j3@u b1@l n0@l
-k3@l j2@l j2@u n1@u k3@u n1@l k2@u Psg' k2@l
-----
-x0@u q0@u q1@l Pos Pmf Pq Pmm u0@u Tsw1@l Pdq Tso Tb@l x1@u Tc0 x3@l Tc1 x0@l Tb.v@u x1@l Th@l Th@u Tr4 x2@u x3@u Tr1 Tr2
-Tn0 Tn1 Tn@u Tn@l wa z0@l x2@l z1@l z3@l z2@l z0@u qz@l p1 s1 l1 z1@u z2@u a0@l p2 s2 a1@l l2 z3@u a2@l a3@l p4 qa@l s4 o
-l4 qz@u p8.4 a0@u s8 so l8 p16.8 a1@u s16 l16 lo a2@u p32.6 f16 a3.v@u s32 l32 qa@u f48.4 f80.8 f112.8 my e0@u mx.v m@u
-e1@u m@l ml@u b1@u e2@u b0@u ml@l e3@u e0@l i3.8@u mo e2@l i2.v@u j3@u j2@u b0@l i2@l e1@l i3@l e3@l n0@u j2@l j3@l b1@l
-n1@u k2@u k3.4@u k2@14-20 y0@0-12 k3@14-20 n1@14-20 n0@20-28 k3@20-28 k2.4@20-28 n0@14-20 y1@12-20 n1@20-28 y2.v@20-28""".split("----")]
-ORDERS = [o.split() for o in """+pm +pf +ka +pf1 +off +ofb +pmu +kb +k16 +keepb +sel0 +offm +sel2 +up +sel1 +nofb +ofb1 +mf Ptt +kc +inv +uq Psg.v +raw +uq2s Pos.v +uq2
-x1.v@u +kd Pq q0@0-12 +m16k Pdq x0@u Pmf Pmm q1@12-20 u0@0-12 x2@u x3@u +far q2@20-28 u1.v@12-14
-Tsw1@14-20 Tsw2@20-28 Tb@l Tso Tb.10@u Tc0.v x1@l Th@l Th@u Tr1 Tr4 x3@l Tr2 x0@l Tc1.v Tn0 x2@l Tn1 Tn@w z1@l +w0 z2@l
-z0@l +num z3@l z2@u wa qz@l +eq2 +keepm a0@l z0@u z1@u z3@u a1@l p1 a2@l +w1.v s1 l1 qz@u +eq1 a3@l p2 qa@l s2 l2 +eq0 o
-p4.6 a1@u s4 l4 a0@u p8.6 a3@u a2@u s8 l8 +eq3 +vq p16 qa@u s16 l16 +keep p32.8 e0@u s32 e1@u f16 so e0@l l32 f48.8 f80.8
-lo f112.8 e1@l e3@l my mx.v m@l m@u e3@u ml@l b1@u e2@l b0@u ml@u b0@l e2@u i3@u i2@u i3.v@l n0@u j3@l i2@l j3@u b1@l j2@u
-j2@l n1@u k3@l k2@u n0@l k3@u k2@l n1@l
-----
-q0@u Ptt q1@l Pmf Psg.v Pmm u0@u Pos.v Tsw1@l Tb@l Pq Tb.10@u Tso x0@u Pdq Th@l Tc0.v Th@u x0@l Tr1 Tr4 Tr2 Tc1.v Tn0 x2@u
-Tn1 x1@u Tn@w x1@l x2@l z0@l x3@l z1@l x3@u z3@l z2@l wa qz@l z0@u p1 a0@l s1 l1 z1@u a1@l p2 a2@l z2@u s2 l2 a3@l qa@l
-z3@u p4 s4 l4 qz@u o p8.4 s8 l8 a0@u p16.8 a1@u s16 a2@u l16 p32.8 s32 so l32 a3.v@u qa@u e0@u e2@u f16 e1@u f48 e0@l e3@l
-e1@l f80.8 lo f112.8 e3@u my mx.v b1@u e2@l m@u b0@u m@l ml@u b0@l i3@u ml@l Ptt' i3.v@l n0@u j3@u i2@l i2@u b1@l j3@l j2@l
-k3@u j2@u n1@u n1@l k3@l k2@u k2@l n0@l
-----
-q0@u Psg.v x1@l q1@l Pos.v Pmf x1@u Pq u0@u Pmm Tsw1@l Pdq Tso x0@u Tb@l Tb.10@u Tc0.v x0@l Th@l Th@u x3@l Tr1 x2@u Tr4 Tr2
-Tc1.v Tn0 Tn1 Tn@w x2@l z0@l wa z1@l z2@l x3@u p1 z3@l z0@u qz@l s1 l1 a0@l z1@u p2 z2@u s2 a3@l l2 a2@l a1@l p4 z3@u qa@l
-s4 l4 qz@u o p8.4 so s8 a0@u l8 p16.8 a1@u s16 l16 a2@u p32.6 f16 a3.v@u s32 l32 qa@u f48.4 lo e3@u f80.8 e1@u f112.8 my
-e0@u mx.v e2@u b0@u m@u b1@u m@l ml@u ml@l i3.8@u i2.v@u e0@l e1@l mo b0@l j3@u e2@l j2@u i2@l n0@u i3@l e3@l j2@l j3@l
-b1@l k2@u n1@u k3.4@u k3@14-20 y0@0-12 k2@14-20 k2@20-28 n0@14-20 k3.4@20-28 n0@20-28 n1@14-20 y1@12-20 n1@20-28 y2.v@20-28""".split("----")]
-ORDERS = [o.split() for o in """+pm +sel0 +sel1 +sel2 +pf +pmu +up +pf1 +off +ofb +ka +kb +offm +ofb1 +nofb +k16 +keepb +mf +uq Ptt +uq2 +uq2s Psg.v Pmf q0@u Pos.v Pmm
-x0@u u0@u q1@l Pq +kc +kd +inv x1@u x2@u x3@u
-Tsw1@l Pdq Tso Tb@l Tb.v@u x0@l x1@l x2@l x3@l Tc0.v Tc1.v Th@l Th@u Tr1 Tr4 Tr2 Tn0 Tn1 Tn@w
-+num +m16k +keepm +raw wa +far +w0 z0@l z1@l z2@l z3@l p1 qz@l z0@u +w1.v +own.v z1@u s1 a0@l l1 a1@l p2
-a2@l a3@l z2@u s2 l2 z3@u p4 qa@l s4 l4 qz@u +eq0 +eq1 +eq2 +eq3 +keep
-o p8 s8 so a0@u l8 p16.8 +vq a2@u s16 lo l16 a1@u a3.v@u p32.8 qa@u s32 f16.6 l32 r.v t st sr lt f48 eb@u f80.8 lr mu.v b1@u
-b0.v@u eb@l m@u mr m@l ml@u ml@l b0@l Ptt' n0@u b1@l i3@u i3.v@l i2@u j3@u i2@l j3@l k3@u j2@u j2@l n0@l k2@u k3@l n1@u n1@l
-k2@l q0@u' x1@u' u0@u' q1@l' x3@u' Psg.v' Pmf' Pos.v' Pmm' Pq'
-----
-Tsw1@l Pdq Tso Tb@l Tb.v@u x0@l x2@u x1@l x0@u x3@l x2@l Tc0.v Tc1.v Th@l Th@u Tr1 Tr4 Tr2 Tn0 Tn1 Tn@w
-wa z0@l z1@l z2@l z3@l qz@l p1 a0@l z0@u s1 l1 z1@u p2 z2@u a1@l a2@l s2 l2 z3@u a3@l qa@l p4 o s4 l4 p8 qz@u s8 a0@u l8
-p16.8 so s16 lo a1@u a2@u l16 a3.v@u p32.8 qa@u s32 l32 f16 eb@u r.v t st sr lt f48 f80.8 lr eb@l b1@u mu.v b0.v@u m@u mr m@l b0@l
-ml@u b1@l ml@l i3@u n0@u i3.v@l j3@u i2@u j3@l Ptt' i2@l k3@u n1@u j2@l j2@u k3@l k2@u n0@l n1@l k2@l x3@u' x1@u' q0@u' u0@u' q1@l'
-x2@l' Psg.v' Pmf' Pos.v' Pmm' Pq' x0@u'
-----
-Tsw1@l Pdq Tso Tb@l Tb.v@u x2@u x1@l x0@l x3@l Tc0.v Tc1.v Th@l Th@u Tr1 Tr4 Tr2 Tn0 Tn1 Tn@w
-wa z0@l z1@l z2@l z3@l p1 qz@l z0@u s1 a0@l l1 p2 z1@u z2@u a1@l s2 a2@l a3@l l2 p4 o z3@u qa@l s4 l4 qz@u p8.8 s8 so l8 lo
-a0@u p16.8 s16 a1@u a2@u l16 a3.v@u p32.8 qa@u f16 t eb@u s32 eb@l l32 r.v st sr lt f48 f80.6 lr mu.6 mr b0.v@u m@u b0@l b1.v@u
-ml@u i2@u m@l ml@l i3@u n0@u b1@l i2@l i3.v@l j3@u j3@l j2@u j2@l n1@u k3@u k2@u k2@14-20 k3@14-20 mo n0@20-28 y0@0-12 n0@14-20
-n1@14-20 k3.v@20-28 y1@12-20 n1@20-28 k2.v@20-28 y2.v@20-28""".split("----")]
-ORDERS = [o.split() for o in """+pm +pf +pmu +off +sel0 +up +offm +mf +pf1 +ofb Ptt +kb +uq +ka +uq2 +k16 +uq2s Psg.v +ofb1 +inv +kc Pmf q0@u q1@l +nofb
-Pos.v +kd x2@u x1@u x3.v@u +keepb +sel2 u0.v@u +sel1 Pmm x0.v@u Pq Tsw1@l Pdq x3@l +raw Tb@l x0@l x1@l Tso Tb.v@u x2@l
-Tc1.v Tc0.v Th@l Th@u Tr4 Tr1 Tr2 Tn1 Tn0 +m16k Tn@w z0@l wa z1@l z3@l +w0 +num z2@l qz@l +keepm +w1.v z0@u +far p1.10
-+own.v a1@l s1 l1 z1@u a0@l p2 z2@u a2@l a3@l s2 l2 z3@u +eq1 p4 qa@l s4 l4 qz@u +eq0 +eq3 +keep +eq2 +vq p8 s8 l8 p16.v o
-a0@u so a2@u s16 a1.v@u l16 a3.v@u p32.8 qa@u e1@u lo s32 f16.6 t e0@u l32 f48 r.v st sr lt lr e3@u e2@u f80.8 b0.v@u mu.v
-e0@l e1@l mr b1.v@u b0@l e3@l m@u m@l b1@l ml@u i3@u i2@u ml@l Ptt' i3.v@l e2@l n0@u i2.4@l j3@u j3@l k3@u j2@u j2@l n1@l
-n1@u x3.v@u' k2@u k2@l k3@l q0@u' n0@l
-----
-x2@u Psg.v q1@l x0.v@u Pmf u0.v@u Pos.v Pmm x1.v@u Pq x1.v@l Tsw1@l Tso x0@l Tb.v@u x2@l Tc0.v Pdq Tb@l Th@u x3@l Th@l
-Tc1.v Tr1 Tr4 Tr2 Tn1 Tn0 Tn@w z2@l z3@l z1@l wa z0@l qz@l z0@u p1 s1 l1 z2@u a0@l z1@u p2 s2 a2@l l2 a1@l p4 a3.v@l z3@u
-qa@l s4 qz@u o l4 p8.v s8 l8 p16.8 a0.v@u s16 a1@u a2@u so l16 a3.v@u p32.8 qa@u s32 lo f16 e0@u l32 e1@u t.6 r.v st sr lt
-e2@u e0@l e1@l f48 e3@u f80.8 e3@l lr mu.v b1@u b0.v@u m@u mr e2@l b0@l m@l ml@u b1@l ml@l n0@u i3.v@l i3@u j3@u i2@u i2@l
-j3@l j2@u k3@l n1@u Ptt' k3@u j2@l n1@l Pmf' n0@l k2@u k2@l
-----
-q0@u q1@l x3.v@u x1@u Psg.v x2@l u0.v@u Pmm x0@u Pos.v Tsw1@l Pq x2@u Tso Tb.v@u Tc1.v Pdq Tb@l Tc0.v Th@u x0@l Th@l Tr2
-Tr1 Tr4 Tn0 x1@l Tn1 Tn@w wa z0@l x3@l z1@l z2@l p1 z3@l qz@l z0@u s1 l1 p2 a0@l z2@u a2@l z1@u s2 a3@l a1.v@l l2 z3@u p4.4
-qa@l s4 o l4 qz@u p8.8 s8 l8 so p16.10 s16 a2.v@u l16 a3.v@u a0@u a1@u p32.8 qa@u f16 s32 e1@u e0@u e0@l e3@u lo e2@u e3@l
-t l32 r.v f48.v e1@l sr st e2@l f80.6 lt lr mu.10 b1.v@u m@u mr mo b0.v@u m@l ml@u b0.v@l ml@l i3.6@u i3.v@l i2@u n0@u i2@l
-b1@l j3@l j3@u j2@u j2@l k3@u k2@u n1@u k3@14-20 k2@14-20 y0@0-12 n1@14-20 n0@14-20 y1@12-20 n0@20-28 k2.v@20-28 k3.v@20-28
-n1@20-28 y2.v@20-28""".split("----")]
-ORDERS = [o.split() for o in """+pm +pf +up +off +ofb +nofb +offm +pf1 +sel0 +ka +sel1 +kb +sel2 +k16 +pmu +keepb +mf +uq +uq2s +uq2 +kc Ptt +inv q0@u
-Psg.v Pmf +raw +kd q1@l Pos.v +ofb1 u0@u Pmm x0@w Pq Tsw1@l Pdq Tso Tb@l Tb.v@u Th@l x1@w Th@u Tr4 x3@w Tr1 Tc1.v Tr2 x2@w
-Tc0.v Tn1 Tn0 Tn@w +m16k +far +w1.v +num z1@l z0@l z2@l wa.4 z3@l +keepm qz@l z0@u +w0 z1@u +eq3 a0.v@l p1 s1 a1@l l1 +eq1
-p2 z2@u a2@l s2 a3@l +own.v l2 p4 z3@u qa@l qz@u s4 o +eq0 +keep l4 +vq p8.4 +eq2 so s8 a0@u l8 p16.8 a2@u a1@u s16 l16
-a3.v@u p32.4 lo qa@u s32 f16.6 l32 t r.10 e0@u st e1@u f48 sr lt e2@u e3@u e3@l f80.8 lr e0@l b0.v@u mu.4 m@u mr e1@l m@l
-ml@u b1@u i3@u ml@l e2@l b0@l Ptt' b1@l i3.v@l j3@u i2@u j3@l i2@l n0@u n1@u j2@u j2@l n0@l n1@l k3@l k3@u k2@u k2@l
-----
-q0@u q1@l Psg.v x0@w Pmf u0@u Pos.v Pq Pmm Tsw1@l Tb@l Pdq Tb.v@u Tso Th@l x2@w x3@w Th@u x1@w Tr4 Tr1 Tc1.v Tr2 Tc0.v Tn1
-Tn0 Tn@w z0@l z3@l wa z1@l z2@l qz@l p1 z0@u z3@u s1 a0@l l1 z2@u p2 z1@u s2 qz@u l2 a1@l a2@l p4.v a3@l qa@l o s4 l4 a0@u
-p8.8 a2@u a1@u so s8 l8 a3.v@u p16.4 s16 lo l16 p32.4 f16 qa@u s32 l32 t e1@u r.v e2@u st f48.6 e0@u lt b1@u sr e0@l f80.6
-lr mu.4 e1@l b0.v@u mr.6 m@u b0@l m@l e3@u ml@u ml@l b1@l e3@l n0@u i3@u i3@l i2@l i2@u e2@l n1@u j3@u j3@l Ptt' j2@l k3@u
-j2@u n0@l n1@l k3@l k2@u k2@l
-----
-x1@w q0@u u0@u q1@l Pmf Psg.v Pos.v Pmm x0.v@w Pq Tsw1@l Tb.v@u Tb@l Tso Th@u Th@l Tc1.v Pdq Tr2 Tr1 Tr4 x3@w Tc0.v Tn1 Tn0
-Tn@w z3@l z1@l x2@w wa z2@l z0@l p1 qz@l z0@u z3@u s1 l1 z2@u z1@u a0@l p2 a1@l s2 a2@l l2 a3.v@l p4 o qz@u qa@l s4 l4 p8.6
-so s8 a0@u l8 p16.10 a2@u s16 lo l16 a1.v@u a3@u p32.10 qa@u e3@u s32 f16 e1@u t l32 e2@u e0@u r.6 st sr e3@l lt e1@l lr
-e0@l f48 e2@l f80.6 mr.8 mu.6 m@l m@u ml@l ml@u i3.v@l i2.v@u b1@u b0@u i3@u i2@l j3@l b1@l b0@l j3@u k3@20-28 k3@u j2@u
-j2@l n0@u k2@u n1@u mo k2@14-20 k3@14-20 y0@0-12 n1@14-20 n0@14-20 n0@20-28 y1@12-20 k2.v@20-28 n1@20-28 y2.v@20-28""".split("----")]
-ORDERS[0] = """+pm +sel0 +sel1 +sel2 +pf +pmu +up +pf1 +off +ofb +ka +kb +offm +ofb1 +nofb +k16 +keepb +mf +uq Ptt +uq2 +uq2s Psg.v Pmf q0@u Pos.v Pmm x0@u u0@u q1@l Pq +kc +kd +inv x1@u x2@u x3@u Tsw1@l Pdq Tso Tb@l Tb.v@u x0@l x1@l x2@l x3@l Tc0.v Tc1.v Th@l Th@u Tr1 Tr4 Tr2 Tn0 Tn1 Tn@w +num +m16k +keepm +raw wa +far +w0 z0@l z1@l z2@l z3@l p1 qz@l z0@u +w1.v +own.v z1@u s1 a0@l l1 a1@l p2 a2@l a3@l z2@u s2 l2 z3@u p4 qa@l s4 l4 qz@u +eq0 +eq1 +eq2 +eq3 +keep o p8 s8 so a0@u l8 p16.8 +vq a2@u s16 lo l16 a1@u a3.v@u p32.8 qa@u s32 f16.6 l32 r.v t st sr lt f48 eb@u f80.8 lr mu.v b1@u b0.v@u eb@l m@u mr m@l ml@u ml@l b0@l Ptt' n0@u b1@l i3@u i3.v@l i2@u j3@u i2@l j3@l k3@u j2@u j2@l n0@l k2@u k3@l n1@u n1@l k2@l""".split()
-ORDERS = [o.split() for o in """+sel0 +pm +pf +pmu +up +off +pf1 +ofb +kd +offm +sel1 +kc +kb +mf +uq +ka +ofb1 +uq2s Ptt +uq2 +far +w1.v x3@u Psg.v q0@u
-+k16 +keepb x2.v@u u0@u Pos.v Pmf q1@l +nofb x2.v@l x0@u Pq Pmm +m16k x1.v@u Tsw1@l x3.v@l Pdq Tso x0@l +sel2 Tb.10@l Tb@u
-Tc0.v Th@l Th@u +raw Tr1 Tr4 Tr2 x1@l Tc1.v Tn0 Tn1 Tn@w +eq0 z2@l z0@l +keepm z3@l z1@l c2.6@u c1@u c0@u qz@l c3@u wa +w0
-+eq2 d@u p1.6 qz@u o s1 +inv a2@l +num a1.v@l a0@l l1 a3.v@l p2.6 qa@l s2 l2 +eq3 a1@u p4.v a2@u so s4 a3@u a0@u +eq1 l4
-+keep qa@u p8.6 s8 l8 eb@u +vq p16.8 s16 b2@u l16 p32.8 lo s32 f16 eb@l l32 f48.10 b0@u f80.8 b1.v@u f112.8 b3.v@u my.4
-b0@l mx.v b1@l m@l b2@l m@u ml@l ml@u b3@l g2@u n0@l g2@l n1@u g3@u n1@l n0@u g3@l h2@u h3@u x0@u' h2@l q0@u' h3@l
-----
-x3@u Ptt q1@l x2@u u0@u x1.v@l Psg.v Pmf Pos.v Pmm Pq x0@l x1@u Tsw1@l Pdq Tb.8@u Tb.6@l Tso Th@u Th@l Tc1.v Tr2 Tr1 Tr4
-x2@l Tc0.v Tn1 Tn0 x3@l Tn@w z3@l z0@l z2@l c2@u c3@u c0@u z1@l c1@u wa p1 qz@l a0@l a1@l d@u s1 qz@u o l1 p2.v a2@l s2 l2
-a3.v@l p4.8 a0.v@u a1@u s4 l4 a2@u a3@u qa@l p8.6 qa@u s8 l8 so eb@u p16.10 s16 l16 b1@u eb@l p32.6 f16.8 b2@u s32 lo l32
-f48.10 f80.8 f112.10 b0@u my mx.v m@u b0@l b1@l m@l b3@l b3@u ml@u b2.v@l g2@u ml@l n0@u n1@l g3@u g3@l n0@l n1@u g2@l h2@u
-h3@u h3@l x0@l' q0@u' h2@l
-----
-Ptt q1@l x1@u Psg.v x1@l Pos.v Pmf u0@u x3@l x0.v@u Pmm Tsw1@l Pq Tso Pdq Tb@l x2@u Tb.v@u Tc0.v Th@l Th@u x3@u Tc1.v Tr1
-Tr4 x2@l Tr2 Tn1 Tn0 Tn@w z0@l c3@u c1@u z2@l c0@u c2@u z3@l wa z1@l qz@l d@u p1 s1 a2.v@l l1 a3.v@l qz@u a0@l a1@l qa@l p2
-s2 l2 o p4.10 s4 a1@u so a2@u l4 p8.v a3@u s8 l8 p16.10 s16 a0@u lo l16 qa@u eb@u p32.4 f16.4 s32 l32 f48.8 eb@l b0.v@u
-f80.6 b2@u b1.v@u f112.10 mx.v b2.v@l b3@u my m@u b0@l b3@l m@l ml@u b1.v@l g2@u n0@u ml@l g3@u mo n1@u g3@14-20 g2@14-20
-h2@u h3@u g2@20-28 g3@20-28 n1@14-20 y0@0-12 h3@14-20 n0@14-20 h2@14-20 y1@12-20 h2@20-28 n1@20-28 n0@20-28 h3@20-28
-y2.v@20-28""".split("----")]
-POWERS, NUMBERS = [1, 2, 3, 5, 8, 13, 21, 34], [5, 13, 26, 47, 81, 115]
-ORDERS = [o.split() for o in """+sel0 +pm +pf +off +sel1 +ofb +pmu +pf1 +kc +ka +kb +offm +kd +up +mf +own.v +uq Ptt +uq2 +uq2s +k16 Psg.v q0@u +w1.v
-+keepb x0@u q1@l +nofb +far +m16k +ofb1 Pos.v u0@u x3@u Pmf +sel2 Pq Pmm x2.v@l x1@l Tsw1@l x1.v@u Tb.10@l Tb@u Pdq Tso
-x3.v@l Tc0.v Th@l +keepm Th@u Tr4 Tr1 Tr2 Tc1.v x0@l Tn0 Tn1 Tn@w x2@u +eq2 +w0 z1@l +raw z0@l c0@u wa.8 c1@u +eq0 z3@l
-z2@l c3@u c2.6@u qz@l d@u +inv p1.6 +num qz@u s1 a1@l l1 a3.v@l a2@l p2 a0.v@l o.10 p3 s2 qa@l a1@u l2 s3 p5 so l3 a0@u p8
-a2.v@u +keep lo a3.v@u s5 l5 qa@u p13 s8 +eq1 l8 f5.6 +eq3 eb@u s13 p21.4 l13 eb@l f13.4 s21 +vq l21 p34 f26.v s34 b2@u r.v
-t.8 f47 l34 sr st lr f81 b3.v@u lt mr b1.v@u b0@u mu.v m@l m@u ml@l b0@l b2@l b1.v@l b3@l ml@u n0@l g2@u g3@u Ptt' n1@l
-g2@l n1@u h2@u h3@u g3@l n0@u h2@l q0@u' x2@u' x1@l' h3@l
-----
-Psg.v q1@l x1@u u0@u Pmf x3@l x0.v@u Pos.v Pq Pmm Pdq Tsw1@l Tso x2@l Tb.10@u Tb.6@l Tc1.v Th@u Th@l x3@u Tr2 Tr4 Tr1 Tc0.v
-x0@l Tn1 Tn0 Tn@w z3@l wa z0@l z2@l c0@u c1@u c2@u z1@l c3@u qz@l d@u p1 s1 l1 qz@u o p2 a1@l a0.v@l so s2 p3.8 l2 a2@l
-a3.v@l p5 a1@u s3 a2@u qa@l a3@u a0.v@u s5 l3 l5 p8 p13 f5.v qa@u s8 l8 p21 lo f13.v s13 eb@u l13 s21 p34 f26.v l21 eb@l
-r.v s34 b2@u f47.6 t l34 sr st lr f81 lt b1@u b0.v@u mr mu.v m@u b0@l m@l b1@l b3@l ml@u b2.v@l b3@u ml@l g2@u g3@u g3@l
-n0@u n1@l n0@l n1@u h2@u h3@u h3@l q0@u' g2@l h2@l
-----
-Ptt q1@l x1@l Pmf u0@u Psg.v Pos.v x0@l Pmm Pq x0.v@u Tsw1@l Pdq Tso Tb.v@u x3@l Tb@l x3@u Tc0.v Th@u x2@l Th@l Tc1.v Tr1
-Tr2 x1@u Tr4 Tn0 Tn1 x2@u Tn@w z0@l c2@u z1@l z3@l z2@l wa c0@u c1@u c3@u p1 qz@l d@u s1 l1 a2.v@l a3.v@l a0@l qz@u a1@l p2
-o qa@l s2 p3.6 l2 so s3 p5.8 l3 s5 a1@u p8.8 a3@u l5 a2.v@u s8 p13 f5.v a0@u l8 s13 p21.4 l13 qa@u f13.10 lo p34 s21 eb@u
-f26.4 l21 t s34 r.v b0.v@u f47 l34 eb@l st sr b2@u f81.10 lr lt b1.v@u mu.v b2.v@l b3@u m@u mr m@l b0@l ml@u b1@l ml@l b3@l
-n0@u g2@u n1@u g3@u g2@14-20 g3@20-28 g3@14-20 h2@u h3@u n1@14-20 mo g2@20-28 y0@0-12 n0@14-20 h2@14-20 h3@14-20 h3@20-28
-y1@12-20 h2@20-28 n1@20-28 n0@20-28 y2.v@20-28""".split("----")]
-ORDERS = [o.split() for o in """+sel0 +pm +sel1 +pf +kc +off +pf1 +up +pmu +kb +ka +offm +ofb +kd +k16 +mf +keepb +own.v Ptt +uq Psg.v +ofb1 +uq2s x3@u
-+far +uq2 q0@u +w1.v q1@l Pos.v +nofb Pmf +sel2 x0@u u0@u Pq +m16k Pmm Tsw1@l x2@l Pdq x3.v@l x1@l Tb.10@l x1.v@u Tso Th@l
-Tb@u +w0 Tc0.v Th@u Tr1 Tr4 +raw Tr2 x2@u +keepm Tc1.v Tn0 Tn1 +eq2 Tn@w x0@l +eq0 z2@l z3@l z0@l z1@l c2.6@u c0@u wa.4
-c3@u c1@u +inv +num qz@l d@u p1.6 qz@u s1 l1 a3.v@l a0.v@l a1@l a2@l p2 o.10 s2 qa@l p3 a1@u l2 s3 p5 a0@u a3.v@u l3 a2.v@u
-p8 s5 so +keep l5 qa@u p13 s8 +eq1 l8 +eq3 f5.10 s13 p21.4 l13 eb@u f13.4 s21 +vq l21 p34 lo f26.v b2@u s34 r.v l34 t.8 sr
-f47 st f81.4 lr lt b1.v@u mu.v b3@u mr eb@l m@l m@u ml@l b0@u b0@l b1@l b2@l b3@l ml@u Ptt' g2@u g3@u n0@l n1@l g2@l n0@u
-n1@u h3@u g3@l h2@u h2@l q0@u' h3@l
-----
-q1@l Psg.v x1@u u0@u Pmf Pos.v Pmm x1@l Pq Pdq Tsw1@l x0@u x2.v@l Tso Tb.10@u Tb.6@l x2@u Th@u x0@l x3@u Th@l x3@l Tr2
-Tc1.v Tr4 Tr1 Tc0.v Tn1 Tn0 Tn@w c2@u z2@l z0@l wa c1@u c3@u z3@l c0@u z1@l qz@l p1 d@u s1 o l1 qz@u p2.6 a0.v@l s2 a1@l
-p3.4 a2@l l2 a3.v@l s3 qa@l p5 a2@u l3 s5 a1.v@u p8 a3@u l5 so a0.v@u s8 p13 f5.6 qa@u l8 s13 p21 eb@u f13.v l13 lo p34
-f26.v s21 eb@l b2@u l21 s34 f47.6 l34 r.v t sr st lr lt f81 b1@u mr b0.v@u mu.v b0@l m@u b3@u b1@l m@l ml@u b3@l ml@l
-b2.v@l g2@u n0@u n1@l g3@u n1@u n0@l h2@u g3@l g2@l h3@u x0@u' h3@l q0@u' h2@l
-----
-Ptt q1@l x3@l x2.v@u Pmf Psg.v u0@u Pos.v Pmm Pq Tsw1@l Pdq x3@u Tb.v@u Tso Tb@l Th@u x2@l Tc1.v x0@l Th@l Tr2 Tr1 x1@l
-x1@u Tr4 Tc0.v Tn1 Tn0 Tn@w wa c0@u c3@u z0@l z2@l z3@l c2@u z1@l c1@u p1 qz@l d@u s1 qz@u l1 a0@l a2.v@l a3.v@l a1@l p2
-qa@l s2 p3.6 l2 o.4 s3 p5.6 l3 so a1@u s5 p8.8 l5 a3@u a2.v@u p13 a0@u s8 f5.v l8 lo s13 p21.6 l13 qa@u f13.10 p34 eb@u
-eb@l s21 f26.6 l21 s34 r.v t l34 b0.v@u f47 st sr b2@u f81.10 lt lr b1.v@u mu.v b3@u b2.v@l mr m@u b0@l m@l ml@u b1@l ml@l
-b3@l g2@u g3@u g3@20-28 n0@u n1@u h2@u g2@14-20 g3@14-20 mo h3@u g2@20-28 n1@14-20 y0@0-12 h3@14-20 n0@14-20 h2@14-20
-h3@20-28 y1@12-20 n1@20-28 n0@20-28 h2@20-28 y2.v@20-28""".split("----")]
+Pos x1@l q@u Ps3 Pq@u q@l Pmf u.v@u Pmm x3@l Pq@l Tsw@l x2.v@l x0@u Psc Tb@u Tso Tb.v@l Tc0.v Tc2 Tc3 Th@l Th@u x3@u Tc1 Tn1 Tn0 Tn@w x1.v@u x2@u z2@l z1@l x0@l z0@l c3@l wa c2@u c0@u d3@l z3@u c1@u qz@l d2@u p1 d0@u a0@l d1@u s1 a1@l l1 +vq a2@l a3@l p2.v qz@u s2 p3.6 l2 qa@l o s3 p5.6 a0@u l3 s5 p8.8 l5 s8 a1@u p13.8 l8 so a3@u s13 p21.10 a2@u l13 lo s21 p34.6 qa@u eb@u l21 s34 r t.v p55 l34 st sr b0.v@u lt eb@l lr p89.6 b2.v@u mu.v b1@u b3@u mr.4 m@u b1.v@l b0@l b2@l b3@l ml@u mo m@l n1@u ml@l g2@20-28 g1@20-28 n0@u n2@u n3@u g0.2@14-20 g3@14-20 g0@20-28 g3@20-28 y0@0-12 n2@14-20 h0@14-20 n1@14-20 h3@14-20 y1@12-20 h0@20-28 h2@20-28 h3@20-28 h1@20-28 y2@20-28""".split("----")]
 
 
 def rank_program(g, core, T, topo):
@@ -316,7 +153,8 @@ def rank_program(g, core, T, topo):
             ts(out, x, a, OP.mult, b, OP.add)
         else:
             reads = [x] + [c for c in (a, b) if isinstance(c, tuple)]
-            op("a", [out], reads, lambda: g.scalar.activation(ap(out), ap(x), SAME, bias=ap(b), scale=ap(a)))
+            f = SAME if isinstance(b, tuple) else COPY
+            op("a", [out], reads, lambda: g.scalar.activation(ap(out), ap(x), f, bias=ap(b), scale=ap(a)))
 
     def vcopy(out, x):
         op("v", [out], [x], lambda: g.vector.tensor_copy(ap(out), ap(x)))
@@ -331,7 +169,7 @@ def rank_program(g, core, T, topo):
         op("v", [out], [d0, d1], lambda: g.vector.tensor_tensor_scan(ap(out), ap(d0), ap(d1), 0.0, o0, o1))
 
     def held(out, x, keep):
-        scan(out, R(keep, 0, x[2] - x[1]), x, OP.mult if keep == "keepm" else OP.add, OP.max)
+        scan(out, R(keep), x, OP.add, OP.max)
 
     def act(out, x, scale=1.0):
         op("a", [out], [x], lambda: g.scalar.activation(ap(out), ap(x), COPY, scale=scale))
@@ -366,21 +204,21 @@ def rank_program(g, core, T, topo):
         nd[0] += 1
         op(q, writes, reads, lambda: Q[q].dma_start(out, in_, **how), sem, 16)
 
-    def lanes(src, dst, k):
+    def lanes(src, dst):
         return topo.engines(src, dst)[:8]
 
     def send(s, land, src, k, codes=False):
         dst = T.cores[rank ^ s]
-        cnt["arr%s%d" % (k, s)] = len(lanes(dst, core, k))
-        note("g", [], [land], ("arr%s%d" % (k, s), len(lanes(dst, core, k))))
-        e = lanes(core, dst, k)
+        cnt["arr%s%d" % (k, s)] = len(lanes(dst, core))
+        note("g", [], [land], ("arr%s%d" % (k, s), len(lanes(dst, core))))
+        e = lanes(core, dst)
         rid, pid, _ = topo.addr(dst)
         hazards("g", [src], [])
         o, i = ap(land), ap(src)
         if codes:
             o, i = o.bitcast(dt.uint8), i.bitcast(dt.uint8)
-        g.remote_dma(out_ap=o, in_ap=i, remote_sem=T.sem["arr%s%d" % (k, s)], local_sem=T.sem["snt%s%d" % (k, s)],
-                     pid=pid, routing_id=rid, dma_engine_mask=sum(1 << j for j in e))
+        ins = g.remote_dma(out_ap=o, in_ap=i, remote_sem=T.sem["arr%s%d" % (k, s)], local_sem=T.sem["snt%s%d" % (k, s)],
+                           pid=pid, routing_id=rid, dma_engine_mask=sum(1 << j for j in e))
         sem = "snt%s%d" % (k, s)
         cnt[sem] = len(e)
         note("g", [src], [], (sem, len(e)))
@@ -398,76 +236,62 @@ def rank_program(g, core, T, topo):
         op("g", [r], [], lambda: g.iota(ap(r), pattern, base, cm, allow_small_or_imprecise_dtypes=True) if f
            else g.iota(ap(r), pattern, base, cm))
 
-    iota(R("pi"), [[0, 14]], 0, 1)
-    iota(R("fi"), [[1, 16]], 0, 0)
-    iota(R("ui"), [[16, 8]], 0, 0)
-    for a, b, c, st in RUNS:
-        iota(R("cc", a, b), [[st, b - a]], c, 0)
-    iota(R("raw", H, C), [[1, H]], PORT, 0)
-    e, one = R("et"), R("ones")
-    iota(one, [[0, 516]], 1, 0)
-    op("g", [e], [one], lambda: g.affine_select(ap(e), ap(one), [[-1, 516]], OP.is_equal, 0.0, 3, 4))
+    def odd(n, a, b):
+        return R(n, 2 * a + 1, 2 * b, 2)
 
-    pf, pf1, off, offm, ofb, ofb1, nofb, inv = [R(n) for n in ("pf", "pf1", "off", "offm", "ofb", "ofb1", "nofb", "inv")]
-    upk, uqc, uq2 = R("up"), R("uq"), R("uq2")
-    small = {
-        "pm": lambda: ts(R("pm"), R("pi"), 15, OP.bitwise_and),
-        "sel0": lambda: fill(R("sel"), 1.0),
-        "sel1": lambda: fill(R("sel", 0, 140, 5), 0.0),
-        "sel2": lambda: fill(R("sel", 2, 140, 5), -1.0),
-        "pf": lambda: vcopy(pf, R("pm", 0, 1)),
-        "pmu": lambda: vcopy(R("pmu"), R("pm")),
-        "up": lambda: vcopy(upk, R("ui")),
-        "pf1": lambda: ts(pf1, pf, 1.0, OP.add),
-        "off": lambda: ts(off, pf, 15.0, OP.is_lt, LIFT, OP.mult),
-        "ofb": lambda: ts(ofb, pf, 15.0, OP.is_lt, BIT, OP.mult),
-        "ka": lambda: ts(R("ka"), R("fi"), pf, OP.is_equal, -2 * BIT, OP.mult),
-        "kb": lambda: ts(R("kb"), R("fi"), pf1, OP.is_equal, BIT, OP.mult),
-        "offm": lambda: ts(offm, off, float(H), OP.subtract),
-        "ofb1": lambda: ts(ofb1, ofb, 1.0, OP.add),
-        "nofb": lambda: ts(nofb, ofb, -1.0, OP.mult),
-        "k16": lambda: tt(R("k16"), R("ka"), R("kb"), OP.add),
-        "keepb": lambda: pick("a", R("keepb", 0, H), R("k16"), R("pmu")),
-        "keep": lambda: act(R("keep", 0, H), R("keepb", 0, H), LIFT / BIT),
-        "keep2": lambda: vcopy(R("keep", H, C), R("keep", 0, H)),
-        "keepb2": lambda: vcopy(R("keepb", H, C), R("keepb", 0, H)),
-        "keepm2": lambda: vcopy(R("keepm", H, C), R("keepm", 0, H)),
-        "mf": lambda: ts(R("mf"), R("mli"), offm, OP.add),
-        "uq": lambda: quant("uq", R("ut")),
-        "uq2": lambda: op("v", [uq2], [uqc, upk], lambda: g.vector.tensor_copy(
-            ap(uq2).bitcast(dt.uint32), ap(uqc).bitcast(dt.uint32).indirect(ap(upk)))),
-        "uq2s": lambda: pick("a", R("uq2s"), R("uqs"), upk),
-        "kc": lambda: ts(R("kc"), R("fi"), pf, OP.not_equal),
-        "kd": lambda: ts(R("kd"), R("fi"), pf1, OP.is_equal, MANY - 1, OP.mult),
-        "inv": lambda: ts(inv, pf, 15.0, OP.is_equal, 1 / MANY, OP.max),
-        "m16k": lambda: tt(R("m16k"), R("kc"), R("kd"), OP.add),
-        "keepm": lambda: pick("a", R("keepm", 0, H), R("m16k"), R("pmu")),
-        "vq": lambda: quant("vq", R("vt")),
-    }
+    def slot(half, j):
+        return R("sel", 98 * half + j, 98 * half + 98, 7)
+
+    def term(j):
+        return R("sc", 105 + 16 * j, 105 + 16 * 98, 112)
+
+    pf, pf1, off, offm, offq, offh, ofb, nofb = [R(n) for n in "pf pf1 off offm offq offh ofb nofb".split()]
+    upk, uqc, uq2, e, one = R("up"), R("uq"), R("uq2"), R("et"), R("ones")
     top = len(POWERS) - 1
-
-    def once(name, q):
-        if name in small:
-            small[name]()
-        elif name in ("w0", "w1"):
-            for a, b, c, st in RUNS:
-                copy(q, R(name, BASE + c, BASE + c + st * (b - a), st), R("cc", a, b))
-        elif name in ("raw", "own"):
-            copy(q, R("raw" if name == "raw" else "w%d" % (top % 2), 0, H), R("cc", 0, H))
-        elif name == "far":
-            copy(q, R("wa", H, C), R("cc", H, C))
-        elif name == "num":
-            for a, b, c, st in RUNS:
-                for w in ("f0", "f1"):
-                    iota(R(w, BASE + c, BASE + c + st * (b - a), st), [[1, b - a]], a - H, 0)
-            iota(R("f0", H, C), [[1, H]], 0, 0)
-        elif name == "nup":
-            iota(R("f%d" % (len(NUMBERS) % 2), 0, H), [[1, H]], -H, 0)
-        else:
-            b = int(name[2])
-            quant("eq", R("et", 3 - b, 515 - b), 128 * b, 128 * b + 128)
-
-    first, lower, banks = {}, {}, {}
+    mid = POWERS.index(MID) if END else top
+    small = {
+        "pi": lambda q: iota(R("pi"), [[0, 14]], 0, 1),
+        "fi": lambda q: iota(R("fi"), [[1, 16]], 0, 0),
+        "ui": lambda q: iota(R("ui"), [[16, 8]], 0, 0),
+        "cc": lambda q: iota(R("cc"), [[2, C]], -C, 0),
+        "port": lambda q: iota(odd("raw", H, C), [[2, H]], 1 - H, 0),
+        "one": lambda q: fill(one, 1.0) if q == "v" else iota(one, [[0, 516]], 1, 0),
+        "et": lambda q: op("g", [e], [one], lambda: g.affine_select(ap(e), ap(one), [[-1, 516]], OP.is_equal, 0.0, 3, 4)),
+        "pm": lambda q: ts(R("pm"), R("pi"), 15, OP.bitwise_and),
+        "sel0": lambda q: fill(R("sel", 0, 98), 0.0),
+        "sc2": lambda q: ts(term(2), R("pm"), 0.0, OP.mult),
+        "sc5": lambda q: ts(term(5), R("pm"), 0.0, OP.mult, 0.25, OP.add),
+        "sc6": lambda q: ts(term(6), R("pm"), 0.0, OP.mult),
+        "pf": lambda q: vcopy(pf, R("pm", 0, 1)),
+        "pmu": lambda q: vcopy(R("pmu"), R("pm")),
+        "up": lambda q: vcopy(upk, R("ui")),
+        "pf1": lambda q: axb(q, pf1, pf, 1.0, 1.0),
+        "off": lambda q: ts(off, pf, 15.0, OP.is_lt, LIFT, OP.mult),
+        "ofb": lambda q: axb(q, ofb, off, BIT / LIFT, 0.0),
+        "ka": lambda q: ts(R("ka"), R("fi"), pf, OP.is_equal, -2 * BIT, OP.mult),
+        "kb": lambda q: ts(R("kb"), R("fi"), pf1, OP.is_equal, BIT, OP.mult),
+        "offm": lambda q: axb(q, offm, off, 1.0, -float(C)),
+        "offq": lambda q: axb(q, offq, off, 1.0 + C * BIT / LIFT, -float(C + 1)),
+        "offh": lambda q: axb(q, offh, off, -0.5, float(H)),
+        "nofb": lambda q: axb(q, nofb, off, -2 * BIT / LIFT, 0.0),
+        "cb0": lambda q: axb(q, R("cb0"), off, BIG * BIT / LIFT, BIG),
+        "cb2": lambda q: axb(q, R("cb2"), off, -BIG * BIT / LIFT, 0.0),
+        "k16": lambda q: tt(R("k16"), R("ka"), R("kb"), OP.add),
+        "keepb": lambda q: pick(q, R("keepb"), R("k16"), R("pmu")),
+        "keep": lambda q: axb(q, R("keep"), R("keepb"), LIFT / BIT, 0.0),
+        "mf": lambda q: ts(R("mf"), R("mli"), 2.0, OP.mult, offm, OP.add),
+        "uq": lambda q: quant("uq", R("ut")),
+        "uq2": lambda q: op("v", [uq2], [uqc, upk], lambda: g.vector.tensor_copy(
+            ap(uq2).bitcast(dt.uint32), ap(uqc).bitcast(dt.uint32).indirect(ap(upk)))),
+        "uq2s": lambda q: pick(q, R("uq2s"), R("uqs"), upk),
+        "vq": lambda q: quant("vq", R("vt")),
+        "own": lambda q: copy(q, odd("w%d" % (mid % NW), 0, H), R("cc", 0, H)),
+        "raw": lambda q: copy(q, odd("raw", 0, H), R("cc", 0, H)),
+        "far": lambda q: copy(q, odd("wa", H, C), R("cc", H, C)),
+    }
+    for b in range(4):
+        small["eq%d" % b] = lambda q, b=b: quant("eq", R("et", 3 - b, 515 - b), 128 * b, 128 * b + 128)
+        small["w%d" % b] = lambda q, b=b: copy(q, R("w%d" % b, H, H + 2 * C, 2), R("cc"))
 
     def step(s, name, q, b0, b1):
         xs, xn = "x%d" % (s - 1), "x%d" % s
@@ -480,152 +304,121 @@ def rank_program(g, core, T, topo):
             return R(x, 4 * c0, 4 * c1) if b is None else R(x, 4 * c0 + b, 4 * c1, 4)
 
         def bank(b):
-            n, a = banks[b, low]
-            return R("p%d" % n, c0 - a, c1 - a)
-
-        def product(b, l, r):
-            n = (b + (2 if low or c1 - c0 == C and l == "eq" else 6)) % 8
-            for half in range(low, 1 + (c1 > H)):
-                banks[b, half] = n, c0
-            mm(n, l, 128 * b, r, c0, c1)
-
-        def scores():
-            return R("p%d" % k, c0 - first[k], c1 - first[k])
+            return R("p%d" % (b + 4 * low), c0 - H * low, c1 - H * low)
 
         def row(j):
-            return R("w%d" % (j % 2), H + c0, H + c1) if j <= top else R("tr", (j - top - 1) * H + c0, (j - top - 1) * H + c1)
+            return odd("w%d" % (j % NW), H, C) if j <= top else R("tr", (j - top - 1) * H, (j - top) * H)
 
         def codes(j):
-            return R("w%d" % (j % 2), BASE)
+            return R("w%d" % (j % NW), H)
+
+        def mates(j):
+            return R("w%d" % (j % NW), 0, 2 * C)
 
         def lst(j):
-            return R("ls", 14 * j + b0, 14 * j + b1)
-
-        def slot(n, half, j):
-            return R(n, 70 * half + j, 70 * half + 70, 5)
+            return R("ls", 14 * j, 14 * j + 14)
 
         if kind == "P":
             if name == "Ptt":
-                ts(R("tt"), m, off, OP.is_ge, float(H), OP.mult)
-            elif name == "Psg":
-                axb(q, R("sg"), R("tt"), -2.0, float(H))
+                ts(R("tt"), m, off, OP.is_ge, float(C), OP.mult)
             elif name == "Pmf":
                 tt(R("mmf"), m, R("tt"), OP.subtract)
             elif name == "Pmm":
                 ts(R("mm"), R("mmf"), offm, OP.subtract)
             elif name == "Pos":
-                axb(q, R("os0"), R("sg"), ofb, offm)
+                axb(q, R("os0"), R("tt"), nofb, offq)
             elif name == "Pq":
-                tt(R("rr", 3, 140, 5), m, R("os0"), OP.subtract)
+                tt(term(1 + 3 * low), R(m[0], m[1] + b0 * m[3], m[1] + b1 * m[3] - m[3] + 1, m[3]), R("os0", b0, b1), OP.subtract)
+            elif name == "Psc":
+                copy(q, R("sel", 98, 196), R("sel", 0, 98))
             else:
-                tt(slot("rr", 1, 0), slot("rr", 1, 3), slot("rr", 0, 3), OP.subtract)
+                axb(q, slot(0, k), R("tt", 14 * (k > 1), 14 + 14 * (k > 1)), -2.0, float(C))
         elif kind == "T":
-            sw, mine = R("sw"), R("sc", C + 15, 672, 16)
-            if name[:3] == "Tsw":
-                tt(R("sw", c0 - H, c1 - H), R("sup", c0 - H, c1 - H), scores(), OP.is_gt)
+            if name == "Tsw":
+                tt(R("sw", 2 * (c0 - H), 2 * (c1 - H), 2), R("sup", c0 - H, c1 - H), bank(0), OP.is_gt)
             elif name == "Tso":
-                held(R("sc", C + c0, C + c1), R("sw", c0, c1), "keepb")
+                held(R("so"), R("sw", 0, C, 2), "keepb")
             elif name == "Tb":
-                pick(q, R("bb", c0, c1), sw, R("mm", b0, b1))
+                pick(q, R("bb", c0, c1), R("sw"), R("mm", b0, b1))
             elif name == "Th":
-                held(R("sc", c0, c1), R("bb", c0, c1), "keepb")
-            elif name == "Tc0":
-                axb(q, slot("sel", 0, 3), mine, -1.0, ofb1)
-            elif name == "Tc1":
-                axb(q, slot("sel", 1, 3), mine, 1.0, nofb)
-            elif name[1] == "r":
-                a = 0 if k == 2 else 14
-                tt(slot("rr", 1, k), R("sc", 16 * a + 15, 16 * a + H, 16), R("sg", a, a + 14), OP.mult)
+                held(R("sc", 48 * low, 48 * low + 7 * H, 7), R("bb", c0, c1), "keepb")
+            elif name in ("Tc0", "Tc2") and q == "a":
+                axb(q, slot(k // 2, 2), R("so", 15, H, 16), BIG * (k - 1), R("cb%d" % k))
+            elif name[1] == "c":
+                ts(slot(k // 2, 2 + 3 * (k % 2)), R("so", 15, H, 16), ofb, [OP.is_equal, OP.not_equal][k in (1, 2)],
+                   [BIG, SMALL][k % 2], [OP.mult, OP.max][k % 2])
             elif name != "Tn":
-                scan(R("nn", 70 * k, 70 * k + 70), R("sel", 70 * k, 70 * k + 70), R("rr", 70, 140), OP.mult, OP.add)
+                scan(R("nn", 98 * k, 98 * k + 98), R("sel", 98 * k, 98 * k + 98), R("sc", 105, 105 + 16 * 98, 16), OP.mult, OP.add)
             else:
-                vcopy(R("n16", b0, b1), R("nn", 4 + 5 * b0, 5 * b1, 5))
-                lower[s] = R("lc%d" % s) if low else R(land_b, 14, 28)
-                send(s, R(lower[s][0], 0, b1 - b0), R("n16", b0, b1), "bc"[low])
+                vcopy(R("n16"), R("nn", 5, 196, 7))
+                send(s, R(land_b), R("n16"), "b")
         elif name == "wa":
-            pick(q, R("wa", c0, c1), R("raw"), R("n16", 14 + b0, 14 + b1))
+            pick(q, odd("wa", c0, c1), R("raw"), R("n16", 14 + b0, 14 + b1))
         elif kind == "z":
             pick_tt(cols("zz", k), R("xp%d" % k), R("n16", b0, b1), cols(xs, k), OP.add)
         elif kind == "c":
             pick(q, cols("zz", k), R("xp%d" % k), R("n16", b0, b1))
-        elif name == "d":
-            tt(cols("zz"), cols("zz"), cols(xs), OP.add)
+        elif kind == "d":
+            tt(cols("zz", k), cols("zz", k), cols(xs, k), OP.add)
+        elif kind == "n":
+            pick_tt(cols(xn, k), R("bp%d" % k), R("m16", b0, b1), cols(xs, k), OP.add)
         elif kind == "g":
             pick(q, cols("ya", k), R("bp%d" % k), R("m16", b0, b1))
         elif kind == "h":
             tt(cols(xn, k), cols("ya", k), cols(xs, k), OP.add)
-        elif name == "dz":
-            o, i = cols("zz"), cols(xs)
-            dma("g", [o], [o, i], ap(o), ap(i), accum_op=OP.add)
         elif name == "qz":
             quant("qz", cols("zz"), c0, c1)
             for b in range(4):
-                product(b, "wq", "qz")
+                mm(b + 4 * low, "wq", 128 * b, "qz", c0, c1)
         elif name == "qa":
             quant("qa" if low else land_q, cols("aa"), c0, c1)
             if low:
                 send(s, R(land_q, c0, c1), R("qa", c0, c1), "q", True)
                 send(s, R(land_q + "s", c0, c1), R("qas", c0, c1), "s")
         elif kind == "a":
-            if q == "v":
-                ts(cols("aa", k), bank(k), 0.015625, OP.mult)
-            else:
-                act(cols("aa", k), bank(k), 0.015625)
-        elif kind == "e":
-            for b in (range(4) if name == "eb" else [k]):
-                product(b, "eq", land_q)
+            axb(q, cols("aa", k), bank(k), 0.015625, 0.0)
+        elif name == "eb":
+            for b in range(4):
+                mm(b + 4 * low, "eq", 128 * b, land_q, c0, c1)
         elif kind == "b":
             copy(q, R("bp%d" % k, c0, c1), bank(k))
         elif name == "p1":
-            pick(q, row(0), R("wa"), R(land_b, b0, b1))
+            pick(q, row(0), R("wa"), R(land_b, 0, 14))
         elif name == "o":
-            pick(q, row(top + 3), R("wa"), R(lower[s][0], lower[s][1] + b0, lower[s][1] + b1))
+            pick(q, row(top + 3), R("wa"), R(land_b, 14, 28))
         elif kind == "p":
             j = POWERS.index(int(name[1:]))
             pick(q, row(j), codes(j - 1), lst(POWERS.index(POWERS[j] - POWERS[j - 1])))
         elif kind in "sl":
             j = top + 1 + "tro".index(name[1]) if name[1] in "tro" else POWERS.index(int(name[1:]))
             if kind == "s":
-                held(R("sa", j * H + c0, j * H + c1), row(j), "keepm")
+                held(R("sa", j * H, j * H + H), row(j), "keep")
             else:
-                ts(lst(j), R("sa", j * H + c0 + 15, j * H + c1, 16), inv, OP.mult)
+                ts(lst(j), R("sa", j * H + 15, j * H + H, 16), offm, OP.subtract)
         elif name == "t":
-            pick(q, row(top + 1), R("w%d" % (top % 2), 0, C), R("n16", b0, b1))
+            pick(q, row(top + 1), mates(mid), R("n16", 0, 14))
+        elif name == "mv":
+            pick(q, odd("wa", 0, H), mates(mid), R("n16", 14, 28))
         elif name == "r":
-            pick(q, row(top + 2), codes(top), lst(top + 3))
-        elif kind == "f":
-            j = NUMBERS.index(int(name[1:]))
-            pick(q, R("f%d" % ((j + 1) % 2), H + c0, H + c1), R("f%d" % (j % 2), BASE),
-                 lst(POWERS.index(NUMBERS[j] - ([0] + NUMBERS)[j])))
-        elif name in ("mu", "mr", "mx", "my"):
-            half = name in ("mr", "my")
-            f = "f%d" % (([n + POWERS[-1] * (name in ("mu", "mr")) >= H // 2 for n in NUMBERS].index(True) + 1) % 2)
-            win, at = {"mu": (R(f, BASE), lst(top + 1)), "mr": (R(f, BASE), lst(top + 2)),
-                       "mx": (R(f, 0, C), R("n16", b0, b1)), "my": (R(f, BASE), lst(top + 3))}[name]
-            pick(q, R("mu", half * H + c0, half * H + c1), win, at)
+            pick(q, row(top + 2), *((R("wa"), R(land_b, 14, 28)) if END == "tv" else (codes(mid), lst(top + 3))))
+        elif name == "mu":
+            pick(q, R("mu", 0, H), *((codes(top), lst(top + 1)) if END else (mates(top), R("n16", 0, 14))))
+        elif name == "mr":
+            pick(q, R("mu", H, C), *((codes(top), lst(top + 2)) if END else (R("wa"), R(land_b, 14, 28))))
         elif name == "mo":
-            op("a", [R("mrow")], [R("mu")], lambda: g.scalar.activation(T.mrow[:, :], T.mu[:, :], COPY, bias=float(H)))
+            axb(q, R("mrow"), R("mu"), 0.5, float(H))
             dma("s", [], [R("mrow")], T.mo[:, :], T.mrow[0:128:16, :])
         elif name == "m":
             held(R("sm", c0, c1), R("mu", c0, c1), "keep")
         elif name == "ml":
-            ts(R("m16", b0, b1), R("sm", c0 + 15, c1, 16), offm, OP.subtract)
-        elif kind == "n":
-            pick_tt(cols(xn, k), R("bp%d" % k), R("m16", b0, b1), cols(xs, k), OP.add)
-        elif kind == "i":
-            pick(q, cols("ya", k), R("xp%d" % k), R("m16", b0, b1))
-        elif kind == "j":
-            tt(R("yb%d" % k, c0, c1), cols("ya", k), bank(k), OP.add)
-        elif kind == "k":
-            pick(q, cols(xn, k), R("yb%d" % k), R("m16", b0, b1))
+            ts(R("m16", b0, b1), R("sm", c0 + 15, c1, 16), 0.5, OP.mult, offh, OP.add)
         elif kind == "x":
-            copy(q, R("xp%d" % k, c0, c1), cols(xs, k))
+            copy(q, odd("xp%d" % k, c0, c1), cols(xs, k))
         elif kind == "u":
-            copy(q, R("sup", c0, c1), scores())
+            copy(q, R("sup", c0, c1), bank(0))
         elif kind == "q":
-            first[k] = c0
             quant("qx", cols(xs), c0, c1)
-            mm(k, "uq2", 0, "qx", c0, c1)
+            mm(4 * low, "uq2", 0, "qx", c0, c1)
         else:
             quant("qx", cols(xn), c0, c1)
             mm(k, "vq", 0, "qx", c0, c1)
@@ -641,12 +434,9 @@ def rank_program(g, core, T, topo):
             head, _, span = word.rstrip("'").partition("@")
             name, _, q = head.partition(".")
             if name[0] == "+":
-                once(name[1:], q or "a")
+                small[name[1:]](q or "a")
             else:
                 step(s + ahead, name, q or "a", *(SPANS[span] if span in SPANS else [int(n) for n in span.split("-")]))
 
     for sem in sorted(cnt, key=lambda k: nd[0] + int(k[1:]) if k[1:].isdigit() else 0):
         need("g", sem, cnt[sem])
-
-
-LOADS = [(0, 14), (14, 28)]

@@ -7,12 +7,11 @@ C, H = 448, 224
 ROUNDS = [1, 2, 3]
 F16, BF, F32, I32, U16, U8, MX = "float16", "bfloat16", "float32", "int32", "uint16", "uint8", "float8_e4m3fn_x4"
 LIFT, BIT = 1024.0, 2.0
-BIG = 2.0 ** -4
-SMALL = 1 / (BIG * C * C)
-POWERS = [1, 2, 3, 5, 8, 13, 21, 34, 55, 89]
-MID = 34
-END = "o"
-NW = 2
+SMALL = 2.0 ** -14
+BIG = round(2.0 ** 18 / (SMALL * C * C)) * 2.0 ** -18
+POWERS = [1, 2, 3, 5, 7, 12, 19, 31, 50, 81]
+RUNS = [0, 192, 320, C]
+MID = 31
 
 SCRATCH = {}
 
@@ -34,47 +33,51 @@ for _n, _w in (("uq", 128), ("uq2", 128), ("vq", 128), ("wq", 512), ("eq", 512),
 for _s in ROUNDS:
     _sb("lq%d" % _s, C, MX)
     _sb("lq%ds" % _s, C, U8)
-    _sb("lb%d" % _s, 28, U16)
-for _j in range(NW):
-    _sb("w%d" % _j, H + 2 * C, BF)
+    _sb("lb%d" % _s, 14, U16)
+    _sb("lc%d" % _s, 14, U16)
 for _n, _w, _d in (("ut", 512, BF), ("vt", 512, BF), ("mli", 28, I32), ("ones", 516, BF), ("et", 516, BF),
                    ("pi", 14, I32), ("pm", 14, I32), ("pmu", 14, U16), ("pf", 1, F32), ("pf1", 1, F32), ("off", 1, F32),
-                   ("offm", 1, F32), ("offq", 1, F32), ("offh", 1, F32), ("ofb", 1, F32), ("nofb", 1, F32), ("cb0", 1, F32), ("cb2", 1, F32),
+                   ("offm", 1, F32), ("offq", 1, F32), ("offh", 1, F32), ("ofb", 1, F32), ("nofb", 1, F32),
                    ("fi", 16, F32), ("ka", 16, F32), ("kb", 16, F32), ("k16", 16, BF), ("keep", H, BF), ("keepb", H, BF),
                    ("cc", C, BF), ("raw", 2 * C, BF), ("ui", 8, I32), ("up", 8, U16),
                    ("mm", 28, U16), ("mf", 28, F32), ("tt", 28, F32), ("os0", 28, F32), ("sel", 196, F32),
                    ("mmf", 28, F32), ("sup", H, F32), ("sw", C, BF), ("bb", C, BF), ("so", H, BF), ("sc", 1680, F16),
-                   ("sa", 16 * H, F16), ("tr", 3 * H, BF), ("mu", C, BF), ("sm", C, F16),
-                   ("nn", 196, F32), ("n16", 28, U16), ("m16", 28, U16), ("ls", 16 * 14, U16), ("wa", 2 * C, BF),
-                   ("mrow", C, F32), ("yo", C, F32)):
+                   ("sa", 13 * H, F16), ("tr", 3 * H, BF), ("mu", C, BF), ("sm", C, F16),
+                   ("nn", 196, F32), ("n16", 28, U16), ("m16", 28, U16), ("ls", 13 * 14, U16), ("wa", 2 * C, BF),
+                   ("w0", H + 2 * C, BF), ("w1", H + 2 * C, BF), ("mrow", C, F32), ("yo", C, F32)):
     _sb(_n, _w, _d)
 for _b in range(8):
     SCRATCH["p%d" % _b] = ("psum", [128, 512], "float32")
 
-SEMAPHORES = ["v", "a", "t", "gp"] + ["d%d" % i for i in range(28)]
+SEMAPHORES = ["v", "a", "t", "gp"] + ["d%d" % i for i in range(19)]
 for _s in ROUNDS:
-    for _k in ("b", "q", "s"):
+    for _k in ("b", "c", "q", "s"):
         SEMAPHORES += ["arr%s%d" % (_k, _s), "snt%s%d" % (_k, _s)]
 
 SPANS = {"u": (0, 14), "l": (14, 28), "w": (0, 28), "": (0, 14)}
-LOADS = [(0, 14), (14, 28)]
-BODY = """q@u u@u q@l Ptt Pmf Pos Pmm Pq@u Pq@l Ps1 Ps3 Ps4 Psc x0@u x1@u x2@u x3@u x0@l x1@l x2@l x3@l Tsw@l Tso Tb@l Tb@u Th@l Th@u
-Tc0 Tc1 Tc2 Tc3 Tn0 Tn1 Tn@w wa c0@l d0@l c1@l d1@l c2@l d2@l c3@l d3@l qz@l c0@u d0@u c1@u d1@u c2@u d2@u c3@u d3@u
-a0@l a1@l a2@l a3@l qa@l qz@u a0@u a1@u a2@u a3@u qa@u eb@u b0@u b1@u b2@u b3@u eb@l b0@l b1@l b2@l b3@l GLUE m@u m@l ml@u ml@l"""
-GLUE = " ".join("p%d" % n + " s%d l%d" % (n, n) * (n in [b - a for a, b in zip(POWERS, POWERS[1:])])
-                + " o so lo" * (n == 1 and END == "o") + {"tv": " t mv r st lt sr lr", "o": " t r st lt sr lr", "": ""}[END] * (n == MID)
-                for n in POWERS) + (" mu mr" if END else " mu mv mr")
-NEW = " g0@u h0@u g1@u h1@u g2@u h2@u g3@u h3@u g0@l h0@l g1@l h1@l g2@l h2@l g3@l h3@l"
-LAST = " mo g0@u h0@u g1@u h1@u g2@u h2@u g3@u h3@u" + "".join(
-    " g%d@%s h%d@%s" % (b, k, b, k) for k in ("14-20", "20-28") for b in range(4)) + " y0@0-12 y1@12-20 y2@20-28"
-ONCE = """+pi +fi +ui +cc +port +one +et +pm +sel0 +sc2 +sc5 +sc6 +pf +pmu +up +pf1 +off +ofb +ka +kb +offm +offq +offh +nofb +cb0 +cb2 +k16
-+keepb +keep +mf +uq +uq2 +uq2s +own +raw +far +eq0 +eq1 +eq2 +eq3 +vq """ + "".join("+w%d " % j for j in range(NW))
-ORDERS = [o.replace("GLUE", GLUE).split() for o in (ONCE + BODY + NEW, BODY + NEW, BODY + LAST)]
-ORDERS = [o.split() for o in """+pi +fi +sel0 +ui +pm +pf +off +pf1 +nofb +sc2 +offm +cc +ka +kb +pmu +sc5 +k16 +sc6 +cb0 +mf +up +offq Ptt +uq +far.v Pos.v +uq2 +keepb +ofb Ps4 Pq@l Ps1 +keep.v Pmf Ps3 +uq2s x2@u q@u Psc.v +port Pq@u Pmm q@l u.v@u x2.v@l x1@u +w0 +cb2.v Tsw@l x0.v@l x0@u Tso Tb.v@u Tb@l Tc0 x3@l Tc2.v +raw Tc1 Th@u Th@l Tc3 +w1 Tn0 Tn1 x3.v@u Tn@w x1.v@l c3@l c2@u z0@l z1@l z2@l +own c1@u +one d3@l d2@u +et qz@l wa z0@u z3@u d1@u p1.v a0@l s1 a1@l a2@l a3@l +offh.v l1 qa@l o p2.6 qz@u s2 p3.6 l2 +eq1 s3 p5.4 so l3 a1.v@u a2@u s5 p8.4 l5 lo +eq3 s8 a0@u p13.8 a3@u l8 +eq0 s13 p21.6 l13 qa@u p34.4 s21 +eq2 l21 eb@u s34 r.v l34 t p55 st eb@l b2@u sr lt p89.8 b3@u lr b1.v@u mr.v mu.4 b0@u m@l b0@l m@u b1@l b3.v@l b2@l ml@u g3@u Ptt' ml@l g1@u n0@u n0@l n3@l g1@l g2@l Pos' Ps4' n2@u h3@u h1@u h1@l x0@u' Ps1' h2@l Ps3' q@u'
+ORDERS = [o.split() for o in """+lm.s +pi +pm +lu +pf +fi +pmu +off +sc5 +sel0 +cc +pf1.v +offm +ka +ui +sc6 +one +kb +nofb.v +offq +mf +k16 Ptt +offh
++lx0.s +uq +w0 Ps1 +up Ps4 +et +ofb.v +uq2s Pos.v Ps3 +keepb Psc +uq2 q0@0-12 Pmf +lx1.s x3@u Pq@u u0@0-12 Pq@l q1@12-20 +lx2.s
+x0.v@u Pmm +far +lw.s +ls.s q2@20-28 x2.v@u +sc2 x2.v@l u1.v@12-14 x3@l Tsw1@14-20 Tsw2@20-28 x1.v@u Tb.v@u Tso Th@u Tc1 Tb@l
+Tc0 Th@l +port Tc2 Tc3 Tn0 Tn1 Tn@u x1@l Tn@l z2@u z3@l x0@l z0@l +raw +w1 c2@l c1@l c0@u d2@l d1@l c3@u +own +eq0 qz@l z1@u wa f1@l d0@u d3@u f3@l
++keep f2@l +eq1 a1@l qz@u f0@l p1.6 f2@u +eq3 a2@l s1 +eq2 a3@l l1 f0@u a0@l a2.v@u f1@u p2.8 qa@l a1@u f3@u s2 p3.6 l2 a3@u
+a0.v@u p5.8 qa@u s5 e2@u p7.6 e1@u l5 s7 p12.6 l7 o.6 s12 p19.8 e0@u b2@u l12 so p31.10 s19 b0@u lo s31 t l19 r.v p50.6 l31
+b1@u sr st e3@u p81.8 b3@u e2@l lr lt mr.v e3@l b3.v@l m@l e0@l e1@l mu m@u b1@l ml@l b0@l b2.v@l ml@u g3@l g2@u g1@u n1@l
+n3@u n0@u h2@u g0@l h1@u h3@l g2@l q@u' x3@u' x2@u' h0@l h2@l
 ----
-Pmf Pq@u q@l Pq@l u.v@u x3.v@l Pmm Tsw@l Psc x1@u x3.v@u Tso x2@l Tb.v@u x0@l Tc1 Tb@l Tc2 Tc3 Th@u Th@l Tc0 x2.v@u Tn0 Tn1 x1.v@l Tn@w c3@u z1@l z0@l c0@u wa z2@l z3@l d3@u c2@u qz@l c1@u d0@u p1 d2@u d1@u s1 l1 a0@l a2@l a1.v@l p2.8 qz@u a3@l s2 p3.4 l2 qa@l s3 o p5.10 l3 so s5 a2@u p8.6 a3@u l5 a0.v@u s8 p13.8 a1@u l8 lo s13 p21.8 l13 qa@u s21 p34.6 l21 t.v s34 r p55.6 l34 st eb@u b0@u sr p89.6 lt lr b3@u b2.v@u mr.v mu.4 b1@u m@l eb@l m@u b2.v@l ml@u ml@l b0@l b1@l Ptt' b3@l n0@u n1@l g2@l g0@l n1@u g2@u n3@u g3@l h2@l h0@l Ps4' Ps1' h2@u h3@l
+x1.v@l q@l Ptt x1@u x2.v@l x0.v@u Pmf x3.v@l Ps4.v u@u Pmm Tsw@l Ps1 Pos Pq@l Pq@u Tb.v@u Ps3 x0@l Tso Psc Tb@l Th@u Tc0
+Tc1 Th@l Tc3 Tc2 Tn0 Tn1 Tn@u Tn@l z3@u c0@l z2@l c1@l z3@l d0@l c2@u wa p1 d1@l z1@u qz@l f0@l d2@u o z0@u f1@l f2@l
+a0@l s1 l1 qz@u f3@l p2.8 f3@u a1@l so s2 p3.6 l2 a2@l a3.v@l p5.6 qa@l f0@u a0@u s5 p7.8 f2@u a3@u l5 s7 p12.8 l7 s12 f1@u
+a1@u p19.8 l12 lo a2@u s19 p31.4 r qa@u e0@u l19 e1@u s31 e2@u t.v p50.6 l31 b0@u st sr p81.8 lt lr b2.v@u e3@u mu.v b3@u e3@l
+b1.v@u m@u b3.v@l ml@u mr e2@l m@l b2@l n3@u ml@l e1@l e0@l b1@l b0@l n1@u g2@u n1@l g0@u h2@u g2@l h0@u n3@l h2@l g0@l x1@u'
+x0@u' h0@l q@u'
 ----
-Pos x1@l q@u Ps3 Pq@u q@l Pmf u.v@u Pmm x3@l Pq@l Tsw@l x2.v@l x0@u Psc Tb@u Tso Tb.v@l Tc0.v Tc2 Tc3 Th@l Th@u x3@u Tc1 Tn1 Tn0 Tn@w x1.v@u x2@u z2@l z1@l x0@l z0@l c3@l wa c2@u c0@u d3@l z3@u c1@u qz@l d2@u p1 d0@u a0@l d1@u s1 a1@l l1 +vq a2@l a3@l p2.v qz@u s2 p3.6 l2 qa@l o s3 p5.6 a0@u l3 s5 p8.8 l5 s8 a1@u p13.8 l8 so a3@u s13 p21.10 a2@u l13 lo s21 p34.6 qa@u eb@u l21 s34 r t.v p55 l34 st sr b0.v@u lt eb@l lr p89.6 b2.v@u mu.v b1@u b3@u mr.4 m@u b1.v@l b0@l b2@l b3@l ml@u mo m@l n1@u ml@l g2@20-28 g1@20-28 n0@u n2@u n3@u g0.2@14-20 g3@14-20 g0@20-28 g3@20-28 y0@0-12 n2@14-20 h0@14-20 n1@14-20 h3@14-20 y1@12-20 h0@20-28 h2@20-28 h3@20-28 h1@20-28 y2@20-28""".split("----")]
+x3@l x2@u q@l x0@l Ptt Ps1 x2.v@l x1.v@l Pmf u.v@u Pmm Pos Ps3.v Tsw@l Pq@u Pq@l Ps4 x3@u Tb.v@u Psc Tso Th@u Tc1 Tc0 Tb@l
+Th@l Tc3 Tc2 Tn0 Tn1 Tn@u Tn@l c2@u z3@l z2@l z0@l c1@l d1@l d2@u qz@l f3@l f2@l f0@l +vt c3@u wa d3@u f1@l z0@u c1@u d1@u
+p1 s1 l1 a3@l qz@u a2@l p2.8 a0.v@l a1@l s2 p3.4 l2 qa@l f3@u a3@u p5.10 o.4 s5 p7.6 l5 f0@u so s7 f2@u a2@u p12.6 f1@u a1@u l7
++vq s12 p19.8 l12 a0@u lo s19 p31.8 qa@u t l19 s31 e0@u e2@u e1@u e3@u e0@l r.v l31 st sr e3@l lt p50 p81.v e1@l b0@u lr b2@u
+mu.v m@u b0.v@l ml@u b1@u mr b3@u b3@l m@l b1@l e2@l n0@u b2@l g1@u ml@l g2@14-20 n3@u n2@u g0@14-20 h1@u g1@14-20 n3@14-20
+Q0@0-12 Sc.s@0-12 h2@14-20 h0@14-20 h1@14-20 mo g3@20-28 Sm.s g1@20-28 n2@20-28 Q1@12-20 Sc.s@12-20 n0@20-28 y0@0-12 Sy@0-12
+h3@20-28 h1@20-28 y1@12-20 Q2@20-28 Sy@12-20 Sc.s@20-28 Ss3@w Ss0@w Ss1.s@w Ss2@w y2.v@20-28 Sy@20-28""".split("----")]
 
 
 def rank_program(g, core, T, topo):
@@ -171,11 +174,11 @@ def rank_program(g, core, T, topo):
     def held(out, x, keep):
         scan(out, R(keep), x, OP.add, OP.max)
 
-    def act(out, x, scale=1.0):
-        op("a", [out], [x], lambda: g.scalar.activation(ap(out), ap(x), COPY, scale=scale))
-
     def copy(q, out, x):
-        (act if q == "a" else vcopy)(out, x)
+        if q == "a":
+            op("a", [out], [x], lambda: g.scalar.activation(ap(out), ap(x), COPY, scale=1.0))
+        else:
+            vcopy(out, x)
 
     def pick(q, out, win, off):
         if q == "a":
@@ -199,10 +202,10 @@ def rank_program(g, core, T, topo):
 
     nd = [0]
 
-    def dma(q, writes, reads, out, in_, **how):
+    def dma(q, writes, reads, out, in_):
         sem = "d%d" % nd[0]
         nd[0] += 1
-        op(q, writes, reads, lambda: Q[q].dma_start(out, in_, **how), sem, 16)
+        op(q, writes, reads, lambda: Q[q].dma_start(out, in_), sem, 16)
 
     def lanes(src, dst):
         return topo.engines(src, dst)[:8]
@@ -217,19 +220,11 @@ def rank_program(g, core, T, topo):
         o, i = ap(land), ap(src)
         if codes:
             o, i = o.bitcast(dt.uint8), i.bitcast(dt.uint8)
-        ins = g.remote_dma(out_ap=o, in_ap=i, remote_sem=T.sem["arr%s%d" % (k, s)], local_sem=T.sem["snt%s%d" % (k, s)],
-                           pid=pid, routing_id=rid, dma_engine_mask=sum(1 << j for j in e))
+        g.remote_dma(out_ap=o, in_ap=i, remote_sem=T.sem["arr%s%d" % (k, s)], local_sem=T.sem["snt%s%d" % (k, s)],
+                     pid=pid, routing_id=rid, dma_engine_mask=sum(1 << j for j in e))
         sem = "snt%s%d" % (k, s)
         cnt[sem] = len(e)
         note("g", [src], [], (sem, len(e)))
-
-    dma("a", [R("mli")], [], T.mli[:, :], T.ml[:, :])
-    dma("s", [R("ut")], [], T.ut[:, :], T.u[:, :])
-    for a, b in LOADS:
-        dma("s", [R("x0", 64 * a, 64 * b)], [], T.x0[:, 64 * a:64 * b], T.x[:, 64 * a:64 * b])
-    dma("s", [R("wq")], [R("x0")], T.wq[:, :].bitcast(dt.uint8), T.wc[:, :])
-    dma("s", [R("wqs")], [], T.wqs[:, :], T.ws[:, :])
-    dma("s", [R("vt")], [], T.vt[:, :], T.v[:, :])
 
     def iota(r, pattern, base, cm):
         f = SCRATCH[r[0]][2] != I32
@@ -247,15 +242,19 @@ def rank_program(g, core, T, topo):
 
     pf, pf1, off, offm, offq, offh, ofb, nofb = [R(n) for n in "pf pf1 off offm offq offh ofb nofb".split()]
     upk, uqc, uq2, e, one = R("up"), R("uq"), R("uq2"), R("et"), R("ones")
-    top = len(POWERS) - 1
-    mid = POWERS.index(MID) if END else top
+    top, mid = len(POWERS) - 1, POWERS.index(MID)
     small = {
+        "lm": lambda q: dma(q, [R("mli")], [], T.mli[:, :], T.ml[:, :]),
+        "lu": lambda q: dma(q, [R("ut")], [], T.ut[:, :], T.u[:, :]),
+        "lw": lambda q: dma(q, [R("wq")], [R("x0")], T.wq[:, :].bitcast(dt.uint8), T.wc[:, :]),
+        "ls": lambda q: dma(q, [R("wqs")], [R("x0")], T.wqs[:, :], T.ws[:, :]),
+        "vt": lambda q: dma("s", [R("vt")], [R("lb1")], T.vt[:, :], T.v[:, :]),
         "pi": lambda q: iota(R("pi"), [[0, 14]], 0, 1),
         "fi": lambda q: iota(R("fi"), [[1, 16]], 0, 0),
         "ui": lambda q: iota(R("ui"), [[16, 8]], 0, 0),
         "cc": lambda q: iota(R("cc"), [[2, C]], -C, 0),
         "port": lambda q: iota(odd("raw", H, C), [[2, H]], 1 - H, 0),
-        "one": lambda q: fill(one, 1.0) if q == "v" else iota(one, [[0, 516]], 1, 0),
+        "one": lambda q: iota(one, [[0, 516]], 1, 0),
         "et": lambda q: op("g", [e], [one], lambda: g.affine_select(ap(e), ap(one), [[-1, 516]], OP.is_equal, 0.0, 3, 4)),
         "pm": lambda q: ts(R("pm"), R("pi"), 15, OP.bitwise_and),
         "sel0": lambda q: fill(R("sel", 0, 98), 0.0),
@@ -274,8 +273,6 @@ def rank_program(g, core, T, topo):
         "offq": lambda q: axb(q, offq, off, 1.0 + C * BIT / LIFT, -float(C + 1)),
         "offh": lambda q: axb(q, offh, off, -0.5, float(H)),
         "nofb": lambda q: axb(q, nofb, off, -2 * BIT / LIFT, 0.0),
-        "cb0": lambda q: axb(q, R("cb0"), off, BIG * BIT / LIFT, BIG),
-        "cb2": lambda q: axb(q, R("cb2"), off, -BIG * BIT / LIFT, 0.0),
         "k16": lambda q: tt(R("k16"), R("ka"), R("kb"), OP.add),
         "keepb": lambda q: pick(q, R("keepb"), R("k16"), R("pmu")),
         "keep": lambda q: axb(q, R("keep"), R("keepb"), LIFT / BIT, 0.0),
@@ -285,17 +282,20 @@ def rank_program(g, core, T, topo):
             ap(uq2).bitcast(dt.uint32), ap(uqc).bitcast(dt.uint32).indirect(ap(upk)))),
         "uq2s": lambda q: pick(q, R("uq2s"), R("uqs"), upk),
         "vq": lambda q: quant("vq", R("vt")),
-        "own": lambda q: copy(q, odd("w%d" % (mid % NW), 0, H), R("cc", 0, H)),
+        "own": lambda q: copy(q, odd("w%d" % (mid % 2), 0, H), R("cc", 0, H)),
         "raw": lambda q: copy(q, odd("raw", 0, H), R("cc", 0, H)),
         "far": lambda q: copy(q, odd("wa", H, C), R("cc", H, C)),
     }
     for b in range(4):
         small["eq%d" % b] = lambda q, b=b: quant("eq", R("et", 3 - b, 515 - b), 128 * b, 128 * b + 128)
+    for b in range(3):
+        small["lx%d" % b] = lambda q, a=4 * RUNS[b], z=4 * RUNS[b + 1]: dma(q, [R("x0", a, z)], [], T.x0[:, a:z], T.x[:, a:z])
+    for b in range(2):
         small["w%d" % b] = lambda q, b=b: copy(q, R("w%d" % b, H, H + 2 * C, 2), R("cc"))
 
     def step(s, name, q, b0, b1):
         xs, xn = "x%d" % (s - 1), "x%d" % s
-        land_b, land_q = "lb%d" % s, "lq%d" % s
+        land_b, land_c, land_q = "lb%d" % s, "lc%d" % s, "lq%d" % s
         c0, c1, low = 16 * b0, 16 * b1, int(b0 >= 14)
         kind, k = name[0], int(name[-1]) if name[-1].isdigit() else 0
         m = R("mf") if s == 1 else R("sm", 15, C, 16)
@@ -306,14 +306,14 @@ def rank_program(g, core, T, topo):
         def bank(b):
             return R("p%d" % (b + 4 * low), c0 - H * low, c1 - H * low)
 
+        def scores():
+            return R("p%d" % k, c0 - RUNS[k], c1 - RUNS[k]) if name[-1].isdigit() else bank(0)
+
         def row(j):
-            return odd("w%d" % (j % NW), H, C) if j <= top else R("tr", (j - top - 1) * H, (j - top) * H)
+            return odd("w%d" % (j % 2), H, C) if j <= top else R("tr", (j - top - 1) * H, (j - top) * H)
 
         def codes(j):
-            return R("w%d" % (j % NW), H)
-
-        def mates(j):
-            return R("w%d" % (j % NW), 0, 2 * C)
+            return R("w%d" % (j % 2), H)
 
         def lst(j):
             return R("ls", 14 * j, 14 * j + 14)
@@ -334,26 +334,25 @@ def rank_program(g, core, T, topo):
             else:
                 axb(q, slot(0, k), R("tt", 14 * (k > 1), 14 + 14 * (k > 1)), -2.0, float(C))
         elif kind == "T":
-            if name == "Tsw":
-                tt(R("sw", 2 * (c0 - H), 2 * (c1 - H), 2), R("sup", c0 - H, c1 - H), bank(0), OP.is_gt)
+            mine = R("so", 15, H, 16)
+            if name[:3] == "Tsw":
+                tt(R("sw", 2 * (c0 - H), 2 * (c1 - H), 2), R("sup", c0 - H, c1 - H), scores(), OP.is_gt)
             elif name == "Tso":
                 held(R("so"), R("sw", 0, C, 2), "keepb")
             elif name == "Tb":
                 pick(q, R("bb", c0, c1), R("sw"), R("mm", b0, b1))
             elif name == "Th":
                 held(R("sc", 48 * low, 48 * low + 7 * H, 7), R("bb", c0, c1), "keepb")
-            elif name in ("Tc0", "Tc2") and q == "a":
-                axb(q, slot(k // 2, 2), R("so", 15, H, 16), BIG * (k - 1), R("cb%d" % k))
             elif name[1] == "c":
-                ts(slot(k // 2, 2 + 3 * (k % 2)), R("so", 15, H, 16), ofb, [OP.is_equal, OP.not_equal][k in (1, 2)],
+                ts(slot(k // 2, 2 + 3 * (k % 2)), mine, ofb, [OP.is_equal, OP.not_equal][k in (1, 2)],
                    [BIG, SMALL][k % 2], [OP.mult, OP.max][k % 2])
             elif name != "Tn":
                 scan(R("nn", 98 * k, 98 * k + 98), R("sel", 98 * k, 98 * k + 98), R("sc", 105, 105 + 16 * 98, 16), OP.mult, OP.add)
             else:
-                vcopy(R("n16"), R("nn", 5, 196, 7))
-                send(s, R(land_b), R("n16"), "b")
+                vcopy(R("n16", b0, b1), R("nn", 5 + 7 * b0, 7 * b1, 7))
+                send(s, R(land_c if low else land_b), R("n16", b0, b1), "bc"[low])
         elif name == "wa":
-            pick(q, odd("wa", c0, c1), R("raw"), R("n16", 14 + b0, 14 + b1))
+            pick(q, odd("wa", 0, H), R("raw"), R("n16", 14, 28))
         elif kind == "z":
             pick_tt(cols("zz", k), R("xp%d" % k), R("n16", b0, b1), cols(xs, k), OP.add)
         elif kind == "c":
@@ -368,8 +367,8 @@ def rank_program(g, core, T, topo):
             tt(cols(xn, k), cols("ya", k), cols(xs, k), OP.add)
         elif name == "qz":
             quant("qz", cols("zz"), c0, c1)
-            for b in range(4):
-                mm(b + 4 * low, "wq", 128 * b, "qz", c0, c1)
+        elif kind == "f":
+            mm(k + 4 * low, "wq", 128 * k, "qz", c0, c1)
         elif name == "qa":
             quant("qa" if low else land_q, cols("aa"), c0, c1)
             if low:
@@ -377,15 +376,14 @@ def rank_program(g, core, T, topo):
                 send(s, R(land_q + "s", c0, c1), R("qas", c0, c1), "s")
         elif kind == "a":
             axb(q, cols("aa", k), bank(k), 0.015625, 0.0)
-        elif name == "eb":
-            for b in range(4):
-                mm(b + 4 * low, "eq", 128 * b, land_q, c0, c1)
+        elif kind == "e":
+            mm(k + 4 * low, "eq", 128 * k, land_q, c0, c1)
         elif kind == "b":
             copy(q, R("bp%d" % k, c0, c1), bank(k))
         elif name == "p1":
-            pick(q, row(0), R("wa"), R(land_b, 0, 14))
+            pick(q, row(0), R("wa"), R(land_b))
         elif name == "o":
-            pick(q, row(top + 3), R("wa"), R(land_b, 14, 28))
+            pick(q, row(top + 3), R("wa"), R(land_c))
         elif kind == "p":
             j = POWERS.index(int(name[1:]))
             pick(q, row(j), codes(j - 1), lst(POWERS.index(POWERS[j] - POWERS[j - 1])))
@@ -396,18 +394,15 @@ def rank_program(g, core, T, topo):
             else:
                 ts(lst(j), R("sa", j * H + 15, j * H + H, 16), offm, OP.subtract)
         elif name == "t":
-            pick(q, row(top + 1), mates(mid), R("n16", 0, 14))
-        elif name == "mv":
-            pick(q, odd("wa", 0, H), mates(mid), R("n16", 14, 28))
+            pick(q, row(top + 1), R("w%d" % (mid % 2), 0, 2 * C), R("n16", 0, 14))
         elif name == "r":
-            pick(q, row(top + 2), *((R("wa"), R(land_b, 14, 28)) if END == "tv" else (codes(mid), lst(top + 3))))
+            pick(q, row(top + 2), codes(mid), lst(top + 3))
         elif name == "mu":
-            pick(q, R("mu", 0, H), *((codes(top), lst(top + 1)) if END else (mates(top), R("n16", 0, 14))))
+            pick(q, R("mu", 0, H), codes(top), lst(top + 1))
         elif name == "mr":
-            pick(q, R("mu", H, C), *((codes(top), lst(top + 2)) if END else (R("wa"), R(land_b, 14, 28))))
+            pick(q, R("mu", H, C), codes(top), lst(top + 2))
         elif name == "mo":
             axb(q, R("mrow"), R("mu"), 0.5, float(H))
-            dma("s", [], [R("mrow")], T.mo[:, :], T.mrow[0:128:16, :])
         elif name == "m":
             held(R("sm", c0, c1), R("mu", c0, c1), "keep")
         elif name == "ml":
@@ -415,18 +410,23 @@ def rank_program(g, core, T, topo):
         elif kind == "x":
             copy(q, odd("xp%d" % k, c0, c1), cols(xs, k))
         elif kind == "u":
-            copy(q, R("sup", c0, c1), bank(0))
+            copy(q, R("sup", c0, c1), scores())
         elif kind == "q":
             quant("qx", cols(xs), c0, c1)
-            mm(4 * low, "uq2", 0, "qx", c0, c1)
-        else:
+            mm(4 * low if name == "q" else k, "uq2", 0, "qx", c0, c1)
+        elif kind == "Q":
             quant("qx", cols(xn), c0, c1)
             mm(k, "vq", 0, "qx", c0, c1)
-            for j in range(4 * (c1 == C)):
-                dma("sa"[j % 2], [], [R("qxs")], T.osc[4 * j:4 * j + 4, :], T.qxs[32 * j:32 * j + 4, :])
-            dma("s", [], [R("qx", c0, c1)], T.oc[:, 4 * c0:4 * c1], T.qx[:, c0:c1].bitcast(dt.uint8))
+        elif kind == "y":
             copy(q, R("yo", c0, c1), R("p%d" % k, 0, c1 - c0))
-            dma("a", [], [R("yo", c0, c1)], T.y[:, c0:c1], T.yo[:, c0:c1])
+        elif name == "Sm":
+            dma(q, [], [R("mrow")], T.mo[:, :], T.mrow[0:128:16, :])
+        elif name == "Sc":
+            dma(q, [], [R("qx", c0, c1)], T.oc[:, 4 * c0:4 * c1], T.qx[:, c0:c1].bitcast(dt.uint8))
+        elif name == "Sy":
+            dma(q, [], [R("yo", c0, c1)], T.y[:, c0:c1], T.yo[:, c0:c1])
+        else:
+            dma(q, [], [R("qxs")], T.osc[4 * k:4 * k + 4, :], T.qxs[32 * k:32 * k + 4, :])
 
     for s, order in zip(ROUNDS, ORDERS):
         for word in order:

import math
from concourse.mybir import dt, AluOpType, ActivationFunctionType

OP = AluOpType
COPY, SAME = ActivationFunctionType.Copy, ActivationFunctionType.Identity
C, H = 448, 224
ROUNDS = [1, 2, 3]
F16, BF, F32, I32, U16, U8, MX = "float16", "bfloat16", "float32", "int32", "uint16", "uint8", "float8_e4m3fn_x4"
LIFT, BIT = 1024.0, 2.0
SMALL = 2.0 ** -14
BIG = round(2.0 ** 18 / (SMALL * C * C)) * 2.0 ** -18
POWERS = [1, 2, 3, 5, 7, 12, 19, 31, 50, 81]
RUNS = [0, 192, 320, C]
MID = 31

SCRATCH = {}


def _sb(name, n, d):
    SCRATCH[name] = ("sbuf", [128, n], d)


for _r in range(4):
    _sb("x%d" % _r, 4 * C, BF)
for _b in range(4):
    _sb("xp%d" % _b, 2 * C, BF)
    _sb("bp%d" % _b, C, BF)
for _n in ("zz", "aa", "ya"):
    _sb(_n, 4 * C, BF)
for _n, _w in (("uq", 128), ("uq2", 128), ("vq", 128), ("wq", 512), ("eq", 512), ("qx", C), ("qz", C), ("qa", C)):
    _sb(_n, _w, MX)
    _sb(_n + "s", _w, U8)
for _s in ROUNDS:
    _sb("lq%d" % _s, C, MX)
    _sb("lq%ds" % _s, C, U8)
    _sb("lb%d" % _s, 14, U16)
    _sb("lc%d" % _s, 14, U16)
for _n, _w, _d in (("ut", 512, BF), ("vt", 512, BF), ("mli", 28, I32), ("ones", 516, BF), ("et", 516, BF),
                   ("pi", 14, I32), ("pm", 14, I32), ("pmu", 14, U16), ("pf", 1, F32), ("pf1", 1, F32), ("off", 1, F32),
                   ("offm", 1, F32), ("offq", 1, F32), ("offh", 1, F32), ("ofb", 1, F32), ("nofb", 1, F32),
                   ("fi", 16, F32), ("ka", 16, F32), ("kb", 16, F32), ("k16", 16, BF), ("keep", H, BF), ("keepb", H, BF),
                   ("cc", C, BF), ("raw", 2 * C, BF), ("ui", 8, I32), ("up", 8, U16),
                   ("mm", 28, U16), ("mf", 28, F32), ("tt", 28, F32), ("os0", 28, F32), ("sel", 196, F32),
                   ("mmf", 28, F32), ("sup", H, F32), ("sw", C, BF), ("bb", C, BF), ("so", H, BF), ("sc", 1680, F16),
                   ("sa", 13 * H, F16), ("tr", 3 * H, BF), ("mu", C, BF), ("sm", C, F16),
                   ("nn", 196, F32), ("n16", 28, U16), ("m16", 28, U16), ("ls", 13 * 14, U16), ("wa", 2 * C, BF),
                   ("w0", H + 2 * C, BF), ("w1", H + 2 * C, BF), ("mrow", C, F32), ("yo", C, F32)):
    _sb(_n, _w, _d)
for _b in range(8):
    SCRATCH["p%d" % _b] = ("psum", [128, 512], "float32")

SEMAPHORES = ["v", "a", "t", "gp"] + ["d%d" % i for i in range(19)]
for _s in ROUNDS:
    for _k in ("b", "c", "q", "s"):
        SEMAPHORES += ["arr%s%d" % (_k, _s), "snt%s%d" % (_k, _s)]

SPANS = {"u": (0, 14), "l": (14, 28), "w": (0, 28), "": (0, 14)}
ORDERS = [o.split() for o in """+lm.s +pi +pm +lu +pf +fi +pmu +off +sc5 +sel0 +cc +pf1.v +offm +ka +ui +sc6 +one +kb +nofb.v +offq +mf +k16 Ptt +offh
+lx0.s +uq +w0 Ps1 +up Ps4 +et +ofb.v +uq2s Pos.v Ps3 +keepb Psc +uq2 q0@0-12 Pmf +lx1.s x3@u Pq@u u0@0-12 Pq@l q1@12-20 +lx2.s
x0.v@u Pmm +far +lw.s +ls.s q2@20-28 x2.v@u +sc2 x2.v@l u1.v@12-14 x3@l Tsw1@14-20 Tsw2@20-28 x1.v@u Tb.v@u Tso Th@u Tc1 Tb@l
Tc0 Th@l +port Tc2 Tc3 Tn0 Tn1 Tn@u x1@l Tn@l z2@u z3@l x0@l z0@l +raw +w1 c2@l c1@l c0@u d2@l d1@l c3@u +own +eq0 qz@l z1@u wa f1@l d0@u d3@u f3@l
+keep f2@l +eq1 a1@l qz@u f0@l p1.6 f2@u +eq3 a2@l s1 +eq2 a3@l l1 f0@u a0@l a2.v@u f1@u p2.8 qa@l a1@u f3@u s2 p3.6 l2 a3@u
a0.v@u p5.8 qa@u s5 e2@u p7.6 e1@u l5 s7 p12.6 l7 o.6 s12 p19.8 e0@u b2@u l12 so p31.10 s19 b0@u lo s31 t l19 r.v p50.6 l31
b1@u sr st e3@u p81.8 b3@u e2@l lr lt mr.v e3@l b3.v@l m@l e0@l e1@l mu m@u b1@l ml@l b0@l b2.v@l ml@u g3@l g2@u g1@u n1@l
n3@u n0@u h2@u g0@l h1@u h3@l g2@l q@u' x3@u' x2@u' h0@l h2@l
----
x1.v@l q@l Ptt x1@u x2.v@l x0.v@u Pmf x3.v@l Ps4.v u@u Pmm Tsw@l Ps1 Pos Pq@l Pq@u Tb.v@u Ps3 x0@l Tso Psc Tb@l Th@u Tc0
Tc1 Th@l Tc3 Tc2 Tn0 Tn1 Tn@u Tn@l z3@u c0@l z2@l c1@l z3@l d0@l c2@u wa p1 d1@l z1@u qz@l f0@l d2@u o z0@u f1@l f2@l
a0@l s1 l1 qz@u f3@l p2.8 f3@u a1@l so s2 p3.6 l2 a2@l a3.v@l p5.6 qa@l f0@u a0@u s5 p7.8 f2@u a3@u l5 s7 p12.8 l7 s12 f1@u
a1@u p19.8 l12 lo a2@u s19 p31.4 r qa@u e0@u l19 e1@u s31 e2@u t.v p50.6 l31 b0@u st sr p81.8 lt lr b2.v@u e3@u mu.v b3@u e3@l
b1.v@u m@u b3.v@l ml@u mr e2@l m@l b2@l n3@u ml@l e1@l e0@l b1@l b0@l n1@u g2@u n1@l g0@u h2@u g2@l h0@u n3@l h2@l g0@l x1@u'
x0@u' h0@l q@u'
----
x3@l x2@u q@l x0@l Ptt Ps1 x2.v@l x1.v@l Pmf u.v@u Pmm Pos Ps3.v Tsw@l Pq@u Pq@l Ps4 x3@u Tb.v@u Psc Tso Th@u Tc1 Tc0 Tb@l
Th@l Tc3 Tc2 Tn0 Tn1 Tn@u Tn@l c2@u z3@l z2@l z0@l c1@l d1@l d2@u qz@l f3@l f2@l f0@l +vt c3@u wa d3@u f1@l z0@u c1@u d1@u
p1 s1 l1 a3@l qz@u a2@l p2.8 a0.v@l a1@l s2 p3.4 l2 qa@l f3@u a3@u p5.10 o.4 s5 p7.6 l5 f0@u so s7 f2@u a2@u p12.6 f1@u a1@u l7
+vq s12 p19.8 l12 a0@u lo s19 p31.8 qa@u t l19 s31 e0@u e2@u e1@u e3@u e0@l r.v l31 st sr e3@l lt p50 p81.v e1@l b0@u lr b2@u
mu.v m@u b0.v@l ml@u b1@u mr b3@u b3@l m@l b1@l e2@l n0@u b2@l g1@u ml@l g2@14-20 n3@u n2@u g0@14-20 h1@u g1@14-20 n3@14-20
Q0@0-12 Sc.s@0-12 h2@14-20 h0@14-20 h1@14-20 mo g3@20-28 Sm.s g1@20-28 n2@20-28 Q1@12-20 Sc.s@12-20 n0@20-28 y0@0-12 Sy@0-12
h3@20-28 h1@20-28 y1@12-20 Q2@20-28 Sy@12-20 Sc.s@20-28 Ss3@w Ss0@w Ss1.s@w Ss2@w y2.v@20-28 Sy@20-28""".split("----")]


def rank_program(g, core, T, topo):
    rank = T.rank_of(core)
    if rank is None:
        return
    Q = {"v": g.vector, "a": g.scalar, "t": g.tensor, "g": g, "s": g.sync}
    OWN = {"v": "v", "a": "a", "t": "t", "g": "gp"}
    cnt, seen, snap, hist = {}, {q: {} for q in Q}, {}, {}
    tick = [0]

    def need(q, sem, val):
        if seen[q].get(sem, 0) >= val:
            return
        Q[q].wait_ge(T.sem[sem], val)
        for k, w in snap.get((sem, val), {}).items():
            if seen[q].get(k, 0) < w:
                seen[q][k] = w
        seen[q][sem] = val

    def meets(x, y):
        (a, b, s), (c, d, t) = x, y
        if a >= d or c >= b:
            return False
        return not (a - c) % math.gcd(s, t)

    def hazards(q, reads, writes):
        tok = []
        for kind, regs in ((0, reads), (1, writes)):
            for n, a, b, s in regs:
                ps = SCRATCH.get(n, ("",))[0] == "psum"
                for reg, k, token, at, eng in hist.get(n, []):
                    if ps and eng != q or (k or kind) and meets(reg, (a, b, s)):
                        tok.append((at, token))
        for at, (sem, val) in sorted(set(tok), reverse=True):
            need(q, sem, val)

    def note(q, reads, writes, token):
        tick[0] += 1
        for kind, regs in ((0, reads), (1, writes)):
            for n, a, b, s in regs:
                h = hist.setdefault(n, [])
                if kind and s == 1:
                    h[:] = [e for e in h if not (e[0][0] >= a and e[0][1] <= b)]
                h.append(((a, b, s), kind, token, tick[0], q))

    def op(q, writes, reads, call, sem=None, inc=1):
        hazards(q, reads, writes)
        sem = sem or OWN[q]
        ins = call()
        ins.then_inc(T.sem[sem], inc)
        cnt[sem] = cnt.get(sem, 0) + inc
        snap[(sem, cnt[sem])] = dict(seen[q])
        note(q, reads, writes, (sem, cnt[sem]))

    def R(n, a=0, b=None, s=1):
        return (n, a, T[n].shape[1] if b is None else b, s)

    def ap(r):
        if not isinstance(r, tuple):
            return r
        return T[r[0]][:, r[1]:r[2]] if r[3] == 1 else T[r[0]][:, r[1]:r[2]:r[3]]

    def tt(out, x, y, o):
        op("v", [out], [x, y], lambda: g.vector.tensor_tensor(ap(out), ap(x), ap(y), o))

    def ts(out, x, s1, o1, s2=None, o2=None):
        reads = [x] + [c for c in (s1, s2) if isinstance(c, tuple)]
        if o2 is None:
            op("v", [out], reads, lambda: g.vector.tensor_scalar(ap(out), ap(x), ap(s1), None, o1))
        else:
            op("v", [out], reads, lambda: g.vector.tensor_scalar(ap(out), ap(x), ap(s1), ap(s2), o1, o2))

    def axb(q, out, x, a, b):
        if q == "v":
            ts(out, x, a, OP.mult, b, OP.add)
        else:
            reads = [x] + [c for c in (a, b) if isinstance(c, tuple)]
            f = SAME if isinstance(b, tuple) else COPY
            op("a", [out], reads, lambda: g.scalar.activation(ap(out), ap(x), f, bias=ap(b), scale=ap(a)))

    def vcopy(out, x):
        op("v", [out], [x], lambda: g.vector.tensor_copy(ap(out), ap(x)))

    def fill(out, c):
        op("v", [out], [], lambda: g.vector.memset(ap(out), c))

    def pick_tt(out, win, off, y, o):
        op("v", [out], [win, off, y], lambda: g.vector.tensor_tensor(ap(out), ap(win).indirect(ap(off)), ap(y), o))

    def scan(out, d0, d1, o0, o1):
        op("v", [out], [d0, d1], lambda: g.vector.tensor_tensor_scan(ap(out), ap(d0), ap(d1), 0.0, o0, o1))

    def held(out, x, keep):
        scan(out, R(keep), x, OP.add, OP.max)

    def copy(q, out, x):
        if q == "a":
            op("a", [out], [x], lambda: g.scalar.activation(ap(out), ap(x), COPY, scale=1.0))
        else:
            vcopy(out, x)

    def pick(q, out, win, off):
        if q == "a":
            op("a", [out], [win, off], lambda: g.scalar.activation(ap(out), ap(win).indirect(ap(off)), COPY))
        elif q == "v":
            op("v", [out], [win, off], lambda: g.vector.tensor_copy(ap(out), ap(win).indirect(ap(off))))
        else:
            k = int(q)
            cut = out[1] + 16 * k * out[3]
            pick("v", R(out[0], out[1], cut, out[3]), win, R(off[0], off[1], off[1] + k))
            pick("a", R(out[0], cut, out[2], out[3]), win, R(off[0], off[1] + k, off[2]))

    def quant(q, x, a=0, b=None):
        o, s = R(q, a, b), R(q + "s", a, b)
        op("v", [o, s], [x], lambda: g.vector.quantize_mx(ap(o), ap(s), ap(x)))

    def mm(bank, l, la, r, ra, rb):
        o = R("p%d" % bank, 0, rb - ra)
        ops = [R(l, la, la + 128), R(l + "s", la, la + 128), R(r, ra, rb), R(r + "s", ra, rb)]
        op("t", [o], ops, lambda: g.tensor.matmul_mx(ap(o), ap(ops[0]), ap(ops[1]), ap(ops[2]), ap(ops[3]), True, True))

    nd = [0]

    def dma(q, writes, reads, out, in_):
        sem = "d%d" % nd[0]
        nd[0] += 1
        op(q, writes, reads, lambda: Q[q].dma_start(out, in_), sem, 16)

    def lanes(src, dst):
        return topo.engines(src, dst)[:8]

    def send(s, land, src, k, codes=False):
        dst = T.cores[rank ^ s]
        cnt["arr%s%d" % (k, s)] = len(lanes(dst, core))
        note("g", [], [land], ("arr%s%d" % (k, s), len(lanes(dst, core))))
        e = lanes(core, dst)
        rid, pid, _ = topo.addr(dst)
        hazards("g", [src], [])
        o, i = ap(land), ap(src)
        if codes:
            o, i = o.bitcast(dt.uint8), i.bitcast(dt.uint8)
        g.remote_dma(out_ap=o, in_ap=i, remote_sem=T.sem["arr%s%d" % (k, s)], local_sem=T.sem["snt%s%d" % (k, s)],
                     pid=pid, routing_id=rid, dma_engine_mask=sum(1 << j for j in e))
        sem = "snt%s%d" % (k, s)
        cnt[sem] = len(e)
        note("g", [src], [], (sem, len(e)))

    def iota(r, pattern, base, cm):
        f = SCRATCH[r[0]][2] != I32
        op("g", [r], [], lambda: g.iota(ap(r), pattern, base, cm, allow_small_or_imprecise_dtypes=True) if f
           else g.iota(ap(r), pattern, base, cm))

    def odd(n, a, b):
        return R(n, 2 * a + 1, 2 * b, 2)

    def slot(half, j):
        return R("sel", 98 * half + j, 98 * half + 98, 7)

    def term(j):
        return R("sc", 105 + 16 * j, 105 + 16 * 98, 112)

    pf, pf1, off, offm, offq, offh, ofb, nofb = [R(n) for n in "pf pf1 off offm offq offh ofb nofb".split()]
    upk, uqc, uq2, e, one = R("up"), R("uq"), R("uq2"), R("et"), R("ones")
    top, mid = len(POWERS) - 1, POWERS.index(MID)
    small = {
        "lm": lambda q: dma(q, [R("mli")], [], T.mli[:, :], T.ml[:, :]),
        "lu": lambda q: dma(q, [R("ut")], [], T.ut[:, :], T.u[:, :]),
        "lw": lambda q: dma(q, [R("wq")], [R("x0")], T.wq[:, :].bitcast(dt.uint8), T.wc[:, :]),
        "ls": lambda q: dma(q, [R("wqs")], [R("x0")], T.wqs[:, :], T.ws[:, :]),
        "vt": lambda q: dma("s", [R("vt")], [R("lb1")], T.vt[:, :], T.v[:, :]),
        "pi": lambda q: iota(R("pi"), [[0, 14]], 0, 1),
        "fi": lambda q: iota(R("fi"), [[1, 16]], 0, 0),
        "ui": lambda q: iota(R("ui"), [[16, 8]], 0, 0),
        "cc": lambda q: iota(R("cc"), [[2, C]], -C, 0),
        "port": lambda q: iota(odd("raw", H, C), [[2, H]], 1 - H, 0),
        "one": lambda q: iota(one, [[0, 516]], 1, 0),
        "et": lambda q: op("g", [e], [one], lambda: g.affine_select(ap(e), ap(one), [[-1, 516]], OP.is_equal, 0.0, 3, 4)),
        "pm": lambda q: ts(R("pm"), R("pi"), 15, OP.bitwise_and),
        "sel0": lambda q: fill(R("sel", 0, 98), 0.0),
        "sc2": lambda q: ts(term(2), R("pm"), 0.0, OP.mult),
        "sc5": lambda q: ts(term(5), R("pm"), 0.0, OP.mult, 0.25, OP.add),
        "sc6": lambda q: ts(term(6), R("pm"), 0.0, OP.mult),
        "pf": lambda q: vcopy(pf, R("pm", 0, 1)),
        "pmu": lambda q: vcopy(R("pmu"), R("pm")),
        "up": lambda q: vcopy(upk, R("ui")),
        "pf1": lambda q: axb(q, pf1, pf, 1.0, 1.0),
        "off": lambda q: ts(off, pf, 15.0, OP.is_lt, LIFT, OP.mult),
        "ofb": lambda q: axb(q, ofb, off, BIT / LIFT, 0.0),
        "ka": lambda q: ts(R("ka"), R("fi"), pf, OP.is_equal, -2 * BIT, OP.mult),
        "kb": lambda q: ts(R("kb"), R("fi"), pf1, OP.is_equal, BIT, OP.mult),
        "offm": lambda q: axb(q, offm, off, 1.0, -float(C)),
        "offq": lambda q: axb(q, offq, off, 1.0 + C * BIT / LIFT, -float(C + 1)),
        "offh": lambda q: axb(q, offh, off, -0.5, float(H)),
        "nofb": lambda q: axb(q, nofb, off, -2 * BIT / LIFT, 0.0),
        "k16": lambda q: tt(R("k16"), R("ka"), R("kb"), OP.add),
        "keepb": lambda q: pick(q, R("keepb"), R("k16"), R("pmu")),
        "keep": lambda q: axb(q, R("keep"), R("keepb"), LIFT / BIT, 0.0),
        "mf": lambda q: ts(R("mf"), R("mli"), 2.0, OP.mult, offm, OP.add),
        "uq": lambda q: quant("uq", R("ut")),
        "uq2": lambda q: op("v", [uq2], [uqc, upk], lambda: g.vector.tensor_copy(
            ap(uq2).bitcast(dt.uint32), ap(uqc).bitcast(dt.uint32).indirect(ap(upk)))),
        "uq2s": lambda q: pick(q, R("uq2s"), R("uqs"), upk),
        "vq": lambda q: quant("vq", R("vt")),
        "own": lambda q: copy(q, odd("w%d" % (mid % 2), 0, H), R("cc", 0, H)),
        "raw": lambda q: copy(q, odd("raw", 0, H), R("cc", 0, H)),
        "far": lambda q: copy(q, odd("wa", H, C), R("cc", H, C)),
    }
    for b in range(4):
        small["eq%d" % b] = lambda q, b=b: quant("eq", R("et", 3 - b, 515 - b), 128 * b, 128 * b + 128)
    for b in range(3):
        small["lx%d" % b] = lambda q, a=4 * RUNS[b], z=4 * RUNS[b + 1]: dma(q, [R("x0", a, z)], [], T.x0[:, a:z], T.x[:, a:z])
    for b in range(2):
        small["w%d" % b] = lambda q, b=b: copy(q, R("w%d" % b, H, H + 2 * C, 2), R("cc"))

    def step(s, name, q, b0, b1):
        xs, xn = "x%d" % (s - 1), "x%d" % s
        land_b, land_c, land_q = "lb%d" % s, "lc%d" % s, "lq%d" % s
        c0, c1, low = 16 * b0, 16 * b1, int(b0 >= 14)
        kind, k = name[0], int(name[-1]) if name[-1].isdigit() else 0
        m = R("mf") if s == 1 else R("sm", 15, C, 16)

        def cols(x, b=None):
            return R(x, 4 * c0, 4 * c1) if b is None else R(x, 4 * c0 + b, 4 * c1, 4)

        def bank(b):
            return R("p%d" % (b + 4 * low), c0 - H * low, c1 - H * low)

        def scores():
            return R("p%d" % k, c0 - RUNS[k], c1 - RUNS[k]) if name[-1].isdigit() else bank(0)

        def row(j):
            return odd("w%d" % (j % 2), H, C) if j <= top else R("tr", (j - top - 1) * H, (j - top) * H)

        def codes(j):
            return R("w%d" % (j % 2), H)

        def lst(j):
            return R("ls", 14 * j, 14 * j + 14)

        if kind == "P":
            if name == "Ptt":
                ts(R("tt"), m, off, OP.is_ge, float(C), OP.mult)
            elif name == "Pmf":
                tt(R("mmf"), m, R("tt"), OP.subtract)
            elif name == "Pmm":
                ts(R("mm"), R("mmf"), offm, OP.subtract)
            elif name == "Pos":
                axb(q, R("os0"), R("tt"), nofb, offq)
            elif name == "Pq":
                tt(term(1 + 3 * low), R(m[0], m[1] + b0 * m[3], m[1] + b1 * m[3] - m[3] + 1, m[3]), R("os0", b0, b1), OP.subtract)
            elif name == "Psc":
                copy(q, R("sel", 98, 196), R("sel", 0, 98))
            else:
                axb(q, slot(0, k), R("tt", 14 * (k > 1), 14 + 14 * (k > 1)), -2.0, float(C))
        elif kind == "T":
            mine = R("so", 15, H, 16)
            if name[:3] == "Tsw":
                tt(R("sw", 2 * (c0 - H), 2 * (c1 - H), 2), R("sup", c0 - H, c1 - H), scores(), OP.is_gt)
            elif name == "Tso":
                held(R("so"), R("sw", 0, C, 2), "keepb")
            elif name == "Tb":
                pick(q, R("bb", c0, c1), R("sw"), R("mm", b0, b1))
            elif name == "Th":
                held(R("sc", 48 * low, 48 * low + 7 * H, 7), R("bb", c0, c1), "keepb")
            elif name[1] == "c":
                ts(slot(k // 2, 2 + 3 * (k % 2)), mine, ofb, [OP.is_equal, OP.not_equal][k in (1, 2)],
                   [BIG, SMALL][k % 2], [OP.mult, OP.max][k % 2])
            elif name != "Tn":
                scan(R("nn", 98 * k, 98 * k + 98), R("sel", 98 * k, 98 * k + 98), R("sc", 105, 105 + 16 * 98, 16), OP.mult, OP.add)
            else:
                vcopy(R("n16", b0, b1), R("nn", 5 + 7 * b0, 7 * b1, 7))
                send(s, R(land_c if low else land_b), R("n16", b0, b1), "bc"[low])
        elif name == "wa":
            pick(q, odd("wa", 0, H), R("raw"), R("n16", 14, 28))
        elif kind == "z":
            pick_tt(cols("zz", k), R("xp%d" % k), R("n16", b0, b1), cols(xs, k), OP.add)
        elif kind == "c":
            pick(q, cols("zz", k), R("xp%d" % k), R("n16", b0, b1))
        elif kind == "d":
            tt(cols("zz", k), cols("zz", k), cols(xs, k), OP.add)
        elif kind == "n":
            pick_tt(cols(xn, k), R("bp%d" % k), R("m16", b0, b1), cols(xs, k), OP.add)
        elif kind == "g":
            pick(q, cols("ya", k), R("bp%d" % k), R("m16", b0, b1))
        elif kind == "h":
            tt(cols(xn, k), cols("ya", k), cols(xs, k), OP.add)
        elif name == "qz":
            quant("qz", cols("zz"), c0, c1)
        elif kind == "f":
            mm(k + 4 * low, "wq", 128 * k, "qz", c0, c1)
        elif name == "qa":
            quant("qa" if low else land_q, cols("aa"), c0, c1)
            if low:
                send(s, R(land_q, c0, c1), R("qa", c0, c1), "q", True)
                send(s, R(land_q + "s", c0, c1), R("qas", c0, c1), "s")
        elif kind == "a":
            axb(q, cols("aa", k), bank(k), 0.015625, 0.0)
        elif kind == "e":
            mm(k + 4 * low, "eq", 128 * k, land_q, c0, c1)
        elif kind == "b":
            copy(q, R("bp%d" % k, c0, c1), bank(k))
        elif name == "p1":
            pick(q, row(0), R("wa"), R(land_b))
        elif name == "o":
            pick(q, row(top + 3), R("wa"), R(land_c))
        elif kind == "p":
            j = POWERS.index(int(name[1:]))
            pick(q, row(j), codes(j - 1), lst(POWERS.index(POWERS[j] - POWERS[j - 1])))
        elif kind in "sl":
            j = top + 1 + "tro".index(name[1]) if name[1] in "tro" else POWERS.index(int(name[1:]))
            if kind == "s":
                held(R("sa", j * H, j * H + H), row(j), "keep")
            else:
                ts(lst(j), R("sa", j * H + 15, j * H + H, 16), offm, OP.subtract)
        elif name == "t":
            pick(q, row(top + 1), R("w%d" % (mid % 2), 0, 2 * C), R("n16", 0, 14))
        elif name == "r":
            pick(q, row(top + 2), codes(mid), lst(top + 3))
        elif name == "mu":
            pick(q, R("mu", 0, H), codes(top), lst(top + 1))
        elif name == "mr":
            pick(q, R("mu", H, C), codes(top), lst(top + 2))
        elif name == "mo":
            axb(q, R("mrow"), R("mu"), 0.5, float(H))
        elif name == "m":
            held(R("sm", c0, c1), R("mu", c0, c1), "keep")
        elif name == "ml":
            ts(R("m16", b0, b1), R("sm", c0 + 15, c1, 16), 0.5, OP.mult, offh, OP.add)
        elif kind == "x":
            copy(q, odd("xp%d" % k, c0, c1), cols(xs, k))
        elif kind == "u":
            copy(q, R("sup", c0, c1), scores())
        elif kind == "q":
            quant("qx", cols(xs), c0, c1)
            mm(4 * low if name == "q" else k, "uq2", 0, "qx", c0, c1)
        elif kind == "Q":
            quant("qx", cols(xn), c0, c1)
            mm(k, "vq", 0, "qx", c0, c1)
        elif kind == "y":
            copy(q, R("yo", c0, c1), R("p%d" % k, 0, c1 - c0))
        elif name == "Sm":
            dma(q, [], [R("mrow")], T.mo[:, :], T.mrow[0:128:16, :])
        elif name == "Sc":
            dma(q, [], [R("qx", c0, c1)], T.oc[:, 4 * c0:4 * c1], T.qx[:, c0:c1].bitcast(dt.uint8))
        elif name == "Sy":
            dma(q, [], [R("yo", c0, c1)], T.y[:, c0:c1], T.yo[:, c0:c1])
        else:
            dma(q, [], [R("qxs")], T.osc[4 * k:4 * k + 4, :], T.qxs[32 * k:32 * k + 4, :])

    for s, order in zip(ROUNDS, ORDERS):
        for word in order:
            ahead = word.endswith("'")
            head, _, span = word.rstrip("'").partition("@")
            name, _, q = head.partition(".")
            if name[0] == "+":
                small[name[1:]](q or "a")
            else:
                step(s + ahead, name, q or "a", *(SPANS[span] if span in SPANS else [int(n) for n in span.split("-")]))

    for sem in sorted(cnt, key=lambda k: nd[0] + int(k[1:]) if k[1:].isdigit() else 0):
        need("g", sem, cnt[sem])
